import numpy as np, ml_dtypes
CORES = [16,17,18,19,32,33,34,35]
N = 8
BF = ml_dtypes.bfloat16
def gentries(a):
    return np.ascontiguousarray(a.reshape(8, 16, -1).transpose(0, 2, 1)).reshape(8, -1)
def gtable(e):
    e = np.asarray(e); return np.ascontiguousarray(e.reshape(8, -1, 16).transpose(0, 2, 1)).reshape(128, -1).astype(np.int32)
V, L, CAP, RO, LO, HI = 3072, 64, 192, 3, 160, 400
SHIFTS = (1, 2, 4)
GH = L * len(SHIFTS)
SZ = np.array([LO // 20, (LO + HI) // 16, HI // 5, 127])
def fold(v):
    return np.abs((v + 127) % 508 - 254) - 127
def steps(rng, a, b):
    u = rng.random((N, 8, 1, V)); w = np.where(u < a, SZ[0], np.where(u < 1 - b, SZ[1], np.where(u < 1 - 0.4 * b, SZ[2], SZ[3])))
    return fold(rng.integers(-127, 128, (N, 8, 16, 1)) + np.add.accumulate(rng.integers(-w, w + 1, (N, 8, 16, V)), axis=3))
def walk(rng, t):
    i = np.arange(16); m = t[..., None] // 16 + ((i + np.arange(V)[:, None]) % 16 < t[..., None] % 16)
    kind = rng.integers(0, 4, t.shape); s = (kind == 1) & (t > 259); one = kind == 2
    four = np.stack([i // 4 == h for h in range(4)] + [i % 4 == h for h in range(4)]); u = rng.integers(0, 8, np.count_nonzero(s))
    fin = np.add.accumulate(four.astype(np.int64), axis=1) - 1; fout = np.add.accumulate((~four).astype(np.int64), axis=1) - 1
    a = 257 + 2 * rng.integers(0, 2, (u.size, 1)); b = t[s][:, None] - a
    m[s] = np.where(four[u], a // 4 + (fin[u] < a % 4), b // 12 + (fout[u] < b % 12))
    y = np.zeros((N, 8, 16, V), np.int64); p = rng.integers(-127, 128, (N, 8, 16)); z = 2 * rng.integers(0, 2, (V, N, 8, 16)) - 1
    for k in range(V):
        y[..., k] = p; tk = t[:, :, k, None]; h = np.abs(p)
        big = np.minimum(tk, 127 + np.max(h, axis=2, keepdims=True)); w = tk - big; o = (i - np.argmax(h, axis=2)[..., None]) % 16
        mk = np.where(one[:, :, k, None], np.where(o == 0, big, w // 15 + (o <= w % 15)), m[:, :, k])
        p = p + mk * np.where(np.abs(p + z[k] * mk) <= 127, z[k], np.where(p > 0, -1, 1))
    return y
def lay(rng, y, n, m, mode, ok):
    x = np.zeros((N, 8, 16, V), np.int64); nx = np.full((N, 8, V), -1, np.int64); hd = np.zeros((N, 8, GH), np.int64)
    for q in range(N):
        for g in range(8):
            k, mm, o = int(n[q, g]), int(m[q, g]), rng.permutation(V)
            if mode[q, g] == 1: o = np.concatenate([V - k + rng.permutation(k), rng.permutation(V - k)])
            if mode[q, g] == 2: o = np.concatenate([rng.permutation(k), k + rng.permutation(V - k)])
            if mode[q, g] == 3:
                o = np.concatenate([rng.permutation(V - 1), np.full(1, V - 1)])
                o = np.concatenate([o[:k][o[:k] % 2 == 1], o[:k][o[:k] % 2 == 0], o[k:]])
            if mode[q, g] == 4:
                ev, od, w = 2 * rng.permutation(V // 2), 2 * rng.permutation(V // 2) + 1, k // 2
                o = np.concatenate([np.stack([ev[:w], od[:w]], axis=1).reshape(-1), rng.permutation(np.concatenate([ev[w:], od[w:]]))])
            if mode[q, g] == 5:
                z = rng.permutation(16)[np.arange(V) % 16]; fr = z == 15
                fr[np.flatnonzero((z > 1) & (z < 15))[-(V - k - V // 16):]] = True
                lv = rng.permutation(np.flatnonzero(~fr)); lv = lv[np.argsort(z[lv], kind="stable")]
                a = ~ok[q, g, :k]; a = a | np.concatenate([a[1:], np.zeros(1, bool)]); c = np.count_nonzero(a)
                o[:k][a] = rng.permutation(lv[:c]); o[:k][~a] = rng.permutation(lv[c:]); o[k:] = np.flatnonzero(fr)
            x[q, g][:, o] = y[q, g]
            u = o[:k]; c = np.sort(rng.permutation(k - 1)[:mm - 1]) + 1
            a = np.concatenate([np.zeros(1, np.int64), c]); b = np.concatenate([c, np.full(1, k)]) - 1
            e = min((mm + 1) // 2 + int(rng.integers(0, mm // 2 + 1)), GH)
            nx[q, g, u[:-1]] = u[1:]; nx[q, g, u[b]] = u[a]
            nx[q, g, u[b[rng.permutation(mm)[:e]]]] = V + rng.permutation(GH)[:e]
            h = u[(u % 2 == 0) & ok[q, g, :k]]; d = rng.permutation(h[nx[q, g, h] >= V])[:GH // 4]
            hd[q, g] = rng.permutation(np.resize(np.concatenate([d, rng.permutation(np.setdiff1d(h, d))]), GH))
    return x, nx, hd
def nears(rng, x, nx, hd):
    for q in range(N):
        for g in range(8):
            i = rng.permutation(np.flatnonzero(nx[q, g] >= V)); i = i[:(i.size + 1) // 2]
            if i.size == 0: continue
            t = nx[q, g, i] - V; src = (q + np.array(SHIFTS)[t // L]) % N
            w = SZ[rng.integers(0, 3, (i.size, 1))]
            x[q, g][:, i] = np.clip(x[src, g, :, hd[src, g, t]] + rng.integers(-w, w + 1, (i.size, 16)), -127, 127).T
def off(rng, p, t):
    m = t[:, None] // 16 + ((np.arange(16) + rng.integers(0, 16, (t.size, 1))) % 16 < t[:, None] % 16)
    z = 2 * rng.integers(0, 2, p.shape) - 1
    return p + m * np.where(np.abs(p + z * m) <= 127, z, np.where(p > 0, -1, 1))
def edge(rng, x, nx, hd):
    for q in range(N):
        for g in range(8):
            i = np.flatnonzero((nx[q, g] >= V) & ~np.isin(np.arange(V), hd[q, g]))
            if i.size == 0: continue
            t = nx[q, g, i] - V; src = (q + np.array(SHIFTS)[t // L]) % N
            x[q, g][:, i] = off(rng, x[src, g, :, hd[src, g, t]], rng.choice(np.array([LO - 1, LO, HI - 1, HI, HI, HI, HI + 1, HI + 1]), i.size)).T
            before = np.full(V, -1, np.int64); own = np.flatnonzero((nx[q, g] >= 0) & (nx[q, g] < V)); before[nx[q, g, own]] = own
            b = before[i]; s = (b >= 0) & ~np.isin(b, hd[q, g])
            x[q, g][:, b[s]] = off(rng, x[q, g][:, i[s]].T, rng.choice(np.array([0, 1, LO // 2, LO - 1, LO - 1, LO]), np.count_nonzero(s))).T
def pack(x, nx, hd):
    return {"x": np.ascontiguousarray(x.reshape(N, 128, V)).astype(np.float32).astype(BF), "nxt": np.stack([gtable(a) for a in nx]), "head": np.stack([gtable(a) for a in hd])}
def sizes(rng):
    return rng.integers(V // 2, V - RO * CAP + 1, (N, 8)), rng.integers(GH // 2, GH + 33, (N, 8))
ANY = np.ones((N, 8, V), bool); MIX = np.zeros((N, 8), np.int64)
def setup_inputs(rng):
    n, m = sizes(rng); a = rng.choice(np.array([0.25, 0.35, 0.5]), (N, 8, 1, 1)); b = rng.choice(np.array([0.02, 0.06, 0.12, 0.25]), (N, 8, 1, 1))
    x, nx, hd = lay(rng, steps(rng, a, b), n, m, MIX, ANY); nears(rng, x, nx, hd)
    return pack(x, nx, hd)
def setup_inputs_cap(rng):
    k = V - RO * CAP; kinds = (CAP, CAP + 1, CAP - 1, 0, 1, k - 4, CAP, 0); modes = (3, 0, 0, 4, 0, 3, 5, 0)
    far = np.zeros((N, 8, V), bool); mode = np.zeros((N, 8), np.int64); m = np.ones((N, 8), np.int64); R = np.full((N, 8, 1, 1), HI // 32)
    for q in range(N):
        for g in range(8):
            j = (g + q) % 8; far[q, g, 3 + 2 * rng.permutation((k - 4) // 2)[:kinds[j] // 2]] = True
            far[q, g, 0] = kinds[j] % 2 == 1; mode[q, g] = modes[j]
            if j == 3: R[q, g] = (LO - 1) // 32
            if j == 7: far[q, g, :k - 48] = True; m[q, g] = 2 * GH
    c = rng.integers(80, 101, (8, 16, 1)) * (2 * rng.integers(0, 2, (8, 16, 1)) - 1)
    y = np.where(far[:, :, None, :], -c, c) + rng.integers(-R, R + 1, (N, 8, 16, V))
    return pack(*lay(rng, y, np.full((N, 8), k), m, mode, ~far))
def setup_inputs_ties(rng):
    n, m = sizes(rng); t = rng.choice(np.array([0, 1, LO - 1, LO, LO + 1, HI - 1, HI, HI, HI + 1, HI + 1]), (N, 8, V))
    x, nx, hd = lay(rng, walk(rng, t), n, m, MIX, ANY); edge(rng, x, nx, hd)
    return pack(x, nx, hd)
def setup_inputs_loops(rng):
    n, m = sizes(rng); m = n // 3
    x, nx, hd = lay(rng, steps(rng, 0.6, 0.1), n, m, rng.integers(0, 3, (N, 8)), ANY)
    hd[:, ::2] = np.take_along_axis(hd[:, ::2], rng.integers(0, 3, (N, 4, GH)), 2)
    q, g, z = int(rng.integers(0, N)), int(rng.integers(0, 8)), V - 2
    nx[q, g] = -1; nx[q, g, z] = z; hd[q, g] = z
    nears(rng, x, nx, hd)
    return pack(x, nx, hd)
def setup_inputs_churn(rng):
    n, m = sizes(rng); n[:, ::2] = V - RO * CAP
    x, nx, hd = lay(rng, steps(rng, 0.55, 0.35), n, m, rng.integers(0, 3, (N, 8)), ANY); nears(rng, x, nx, hd)
    return pack(x, nx, hd)
def setup_inputs_spread(rng):
    n, m = sizes(rng); y = np.rint(127 * np.exp2(-7 * rng.random((N, 8, 1, V))) * (2 * rng.random((N, 8, 16, V)) - 1)).astype(np.int64)
    x, nx, hd = lay(rng, y, n, m, MIX, ANY)
    return pack(x, nx, hd)
def check_inputs(d):
    bad = []; xf = np.asarray(d["x"]).astype(np.float32)
    if not np.all(np.abs(xf) <= 127) or not np.all(np.rint(xf) == xf): bad.append("x: whole numbers from -127 to 127")
    nl = np.stack([gentries(a) for a in d["nxt"]]).astype(np.int64); hl = np.stack([gentries(a) for a in d["head"]]).astype(np.int64)
    if np.min(nl) < -1 or np.max(nl) > V + GH - 1: bad.append("range of nxt")
    if np.min(hl) < 0 or np.max(hl) > V - 1: bad.append("range of head")
    if "range of nxt" in bad or "range of head" in bad: return bad
    live = nl >= 0; own = live & (nl < V); s = np.sort(nl, axis=2)
    if np.any((s[:, :, 1:] == s[:, :, :-1]) & (s[:, :, 1:] >= 0)): bad.append("nxt: one predecessor a node")
    if np.any(own & ~np.take_along_axis(live, np.where(own, nl, 0), 2)): bad.append("nxt names live nodes only")
    if np.any(hl % 2 == 1): bad.append("heads are even")
    if not np.all(np.take_along_axis(live, hl, 2)): bad.append("heads are live")
    if np.min(np.count_nonzero(~live, axis=2)) < RO * CAP: bad.append("free nodes")
    return bad
def reference(x, nxt, head):
    X = x.astype(np.float32).astype(np.int64).reshape(N, 8, 16, V)
    nx = np.stack([gentries(a) for a in nxt]).astype(np.int64); hd = np.stack([gentries(a) for a in head]).astype(np.int64)
    even = np.arange(V) % 2 == 0
    for rnd in range(RO):
        ghost = np.stack([np.concatenate([np.take_along_axis(X[(r + s) % N], hd[(r + s) % N][:, None, b * L:(b + 1) * L], 2) for b, s in enumerate(SHIFTS)], axis=2) for r in range(N)])
        live = nx >= 0
        Xn = np.take_along_axis(np.concatenate([X, ghost], axis=3), np.where(live, nx, 0)[:, :, None, :], 3)
        ln = np.add.reduce(np.abs(X - Xn), axis=2)
        far = live & (ln > HI); split = far & (np.add.accumulate(far.astype(np.int64), axis=2) <= CAP)
        own = live & (nx < V); j = np.where(own, nx, 0)
        merge = own & even & (j % 2 == 1) & (ln < LO) & (np.take_along_axis(ln, j, 2) <= HI)
        new = np.where(merge, np.take_along_axis(nx, j, 2), nx)
        for r in range(N):
            for g in range(8):
                i = np.flatnonzero(split[r, g]); f = np.flatnonzero(~live[r, g])[:i.size]
                X[r, g][:, f] = (X[r, g][:, i] + Xn[r, g][:, i]) >> 1
                new[r, g, f] = nx[r, g, i]; new[r, g, i] = f
                new[r, g, j[r, g][merge[r, g]]] = -1
        nx = new; live = nx >= 0
        Xn = np.take_along_axis(np.concatenate([X, ghost], axis=3), np.where(live, nx, 0)[:, :, None, :], 3)
        X = X + np.where(live[:, :, None, :], np.clip(Xn - X, -1, 1), 0)
    X = np.where((nx >= 0)[:, :, None, :], X, 0)
    return {"yx": X.reshape(N, 128, V).astype(np.float32).astype(BF), "yn": np.stack([gtable(a) for a in nx]).astype(np.float32)}

@@ -1,0 +1,521 @@
+from concourse.bass import DstId, RemoteDMATransfer
+from concourse.mybir import AluOpType as Op, ActivationFunctionType as AF
+
+V, H, SP, W, RO = 3072, 1536, 3264, 3456, 3
+SHIFTS = (1, 2, 4)
+G1A = ((0,), (0, 1), (0, 1))
+G3A = (0, 1, 2)
+AV = 8
+FC = 16
+CY, PY, GA, SC, FIX, HOP = 1.04e-3, 0.53e-3, 1.56, 3.8, 0.06, 0.1
+PASSES, JIT = 1000, 0.5
+ORDER = []
+bf, f32, i32, u16 = "bfloat16", "float32", "int32", "uint16"
+SCRATCH = {}
+
+
+def _sb(names, cols, dt):
+    for n in names.split():
+        SCRATCH[n] = ("sbuf", [128, cols], dt)
+
+
+_sb("XW0 XW1 XW2 XW3 A F0 F1 F2 LA0 LA1 LA2 LB0 LB1 LB2", W, bf)
+_sb("XO DX U", SP, bf)
+_sb("CO", V, bf)
+_sb("AB0 AB1 AB2 ABo CE D3 X0E", H, bf)
+_sb("HG0 HG1 HG2 LOHI UI NI ZR", 192, bf)
+_sb("BM BN BP0 BD BU BKn BKp BK2", 144, bf)
+_sb("IDb IDn I8192p I8192n M1 M2 TST TGE SG SELA DG34", 128, bf)
+_sb("IDf SGf AQ GQ AQm PE0 PE1 PO0 PO1 QE0 QE1 QO0 QO1", 128, f32)
+_sb("UMA", 16 * 144, bf)
+_sb("JJ", 144, f32)
+_sb("COL MK CD CK CE16 OF16 I16", 16, f32)
+_sb("PI", 8, i32)
+_sb("NX TI HI DI HH", 192, i32)
+_sb("HD", 12, i32)
+_sb("HU", 12, u16)
+_sb("OU", 16, u16)
+_sb("BL SL", 24, u16)
+_sb("BLb", 24, bf)
+_sb("LS0 LS1 LS2", 192, u16)
+_sb("L3 LZ", 96, u16)
+_sb("NXF SELF N2 IDX T1 T2 T3 YN", 192, f32)
+_sb("MD THE I3 QF", 96, f32)
+_sb("MM REM", 96, bf)
+_sb("LO256 HI256 SW", 256, f32)
+_sb("FL", 512, bf)
+_sb("R", 272, bf)
+_sb("BV", 112, bf)
+_sb("THR", 8, f32)
+_sb("BS U2 CN BB CB SRC", 384, bf)
+for _k in range(8):
+    SCRATCH["ps%d" % _k] = ("psum", [128, 512], f32)
+SEMAPHORES = ["sv", "sa", "sp", "sg", "ldx", "ldn", "ldh", "stx", "stn"] + [s + str(r) for s in ("arr", "snt", "cp", "acc") for r in range(RO)]
+
+
+def engines_for(T, topo, q):
+    n = len(T.cores)
+    allowed = [topo.engines(T.cores[q], T.cores[(q - s) % n]) for s in SHIFTS]
+    narrow = min(len(a) for a in allowed)
+    tight = [b for b in range(3) if len(allowed[b]) == narrow]
+    share = {1: [4], 2: [4, 4], 3: [4, 2, 2]}[len(tight)] if narrow < 12 else [4, 4, 4]
+    out, used = {}, set()
+    for b, k in zip(reversed(tight), share):
+        out[b] = [e for e in allowed[b] if e not in used][:k]
+        used |= set(out[b])
+    for b in range(3):
+        if b not in out:
+            out[b] = [e for e in reversed(allowed[b]) if e not in used][:4]
+            used |= set(out[b])
+    return [out[b] for b in range(3)]
+
+
+def schedule(nodes):
+    if ORDER:
+        return ORDER[0]
+    n = len(nodes)
+    users = [[] for _ in nodes]
+    for i, x in enumerate(nodes):
+        for d in x["dep"]:
+            users[d].append(i)
+    before = [sorted(x["dep"]) for x in nodes]
+    dur, lat, eng = [x["dur"] for x in nodes], [x["lat"] for x in nodes], [x["e"] for x in nodes]
+
+    def place(rank, pred, succ, back):
+        left, start, est = [len(p) for p in pred], [0.0] * n, [lat[i] if back else 0.0 for i in range(n)]
+        busy = {e: [] for e in eng}
+        ready = [(rank[i], i) for i in range(n) if left[i] == 0]
+        while ready:
+            m = min(ready)
+            ready.remove(m)
+            i = m[1]
+            t, d, row = est[i], dur[i], busy[eng[i]]
+            k = len(row)
+            while k > 0 and row[k - 1][1] > t:
+                k -= 1
+            while k < len(row) and row[k][0] < t + d - 1e-9:
+                t = row[k][1]
+                k += 1
+            row.insert(k, (t, t + d))
+            start[i] = t
+            for u in succ[i]:
+                e = t + d + (lat[u] if back else lat[i])
+                if e > est[u]:
+                    est[u] = e
+                left[u] -= 1
+                if left[u] == 0:
+                    ready.append((rank[u], u))
+        return start, max(start[i] + dur[i] + lat[i] for i in range(n))
+
+    path = [0.0] * n
+    for i in reversed(range(n)):
+        path[i] = dur[i] + lat[i] + max([path[u] for u in users[i]], default=0.0)
+    rank, best, seed = [-p for p in path], None, 1
+    for it in range(PASSES):
+        if it % 2 == 1 and it > 4:
+            rank, amp = [], JIT * (1 + it // 2 % 3)
+            for i in range(n):
+                seed = (seed * 1103515245 + 12345) % 2147483648
+                rank.append(best[1][i] + amp * seed / 2147483648)
+        start, span = place(rank, before, users, False)
+        if best is None or span <= best[0]:
+            best = (span, start)
+        back, _s = place([-(start[i] + dur[i]) for i in range(n)], users, before, True)
+        rank = [-(back[i] + dur[i]) for i in range(n)]
+    ORDER.append(sorted(range(n), key=lambda i: (best[1][i], i)))
+    return ORDER[0]
+
+
+def rank_program(g, core, T, topo):
+    rank = T.rank_of(core)
+    if rank is None:
+        return
+    n = len(T.cores)
+    S = T.sem
+    q = {"v": g.vector, "a": g.scalar, "p": g.tensor, "g": g, "s": g.sync}
+    sem = {"v": S.sv, "a": S.sa, "p": S.sp, "g": S.sg}
+    nodes, lastw, readers, bank = [], {}, {}, {}
+
+    def op(e, fns, dur, r=(), w=(), b=(), tok=None, lat=HOP):
+        i = len(nodes)
+        dep = {lastw[x] for x in list(r) + list(w) if x in lastw}
+        for x in w:
+            dep |= set(readers.get(x, []))
+        for k in b:
+            cur, prev = bank.get(k, ([], []))
+            same = e != "p" and cur and nodes[cur[0]]["e"] == e
+            dep |= set(prev if same else cur)
+            bank[k] = (cur + [i], prev) if same else ([i], cur)
+        nodes.append(dict(e=e, fns=fns, dur=dur, lat=lat, dep=dep, tok=tok))
+        for x in r:
+            readers.setdefault(x, []).append(i)
+        for x in w:
+            lastw[x], readers[x] = i, []
+
+    def dma(e, name, out, in_, r, w, lat, **kw):
+        op(e, [lambda: q[e].dma_start(out, in_, **kw).then_inc(S[name], 16)], 1.0 if e == "g" else 0.1, r, w, tok=(name, 16), lat=lat)
+
+    vec, act, pe = g.vector, g.scalar, g.tensor
+    ps = [T["ps%d" % k] for k in range(8)]
+    two = (T.XO.dtype, T.HU.dtype)
+
+    def ix(win, off):
+        return (win.indirect(off), 16 * off.shape[1])
+
+    def el(e, call, out, ins, r, w, b, k=1.0):
+        if isinstance(out, tuple):
+            c = SC * out[1]
+        elif ins and isinstance(ins[0], tuple):
+            c = GA * ins[0][1]
+        else:
+            c = out.shape[1] * k * (0.5 if e == "v" and all(x.dtype in two for x in [out] + ins) else 1.0)
+        a = [x[0] if isinstance(x, tuple) else x for x in [out] + ins]
+        op(e, [lambda: call(*a)], FIX + CY * max(64, c), r, w, b)
+
+    def ts(out, in0, s1, s2, o0, o1=None, r=(), w=(), b=()):
+        el("v", lambda o, i: vec.tensor_scalar(o, i, s1, None, o0) if o1 is None else vec.tensor_scalar(o, i, s1, s2, o0, o1), out, [in0], r, w, b)
+
+    def tt(out, in0, in1, o, r=(), w=(), b=()):
+        el("v", lambda x, y, z: vec.tensor_tensor(x, y, z, o), out, [in0, in1], r, w, b, 1.0 if b else 2.0)
+
+    def cp(out, in_, r=(), w=(), b=()):
+        el("v", vec.tensor_copy, out, [in_], r, w, b)
+
+    def ms(ap, c, w):
+        el("v", lambda o: vec.memset(o, c), ap, [], (), w, ())
+
+    def scan(out, a, b, o, r, w):
+        el("v", lambda x, y, z: vec.tensor_tensor_scan(x, y, z, 0.0, o, Op.add), out, [a, b], r, w, ())
+
+    def ac(out, in_, func=AF.Copy, r=(), w=(), b=(), **kw):
+        el("a", lambda o, i: act.activation(o, i, func, **kw), out, [in_], r, w, b)
+
+    def lin(out, in_, sc, bi, r, w):
+        ac(out, in_, AF.Identity, r, w, scale=sc, bias=bi)
+
+    def mm(k, out, terms, r=(), start=True, stop=True):
+        def one(j, l, x):
+            return lambda: pe.matmul(out, l, x, start and j == 0, stop and j == len(terms) - 1)
+        op("p", [one(j, l, x) for j, (l, x) in enumerate(terms)],
+           sum(PY * max(64, x.shape[1]) * (1 if x.dtype in two else 4) for l, x in terms), r, (), (k,))
+
+    def sel(B, a):
+        return B[:, 15 - a:143 - a]
+
+    def conv(B, view):
+        return [(sel(B, a), view(a)) for a in range(16)]
+
+    def iota(out, pat, base, w, r=()):
+        op("g", [lambda: g.iota(out, pat, base, 0, allow_small_or_imprecise_dtypes=True)], 0.13 + 2 * CY * out.shape[1], r, w)
+
+    def late(out, c, w):
+        iota(out, [[0, out.shape[1]]], c, w, ["HG0"])
+
+    def nm(s, r=None):
+        return [s + str(k) + ("" if r is None else "r%d" % r) for k in range(3)]
+
+    def ev(buf, k):
+        return buf[:, 1024 * k:1024 * (k + 1):2]
+
+    def od(buf, k):
+        return buf[:, 1024 * k + 1:1024 * (k + 1):2]
+
+    def ch(buf, k):
+        return buf[:, 512 * k:512 * (k + 1)]
+
+    def mk(a):
+        return T.MK[:, a:a + 1]
+
+    XW = [T["XW%d" % r] for r in range(4)]
+    FW, LA, LB, LS, HG, AB = ([T[s + str(r)] for r in range(3)] for s in ("F", "LA", "LB", "LS", "HG", "AB"))
+    A, U, DX, FL, R, COL = T.A, T.U, T.DX, T.FL, T.R, T.COL
+    K3 = range(3)
+    Xs = [nm("Xe", r) + nm("Xo", r) for r in range(4)]
+
+    for name, out, in_, w, lat in (("ldh", T.HD[:], T.head[:], ["HD"], 2.0), ("ldn", T.NX[:], T.nxt[:], ["NX"], 2.5), ("ldx", T.XW0[:, 0:V], T.x[:], Xs[0], 6.5)):
+        g.sync.dma_start(out, in_).then_inc(S[name], 16)
+        op("x", [], 0.0, (), w, tok=(name, 16), lat=lat)
+    mine = engines_for(T, topo, rank)
+    sent = sum(len(m) for m in mine)
+    inc = sum(len(engines_for(T, topo, (rank + s) % n)[b]) for b, s in enumerate(SHIFTS))
+
+    def heads(r):
+        (cp if r == 0 else ac)(HG[r][:], ix(XW[r][:, 0:V], T.HU[:]), r=Xs[r] + ["HU"], w=["HG%d" % r])
+        trs = []
+        for b, s in enumerate(SHIFTS):
+            rid, pid, _se = topo.addr(T.cores[(rank - s) % n])
+            trs.append(RemoteDMATransfer(dst_ids=[DstId(rid=rid, pnc=pid)], dma_engine_mask=sum(1 << e for e in mine[b]), remote_sem=S["arr%d" % r],
+                                         src=HG[r][:, 64 * b:64 * b + 64], dst=XW[r][:, SP + 64 * b:SP + 64 * b + 64]))
+        op("g", [lambda: g.remote_dma_fused(trs, local_sem=S["snt%d" % r])], 1.0, ["HG%d" % r], ["snt%d" % r], tok=("snt%d" % r, sent), lat=1.3 if r else 4.3)
+        op("x", [], 0.0, ["snt%d" % r], ["gh%d" % r], tok=("arr%d" % r, inc), lat=0.7)
+        dma("s", "cp%d" % r, XW[r + 1][:, 0:V], XW[r][:, 0:V], Xs[r] + ["snt%d" % r], Xs[r + 1], 6.0)
+
+    op("g", [lambda: g.iota(T.PI[:, 0:1], [[0, 1]], 0, 1)], 0.13, (), ["PI"])
+    iota(T.I16[:], [[1, 16]], 0, ["I16"])
+    iota(T.GQ[:], [[1, 8], [0, 16]], 0, ["GQ"])
+    iota(T.AQ[:], [[0, 8], [1, 16]], 0, ["AQ"])
+    iota(T.JJ[:], [[1, 144]], 0, ["JJ"])
+    iota(T.SELF[:], [[1, 2], [32, 96]], 0, ["SELF"])
+    iota(T.LO256[:], [[0, 8], [1, 32]], 0, ["LO256"])
+    iota(T.HI256[:], [[1, 8], [0, 32]], 0, ["HI256"])
+    iota(T.CD[:], [[0, 2], [16, 8]], 3328, ["CD"])
+    ms(FL[:], 0.0, ["Le", "Lo", "Fe", "Fo", "FLp", "FLq"])
+    ts(T.PI[:, 1:2], T.PI[:, 0:1], 15, None, Op.bitwise_and, r=["PI"], w=["PI1"])
+    ts(T.PI[:, 2:3], T.PI[:, 0:1], 4, None, Op.arith_shift_right, r=["PI"], w=["PI2"])
+    ms(XW[0][:, V:SP], 0.0, ["Xd0"])
+    cp(COL[:, 0:3], T.PI[:, 0:3], r=["PI", "PI1", "PI2"], w=["c0"])
+    pa, pg = COL[:, 1:2], COL[:, 2:3]
+    ms(FL[:, 96:102], 1.0, ["FLp"])
+    ms(FL[:, 352:358], 1.0, ["FLq"])
+
+    def col(j, src, m, a, r):
+        lin(COL[:, j:j + 1], src, m, a, r, ["c%d" % j])
+        return COL[:, j:j + 1]
+
+    ts(T.MK[:], T.I16[:], pa, None, Op.is_equal, r=["I16", "c0"], w=["MK"])
+    cg = COL[:, 7:8]
+    ts(cg, pg, 16.0, 15.0, Op.mult, Op.add, r=["c0"], w=["c7"])
+    ts(T.AQm[:], T.GQ[:], pg, 1000.0, Op.not_equal, Op.mult, r=["GQ", "c0"], w=["AQm"])
+    c2a = col(6, pa, 2.0, 0.0, ["c0"])
+    ts(T.BM[:], T.JJ[:], cg, None, Op.is_equal, r=["JJ", "c7"], w=["BM"])
+    tt(T.AQm[:], T.AQm[:], T.AQ[:], Op.add, r=["AQ"], w=["AQm"])
+    cp(T.HU[:], T.HD[:], r=["HD"], w=["HU"])
+    cp(T.NXF[:], T.NX[:], r=["NX"], w=["NXF"])
+    lin(T.GQ[:], T.AQm[:], 2.0, 0.0, ["AQm"], ["AQ2", "GQ"])
+    ts(T.SG[:], T.AQm[:], 100.0, None, Op.is_lt, r=["AQm"], w=["SG"])
+    for M, c in ((T.PE0, 0.0), (T.PE1, -16.0), (T.PO0, 1.0), (T.PO1, -15.0)):
+        ts(M[:], T.GQ[:], c, pa, Op.add, Op.is_equal, r=["AQ2", "c0"], w=["PE%d" % c])
+    mm(6, ps[6][:, 0:96], [(T.PE0[:], T.NXF[:, 0:192:2]), (T.PE1[:], T.NXF[:, 1:192:2])], r=["NXF", "PE0", "PE-16"])
+    mm(6, ps[6][:, 96:192], [(T.PO0[:], T.NXF[:, 0:192:2]), (T.PO1[:], T.NXF[:, 1:192:2])], r=["NXF", "PE1", "PE-15"])
+    lin(T.SELF[:], T.SELF[:], 1.0, c2a, ["c6"], ["SELF"])
+    for a in range(16):
+        lin(T.UMA[:, 144 * a:144 * a + 129], T.BM[:, 11:140], mk(a), 0.0, ["BM", "MK"], ["UMA%d" % a])
+    ts(T.IDb[:], T.AQm[:], pa, None, Op.is_equal, r=["AQm", "c0"], w=["IDb"])
+    Le, Lo, Fe, Fo = FL[:, 0:96], FL[:, 256:352], FL[:, 128:224], FL[:, 384:480]
+    ts(T.T1[:], ps[6][:, 0:192], 3072.0, 192.0, Op.is_ge, Op.mult, w=["T1"], b=[6])
+    ts(Fe, ps[6][:, 0:96], 0.0, None, Op.is_lt, w=["Fe"], b=[6])
+    ts(Fo, ps[6][:, 96:192], 0.0, None, Op.is_lt, w=["Fo"], b=[6])
+    tt(T.T1[:], ps[6][:, 0:192], T.T1[:], Op.add, w=["T1"], b=[6])
+    tt(T.T2[:, 96:192], T.SELF[:, 96:192], Fo, Op.mult, r=["SELF", "Fo"], w=["T2b"])
+    tt(T.T2[:, 0:96], T.SELF[:, 0:96], Fe, Op.mult, r=["SELF", "Fe"], w=["T2"])
+    ts(T.QF[:], Fe, 3072.0, None, Op.mult, r=["Fe"], w=["QF"])
+    tt(T.IDX[:], T.T1[:], T.T2[:], Op.max, r=["T1", "T2", "T2b"], w=["IDX"])
+    heads(0)
+    cp(T.TI[:, 0:96], T.IDX[:, 96:192], r=["IDX"], w=["TI"])
+    tt(T.QF[:], T.QF[:], T.SELF[:, 0:96], Op.max, r=["SELF"], w=["QF"])
+    ts(T.HI[:, 0:96], T.TI[:, 0:96], 31, None, Op.bitwise_and, r=["TI"], w=["HIa"])
+    ts(T.HI[:, 96:192], T.TI[:, 0:96], 5, None, Op.arith_shift_right, r=["TI"], w=["HIb"])
+    cp(T.LZ[:], T.QF[:], r=["QF"], w=["LZ"])
+    cp(T.LOHI[:], T.HI[:], r=["HIa", "HIb"], w=["LOHI"])
+    cp(LS[0][:], T.IDX[:], r=["IDX"], w=["LE0", "LO0"])
+    for k in K3:
+        op("p", [lambda k=k, a=a, h=h: pe.matmul(ps[k][:, a:512:16], T.UMA[:, 144 * a + 1 - h:144 * a + 129 - h],
+                                                 T.LOHI[:, 96 * h + 32 * k:96 * h + 32 * k + 32], h == 0, h == 1)
+                 for a in range(16) for h in range(2)], 32 * 64 * PY, ["LOHI"] + ["UMA%d" % a for a in range(16)], (), (k,))
+    ts(T.LO256[:], T.LO256[:], mk(3), None, Op.mult, r=["MK"], w=["LO256"])
+    ts(T.HI256[:], T.HI256[:], mk(4), None, Op.mult, r=["MK"], w=["HI256"])
+    ts(T.CK[:], T.I16[:], mk(4), 8.0, Op.mult, Op.mult, r=["MK", "I16"], w=["CK"])
+    tt(A[:, 0:256], T.LO256[:], T.HI256[:], Op.add, r=["LO256", "HI256"], w=["A00"])
+    lin(T.IDn[:], T.IDb[:], -1.0, 0.0, ["IDb"], ["IDn"])
+    c34 = col(8, mk(3), 1.0, mk(4), ["MK"])
+    wU = col(9, mk(4), 32.0, mk(3), ["MK"])
+    w12 = col(10, mk(2), 32.0, mk(1), ["MK"])
+    wD = col(15, wU, -1.0, w12, ["c9", "c10"])
+    scA, biA = col(11, mk(0), -2.0, 1.0, ["MK"]), col(12, mk(0), 401.0, 0.0, ["MK"])
+    cT = col(13, mk(0), 0.0, -159.5 * 2048.0, ["MK"])
+    for j in range(1, 14):
+        wd = min(256, W - 256 * j)
+        if j > AV:
+            lin(A[:, 256 * j:256 * j + wd], A[:, 0:wd], 1.0, T.CK[:, j:j + 1], ["A00", "CK"], ["As%d" % j])
+        else:
+            ts(A[:, 256 * j:256 * j + wd], A[:, 0:wd], T.CK[:, j:j + 1], None, Op.add, r=["A00", "CK"], w=["As%d" % j])
+    Ainit = ["A00"] + ["As%d" % j for j in range(1, 14)]
+    for k in K3:
+        ac(od(U, k), ps[k][:], w=["Uo%d" % k], b=[k])
+    ts(T.SELA[:], T.AQm[:], 2.0, pa, Op.add, Op.is_equal, r=["AQm", "c0"], w=["SELA"])
+    ts(T.DG34[:], T.IDb[:], c34, None, Op.mult, r=["IDb", "c8"], w=["DG34"])
+    ts(T.SELA[:], T.SELA[:], c34, None, Op.mult, r=["c8"], w=["SELA"])
+    ts(T.TST[:], T.AQ[:], pa, None, Op.is_gt, r=["AQ", "c0"], w=["TST"])
+    ts(T.CD[:], T.CD[:], pa, None, Op.add, r=["c0"], w=["CD"])
+    for M, wv, nme in ((T.IDf, 1.0, "IDf"), (T.I8192p, 8192.0, "Ip"), (T.I8192n, -8192.0, "In")):
+        ts(M[:], T.IDb[:], wv, None, Op.mult, r=["IDb"], w=[nme])
+    tt(T.TST[:], T.TST[:], T.SG[:], Op.mult, r=["SG"], w=["TST"])
+    for M, wv, rn, nme in ((T.BKn, -8192.0, [], "BKn"), (T.BKp, 8192.0, [], "BKp"), (T.BN, -1.0, [], "BN"), (T.BP0, mk(0), ["MK"], "BP0"),
+                           (T.BD, wD, ["c15"], "BD"), (T.BU, wU, ["c9"], "BU")):
+        ts(M[:], T.BM[:], wv, None, Op.mult, r=["BM"] + rn, w=[nme])
+    tt(T.TGE[:], T.SG[:], T.TST[:], Op.subtract, r=["SG", "TST"], w=["TGE"])
+    tt(T.M1[:], T.TST[:], T.IDb[:], Op.add, r=["TST", "IDb"], w=["M1"])
+    tt(T.BK2[:, 0:143], T.BKp[:, 0:143], T.BKn[:, 1:144], Op.add, r=["BKn", "BKp"], w=["BK2"])
+    tt(T.M2[:], T.TGE[:], T.IDn[:], Op.add, r=["TGE", "IDn"], w=["M2"])
+    tt(T.M1[:], T.M1[:], T.TST[:], Op.add, r=["TST"], w=["M1"])
+    tt(T.M2[:], T.M2[:], T.TGE[:], Op.add, r=["TGE"], w=["M2"])
+    lin(T.SGf[:], T.SG[:], 1.0, 0.0, ["SG"], ["SGf"])
+    for k in K3:
+        ac(ch(T.X0E, k), ix(XW[0][:, 0:SP], T.LZ[:, 32 * k:32 * k + 32]), r=Xs[0] + ["Xd0", "LZ"], w=["X0E%d" % k])
+    late(R[:], 0, ["Rl", "Rf"])
+    for k in K3:
+        late(ev(T.CO, k), 0, ["COz%d" % k])
+    iota(T.BV[:], [[1, 112]], 0, ["BV"])
+    iota(T.N2[:], [[2, 192]], 2, ["N2"])
+    for ap, nme in [(T.ZR[:], "ZR"), (U[:, V:SP], "Ud"), (DX[:, V:SP], "DXd")] + [(XW[r][:, V:SP], "Xd%d" % r) for r in (1, 2, 3)]:
+        late(ap, 0, [nme])
+    for r in K3:
+        late(LA[r][:, 0:192], 0, ["LA%d" % r])
+        late(LB[r][:, 0:192], 0, ["LB%d" % r])
+        for k in K3:
+            late(od(FW[r], k), 255, ["F%d" % r])
+    for M, c in ((T.QE0, 0), (T.QE1, -16), (T.QO0, 1), (T.QO1, -15)):
+        op("g", [lambda M=M, c=c: g.affine_select(M[:], T.SGf[:], [[-32, 8], [-1, 16]], Op.is_equal, 0.0, c, 2)], 0.45, ["SGf", "HG0"], ["Q%d" % c])
+    IDb, IDn, IDf = T.IDb[:], T.IDn[:], T.IDf[:]
+    cI = ["IDb", "IDn"]
+
+    def freed(r):
+        for j in range(0, 96, FC):
+            cp(ix(FW[r][:], LS[r][:, j:j + FC]), AB[r][:, 16 * j:16 * (j + FC)], r=[nm("ABe", r)[j // 32], "LE%d" % r], w=["F%d" % r])
+        mm(0, ps[0][:, 192:288], conv(T.BM, lambda a: FW[r][:, 2 * a + 1:V:32]) + [(T.I8192p[:], Lo), (T.I8192n[:], T.REM[:])],
+           r=["F%d" % r, "Lo", "REM", "Ip", "In"])
+        ts(Fo, ps[0][:, 192:288], 160.0, None, Op.is_lt, w=["Fo"], b=[0])
+
+    for r in range(RO):
+        last = r == RO - 1
+        X, Xn = XW[r], XW[r + 1]
+        Y, Yn = (T.XO, nm("Ye") + nm("Yo")) if last else (Xn, Xs[r + 1])
+        Xall = Xs[r] + ["Xd%d" % r]
+        Xwin = Xall + ["gh%d" % r]
+        Aall = nm("Ao") + Ainit
+        Uall = nm("Uo") + ["Ue0", "Ue1", "Ud"]
+        BE, BO = (1, 6, 1), (2, 7, 0)
+        for k in K3:
+            mm(3 + k, ps[3 + k][:], [(T.SELA[:], od(U, k)), (T.DG34[:], od(A, k))], r=["SELA", "DG34", "Uo%d" % k, "Ao%d" % k] + Ainit, stop=False)
+        if r > 0:
+            freed(r - 1)
+        for k in K3:
+            cp(od(DX, k), ix(X[:], LS[r][:, 96 + 32 * k:128 + 32 * k]), r=Xwin + ["LO%d" % r], w=["DXo%d" % k])
+            mm(BO[k], ps[BO[k]][:], [(IDb, od(DX, k)), (IDn, od(X, k))], r=["DXo%d" % k, Xs[r][3 + k]] + cI)
+            ac(ch(T.ABo, k), ps[BO[k]][:], AF.Abs, w=["ABo%d" % k], b=[BO[k]])
+            ts(od(T.CO, k), ps[BO[k]][:], 1.0, -1.0, Op.min, Op.max, w=["CO%d" % k], b=[BO[k]])
+            mm(3 + k, ps[3 + k][:], [(sel(T.BM, 0), ch(T.ABo, k))], r=["ABo%d" % k, "BM"], start=False)
+            ac(od(A, k), ps[3 + k][:], AF.Relu, scale=scA, bias=biA, r=["c11", "c12"] + Ainit, w=["Ao%d" % k], b=[3 + k])
+            (ac if k in G1A[r] else cp)(ev(DX, k), ix(X[:], LS[r][:, 32 * k:32 * k + 32]), r=Xwin + ["LE%d" % r], w=["DXe%d" % k])
+            mm(BE[k], ps[BE[k]][:], [(IDb, ev(DX, k)), (IDn, ev(X, k))], r=["DXe%d" % k, Xs[r][k]] + cI)
+            ac(ch(AB[r], k), ps[BE[k]][:], AF.Abs, w=[nm("ABe", r)[k]], b=[BE[k]])
+        dma("g", "acc%d" % r, Xn[:, 0:V], T.CO[:], nm("CO") + nm("COz"), Xs[r + 1], 9.0, accum_op=Op.add, max_dma_last_dim=4096)
+        mm(6, ps[6][:, 96:192], conv(T.BM, lambda a: T.ABo[:, a:H:16]), r=nm("ABo") + ["BM"], stop=False)
+        mm(6, ps[6][:, 96:192], [(T.I8192n[:], Fo)], r=["Fo", "In"], start=False)
+        mm(1, ps[1][:, 256:352], conv(T.BM, lambda a: AB[r][:, a:H:16]), r=nm("ABe", r) + ["BM"])
+        for h in range(2):
+            ac(U[:, H * h:H * (h + 1):2], ix(A[:], LS[r][:, 48 * h:48 * h + 48]), r=Aall + ["LE%d" % r], w=["Ue%d" % h])
+        scan(R[:, 129:241], FL[:, 128:240], FL[:, 384:496], Op.add, ["Fe", "Fo", "FLp", "FLq"], ["Rf"])
+        ts(Le, ps[1][:, 256:352], 400.0, None, Op.is_gt, w=["Le"], b=[1])
+        ts(Lo, ps[6][:, 96:192], 400.0, None, Op.is_gt, w=["Lo"], b=[6])
+        scan(R[:, 1:113], FL[:, 0:112], FL[:, 256:368], Op.add, ["Le", "Lo", "FLp", "FLq"], ["Rl"])
+        ac(T.THE[:], ps[1][:, 256:352], AF.Relu, scale=2048.0, bias=cT, r=["c13"], w=["THE"], b=[1])
+        RR = ["Rl", "Rf"]
+        mm(7, ps[7][:, 240:256], conv(T.BM, lambda a: R[:, a:256:16]), r=RR)
+        mm(7, ps[7][:, 256:272], [(sel(T.BKp, 0), R[:, 0:256:16]), (sel(T.BKn, 15), R[:, 16:272:16])]
+           + conv(T.BK2, lambda a: R[:, a:256:16])[1:] + [(IDf, T.CD[:])], r=RR + ["BKp", "BKn", "BK2", "IDf", "CD"])
+        mm(7, ps[7][:, 272:273], [(T.SG[:], R[:, 96:97])], r=RR + ["SG"])
+        mm(2, ps[2][:, 0:240], [(T.M1[:], R[:, 1:241]), (T.M2[:], R[:, 0:240]), (IDb, FL[:, 0:240])], r=RR + ["M1", "M2", "Le", "Fe", "FLp"])
+        ex = [(T.TST[:], R[:, 129:225]), (T.TGE[:], R[:, 128:224])]
+        mm(0, ps[0][:, 0:96], ex + [(T.I8192p[:], Fe)], r=["Rf", "TST", "TGE", "Fe", "Ip"])
+        mm(0, ps[0][:, 96:192], ex + [(IDb, Fe), (T.I8192p[:], Fo)], r=["Rf", "TST", "TGE", "Fe", "Fo", "Ip"])
+        ac(T.CE16[:], ps[7][:, 240:256], w=["CE16"], b=[7])
+        tt(T.OF16[:], ps[7][:, 256:272], T.CE16[:], Op.max, r=["CE16"], w=["OF16"], b=[7])
+        ts(T.THR[:, 0:1], ps[7][:, 272:273], 192.0, 8192.0, Op.min, Op.add, w=["THR"], b=[7])
+        cp(T.OU[:], T.OF16[:], r=["OF16"], w=["OU"])
+        ac(T.SW[:, 0:240], ps[2][:, 0:240], w=["SW"], b=[2])
+        cp(ix(LA[r][:], T.OU[:, 0:7]), T.BV[:], r=["OU", "BV"], w=["LA%d" % r])
+        cp(ix(LB[r][:], T.OU[:, 8:15]), T.BV[:], r=["OU", "BV"], w=["LB%d" % r])
+        scan(T.BS[:, 0:192], LA[r][:, 0:192], T.ZR[:], Op.max, ["LA%d" % r, "ZR"], ["BSa"])
+        scan(T.BS[:, 192:384], LB[r][:, 0:192], T.ZR[:], Op.max, ["LB%d" % r, "ZR"], ["BSb"])
+        mm(7, ps[7][:, 280:304], conv(T.BP0, lambda a: T.BS[:, a:384:16]), r=["BSa", "BSb", "BP0"])
+        cp(T.BL[:], ps[7][:, 280:304], w=["BL"], b=[7])
+        ac(T.BLb[:], ps[7][:, 280:304], AF.Identity, scale=32.0, w=["BLb"], b=[7])
+        tt(T.U2[:, 0:192], ix(T.SW[:, 0:112], T.BL[:, 0:12]), T.N2[:], Op.subtract, r=["SW", "BL", "N2"], w=["U2a"])
+        tt(T.U2[:, 192:384], ix(T.SW[:, 128:240], T.BL[:, 12:24]), T.N2[:], Op.subtract, r=["SW", "BL", "N2"], w=["U2b"])
+        ts(T.CN[:], T.U2[:], -2.0, 0.0, Op.max, Op.min, r=["U2a", "U2b"], w=["CN"])
+        mm(7, ps[7][:, 304:328], conv(T.BN, lambda a: T.CN[:, a:384:16]) + [(IDb, T.BLb[:])], r=["CN", "BLb", "BN"])
+        cp(T.SL[:], ps[7][:, 304:328], w=["SL"], b=[7])
+        ts(T.REM[:], ps[0][:, 96:192], T.THR[:, 0:1], None, Op.is_ge, r=["THR"], w=["REM"], b=[0])
+        ts(Fe, ps[0][:, 0:96], T.THR[:, 0:1], None, Op.is_ge, r=["THR"], w=["Fe"], b=[0])
+        mm(3, ps[3][:, 0:96], conv(T.BP0, lambda a: U[:, 2 * a:V:32]), r=["Ue0", "Ue1", "BP0"])
+        mm(4, ps[4][:, 0:96], conv(T.BD, lambda a: U[:, 2 * a:V:32]), r=["Ue0", "Ue1", "BD"])
+        tt(T.MM[:], ps[3][:, 0:96], T.THE[:], Op.is_gt, r=["THE"], w=["MM"], b=[3])
+        tt(T.MD[:], ps[4][:, 0:96], T.MM[:], Op.mult, r=["MM"], w=["MD"], b=[4])
+        tt(T.I3[:], T.IDX[:, 0:96], T.MD[:], Op.add, r=["IDX", "MD"], w=["I3"])
+        cp(T.L3[:], T.I3[:], r=["I3"], w=["L3"])
+        ac(T.UI[:], ix(U[:], T.SL[:, 0:12]), r=Uall + ["SL"], w=["UI"])
+        mm(7, ps[7][:, 0:192], [(sel(T.BN, 3), T.CN[:, 192:384]), (sel(T.BP0, 4), T.BS[:, 192:384])], r=["CN", "BSb"])
+        mm(7, ps[7][:, 192:384], [(T.DG34[:], T.UI[:])], r=["UI", "DG34"])
+        ac(T.SRC[:], ps[7][:, 0:384], w=["SRC"], b=[7])
+        if last:
+            freed(r)
+        bo = 6 if last else 0
+        cp(ix(U[:], T.SL[:]), T.SRC[:], r=["SL", "SRC"], w=Uall)
+        mm(6, ps[6][:, 288:384], conv(T.BU, lambda a: U[:, 2 * a:V:32]) + [(IDf, T.MD[:]), (T.I8192n[:], Fe)], r=Uall + ["MD", "Fe", "BU"])
+        mm(bo, ps[bo][:, 384:480], conv(T.BU, lambda a: U[:, 2 * a + 1:V:32]) + ([(T.I8192n[:], Fo)] if last else []), r=Uall + ["BU"] + (["Fo"] if last else []))
+        if not last:
+            tt(T.QF[:], T.SELF[:, 0:96], Fe, Op.mult, r=["SELF", "Fe"], w=["QF"])
+            tt(T.IDX[:, 0:96], ps[6][:, 288:384], T.QF[:], Op.max, r=["QF"], w=["IDX"], b=[6])
+            cp(LS[r + 1][:, 0:96], T.IDX[:, 0:96], r=["IDX"], w=["LE%d" % (r + 1)])
+            cp(LS[r + 1][:, 96:192], ps[bo][:, 384:480], w=["LO%d" % (r + 1)], b=[bo])
+        else:
+            ts(T.T1[:], ps[6][:, 288:480], 3072.0, 192.0, Op.is_ge, Op.mult, w=["T1"], b=[6])
+            ts(T.T2[:], ps[6][:, 288:480], -1.0, None, Op.max, w=["T2", "T2b"], b=[6])
+            tt(T.T3[:], T.T2[:], T.T1[:], Op.subtract, r=["T1", "T2"], w=["T3"])
+            mm(6, ps[6][:, 0:192:2], [(T.QE0[:], T.T3[:, 0:96]), (T.QO0[:], T.T3[:, 96:192])], r=["T3", "Q0", "Q1"])
+            mm(6, ps[6][:, 1:192:2], [(T.QE1[:], T.T3[:, 0:96]), (T.QO1[:], T.T3[:, 96:192])], r=["T3", "Q-16", "Q-15"])
+            ac(T.YN[:], ps[6][:, 0:192], w=["YN"], b=[6])
+            dma("a", "stn", T.yn[:], T.YN[:], ["YN"], ["yn"], 4.0)
+        for k in K3:
+            bd, bk = (1, 2, 1)[k], (5, 3, 4)[k]
+            (ac if k in G3A else cp)(ch(T.D3, k), ix(X[:], T.L3[:, 32 * k:32 * k + 32]), r=Xwin + ["L3"], w=["D3%d" % k])
+            mm(bd, ps[bd][:], [(IDb, ch(T.D3, k)), (IDn, ev(X, k))], r=["D3%d" % k, Xs[r][k]])
+            ac(ch(T.CE, k), ps[bd][:], AF.Sign, w=["CE%d" % k], b=[bd])
+            mm(bk, ps[bk][:], [(IDb, ev(X, k) if r > 0 else ch(T.X0E, k)), (IDb, ch(T.CE, k))], r=[Xs[r][k], "X0E%d" % k, "CE%d" % k])
+            ac(ev(Y, k), ps[bk][:], w=[Yn[k]], b=[bk])
+        DXall = nm("DXe") + nm("DXo") + ["DXd", "SL"]
+        ac(T.BB[:, 0:192], ix(X[:, 0:SP], T.SL[:, 0:12]), r=Xall + ["SL"], w=["BBa"])
+        tt(T.DI[:], ix(DX[:], T.SL[:, 0:12]), T.BB[:, 0:192], Op.add, r=DXall + ["BBa"], w=["DI"])
+        ac(T.NI[:], ix(DX[:], T.SL[:, 0:12]), r=DXall, w=["NI"])
+        ts(T.HH[:], T.DI[:], 1, None, Op.arith_shift_right, r=["DI"], w=["HH"])
+        cp(T.BB[:, 192:384], T.HH[:], r=["HH"], w=["BBb"])
+        mm(7, ps[7][:, 0:192], [(IDb, T.BB[:, 192:384]), (IDn, T.BB[:, 0:192])], r=["BBa", "BBb"])
+        mm(7, ps[7][:, 192:384], [(IDb, T.NI[:]), (IDn, T.BB[:, 192:384])], r=["NI", "BBb"])
+        ac(T.CB[:], ps[7][:, 0:384], AF.Sign, w=["CB"], b=[7])
+        if last:
+            ts(T.QF[:], ps[0][:, 192:288], 160.0, 3072.0, Op.is_lt, Op.mult, w=["QF"], b=[0])
+            tt(T.QF[:], T.QF[:], T.SELF[:, 96:192], Op.max, r=["SELF"], w=["QF"])
+            cp(T.LZ[:], T.QF[:], r=["QF"], w=["LZ"])
+            ac(Y[:, 1:H:2], ix(Xn[:, 0:SP], T.LZ[:, 0:48]), r=Xs[3] + ["Xd3", "LZ"], w=["Yo0"])
+            cp(Y[:, H + 1:V:2], ix(Xn[:, 0:SP], T.LZ[:, 48:96]), r=Xs[3] + ["Xd3", "LZ"], w=["Yo1"])
+        tt(ix(Y[:, 0:SP], T.SL[:]), T.CB[:], T.BB[:], Op.add, r=["SL", "CB", "BBa", "BBb"], w=Yn + ([] if last else ["Xd%d" % (r + 1)]))
+        if not last:
+            heads(r + 1)
+        else:
+            dma("s", "stx", T.yx[:], Y[:, 0:V], Yn, ["yx"], 6.0)
+
+    cnt, waited, toks = {e: 0 for e in sem}, {}, {}
+    for i in schedule(nodes):
+        x = nodes[i]
+        e = x["e"]
+        if e != "x":
+            need = {}
+            for d in x["dep"]:
+                name, val = toks[d]
+                if not (name == "p" and e == "p"):
+                    need[name] = max(need.get(name, 0), val)
+            for name in sorted(need):
+                if waited.get((e, name), 0) < need[name]:
+                    q[e].wait_ge(sem[name] if name in sem else S[name], need[name])
+                    waited[(e, name)] = need[name]
+        for fn in x["fns"]:
+            ins = fn()
+            if x["tok"] is None:
+                cnt[e] += 1
+                ins.then_inc(sem[e], 1)
+        toks[i] = x["tok"] or (e, cnt[e])
+    g.sync.wait_ge(S.stx, 16)
+    g.sync.wait_ge(S.stn, 16)
+    for e in sem:
+        g.sync.wait_ge(sem[e], cnt[e])

@@ -1,56 +1,75 @@
+import numpy as np
 from concourse.bass import DstId, RemoteDMATransfer
 from concourse.mybir import AluOpType as Op, ActivationFunctionType as AF
 
-V, H, SP, W, RO = 3072, 1536, 3264, 3456, 3
+V, H, HS, GB, W, RO = 3072, 1536, 1728, 3264, 3456, 3
 SHIFTS = (1, 2, 4)
-G1A = ((0,), (0, 1), (0, 1))
-G3A = (0, 1, 2)
-AV = 8
 FC = 16
-CY, PY, GA, SC, FIX, HOP = 1.04e-3, 0.53e-3, 1.56, 3.8, 0.06, 0.1
-PASSES, JIT = 1000, 0.5
-ORDER = []
+FW = 8192 + W
+FSRC, FTHR = (-3, -1, 9), (0.03, 0.17, 0.65)
+FV = (0, 0, 0)
+EVV = (3, 3, 3)
+L3V = False
+APART = (False, False, False)
+BE = (6, 7, 4)
+CY, GA, SC = np.array([0.83e-3, 1.15e-3, 1.1e-3, 1.0e-3]), np.array([1.56, 1.1, 1.9, 1.3]), np.array([3.8, 1.8, 3.0, 5.3])
+SLOW = (1.0, 1.3, 1.0, 1.2)
+PY, FIX, HOP = CY * np.array([0.55, 0.58, 0.5, 0.55]), dict(v=0.05, a=np.array([0.065, 0.1, 0.065, 0.1])), 0.07
+LAT = dict(h=1.5, n=1.8, x=4.0, acc=4.5, arr0=2.6, arr=2.8, row=1.8, cast=1.8, zero=4.5, stx=2.6, stn=2.2)
+ON_VECTOR = ("G1e", "CO", "Lo", "Le", "Fo", "MM", "PP", "KH", "XD", "YE", "AS", "B")
+TRIES, SEED, SPAN, SHAKE, KEEP = 9000, 1, 5.0, (0.0, 0.5, 1.5, 3.0), 0.1
+PLAN = []
 bf, f32, i32, u16 = "bfloat16", "float32", "int32", "uint16"
-SCRATCH = {}
+SCRATCH, INFO, PLACE = {}, {}, {}
 
 
 def _sb(names, cols, dt):
     for n in names.split():
-        SCRATCH[n] = ("sbuf", [128, cols], dt)
+        pool = n if cols > 600 else "pool_" + dt
+        at = SCRATCH[pool][1][1] if pool in SCRATCH else 0
+        SCRATCH[pool] = ("sbuf", [128, at + (cols + 15) // 16 * 16], dt)
+        INFO[n], PLACE[n] = ("sbuf", cols, dt), (pool, at)
 
 
-_sb("XW0 XW1 XW2 XW3 A F0 F1 F2 LA0 LA1 LA2 LB0 LB1 LB2", W, bf)
-_sb("XO DX U", SP, bf)
-_sb("CO", V, bf)
-_sb("AB0 AB1 AB2 ABo CE D3 X0E", H, bf)
-_sb("HG0 HG1 HG2 LOHI UI NI ZR", 192, bf)
-_sb("BM BN BP0 BD BU BKn BKp BK2", 144, bf)
-_sb("IDb IDn I8192p I8192n M1 M2 TST TGE SG SELA DG34", 128, bf)
-_sb("IDf SGf AQ GQ AQm PE0 PE1 PO0 PO1 QE0 QE1 QO0 QO1", 128, f32)
-_sb("UMA", 16 * 144, bf)
+_sb("XW0 XW1 XW2 XW3 A LA0 LA1 LA2 LB0 LB1 LB2", W, bf)
+_sb("XR", V + 16, bf)
+_sb("XO", V, bf)
+_sb("U DX", GB, bf)
+_sb("FV", FW, bf)
+_sb("FA", FW, f32)
+_sb("SV", RO * 16 * FC, bf)
+_sb("SA", RO * 16 * FC, f32)
+_sb("ABe ABo CE D3", H, bf)
+_sb("LO HI", 512, bf)
+_sb("HG0 HG1 HG2 ZR DD ABh HA KH DH", 192, bf)
+_sb("BM BP0 B01 BZ BU BKn BKp BK2 BHS", 144, bf)
 _sb("JJ", 144, f32)
-_sb("COL MK CD CK CE16 OF16 I16", 16, f32)
+_sb("IDb I8p I8n IDn IHn M1 M2 TST TGE SG SG5", 128, bf)
+_sb("IDf SGf AQ GQ AQm PE0 PE1 PO0 PO1 QE0 QE1 QO0 QO1", 128, f32)
+_sb("COL", 32, f32)
+_sb("MK CD CK CE16 OF16 I16", 16, f32)
 _sb("PI", 8, i32)
-_sb("NX TI HI DI HH", 192, i32)
+_sb("NX TI HH HC", 192, i32)
 _sb("HD", 12, i32)
-_sb("HU", 12, u16)
+_sb("HU HU2", 12, u16)
 _sb("OU", 16, u16)
 _sb("BL SL", 24, u16)
 _sb("BLb", 24, bf)
 _sb("LS0 LS1 LS2", 192, u16)
-_sb("L3 LZ", 96, u16)
-_sb("NXF SELF N2 IDX T1 T2 T3 YN", 192, f32)
-_sb("MD THE I3 QF", 96, f32)
-_sb("MM REM", 96, bf)
-_sb("LO256 HI256 SW", 256, f32)
-_sb("FL", 512, bf)
+_sb("L3 LZ LF", 96, u16)
+_sb("NXF N2 IDX T1 T2 T3 T4 YN HCOL", 192, f32)
+_sb("MD TT QF SE2 SEN SEO", 96, f32)
+_sb("MM NS OK RK", 96, bf)
+_sb("SW", 256, f32)
+_sb("FL", 560, bf)
 _sb("R", 272, bf)
 _sb("BV", 112, bf)
 _sb("THR", 8, f32)
-_sb("BS U2 CN BB CB SRC", 384, bf)
+_sb("BS U2 PP QQ BB CB SRC", 384, bf)
 for _k in range(8):
     SCRATCH["ps%d" % _k] = ("psum", [128, 512], f32)
-SEMAPHORES = ["sv", "sa", "sp", "sg", "ldx", "ldn", "ldh", "stx", "stn"] + [s + str(r) for s in ("arr", "snt", "cp", "acc") for r in range(RO)]
+    INFO["ps%d" % _k], PLACE["ps%d" % _k] = ("psum", 512, f32), ("ps%d" % _k, 0)
+SEMAPHORES = ["sv", "sa", "sp", "sg", "ldx", "ldn", "ldh", "stn", "zfa"] + [s + str(r) for s in ("stx", "arr", "snt", "acc", "okd", "nxd", "fcd") for r in range(RO)]
 
 
 def engines_for(T, topo, q):
@@ -70,20 +89,22 @@ def engines_for(T, topo, q):
     return [out[b] for b in range(3)]
 
 
-def schedule(nodes):
-    if ORDER:
-        return ORDER[0]
-    n = len(nodes)
-    users = [[] for _ in nodes]
-    for i, x in enumerate(nodes):
-        for d in x["dep"]:
+def plan(on_v, on_a):
+    n = len(on_v)
+    before = [sorted(x["dep"]) for x in on_v]
+    users = [[] for _ in on_v]
+    for i in range(n):
+        for d in before[i]:
             users[d].append(i)
-    before = [sorted(x["dep"]) for x in nodes]
-    dur, lat, eng = [x["dur"] for x in nodes], [x["lat"] for x in nodes], [x["e"] for x in nodes]
+    lat = [x["lat"] for x in on_v]
+    cost = {e: [[float((x["dur"] + 0 * CY)[m]) for x in nodes] for m in range(len(CY))] for e, nodes in (("v", on_v), ("a", on_a))}
+    weight = [1.0 / sum(c) for c in cost["v"]]
+    weight = [k / sum(weight) for k in weight]
+    free = [i for i in range(n) if on_v[i]["key"]]
 
-    def place(rank, pred, succ, back):
+    def place(rank, pred, succ, back, eng, dur):
         left, start, est = [len(p) for p in pred], [0.0] * n, [lat[i] if back else 0.0 for i in range(n)]
-        busy = {e: [] for e in eng}
+        busy = {e: [] for e in "vapgsx"}
         ready = [(rank[i], i) for i in range(n) if left[i] == 0]
         while ready:
             m = min(ready)
@@ -105,403 +126,522 @@ def schedule(nodes):
                 left[u] -= 1
                 if left[u] == 0:
                     ready.append((rank[u], u))
-        return start, max(start[i] + dur[i] + lat[i] for i in range(n))
+        return start
 
-    path = [0.0] * n
-    for i in reversed(range(n)):
-        path[i] = dur[i] + lat[i] + max([path[u] for u in users[i]], default=0.0)
-    rank, best, seed = [-p for p in path], None, 1
-    for it in range(PASSES):
-        if it % 2 == 1 and it > 4:
-            rank, amp = [], JIT * (1 + it // 2 % 3)
-            for i in range(n):
-                seed = (seed * 1103515245 + 12345) % 2147483648
-                rank.append(best[1][i] + amp * seed / 2147483648)
-        start, span = place(rank, before, users, False)
-        if best is None or span <= best[0]:
-            best = (span, start)
-        back, _s = place([-(start[i] + dur[i]) for i in range(n)], users, before, True)
-        rank = [-(back[i] + dur[i]) for i in range(n)]
-    ORDER.append(sorted(range(n), key=lambda i: (best[1][i], i)))
-    return ORDER[0]
+    lats = [[x * k for x in lat] for k in SLOW]
+    lat = [x * sum(SLOW) / len(SLOW) for x in lat]
+
+    def replay(order, eng, d, lat):
+        end, at = [0.0] * n, {e: 0.0 for e in "vapgsx"}
+        for i in order:
+            t = at[eng[i]]
+            for j in before[i]:
+                if end[j] > t:
+                    t = end[j]
+            at[eng[i]] = t + d[i]
+            end[i] = t + d[i] + lat[i]
+        return max(end)
+
+    def solve(eng, rank, passes):
+        cases = [[cost["a" if eng[i] == "a" else "v"][m][i] for i in range(n)] for m in range(len(CY))]
+        dur = [sum(c[i] * k for c, k in zip(cases, weight)) for i in range(n)]
+        best = None
+        for it in range(passes):
+            start = place(rank, before, users, False, eng, dur)
+            if passes > 2 or it == 1:
+                order = sorted(range(n), key=lambda i: (start[i], i))
+                spans = [replay(order, eng, c, x) for c, x in zip(cases, lats)]
+                span = sum(s * k for s, k in zip(spans, weight))
+                if best is None or span < best[0]:
+                    best = (span, start, order, eng, spans)
+            if it + 1 < passes:
+                back = place([-(start[i] + dur[i]) for i in range(n)], users, before, True, eng, dur)
+                rank = [-(back[i] + dur[i]) for i in range(n)]
+        return best
+
+    seed = [SEED]
+
+    def draw():
+        seed[0] = (seed[0] * 1103515245 + 12345) % 2147483648
+        return seed[0] / 2147483648
+
+    eng = [("v" if x["key"][0] in ON_VECTOR else "a") if x["key"] else x["e"] for x in on_v]
+    cur = top = solve(eng, list(range(n)), 12)
+    for it in range(TRIES):
+        eng, mid = list(cur[3]), cur[0] * draw()
+        near = [i for i in free if abs(cur[1][i] - mid) < SPAN]
+        for _ in range((0, 1, 1, 2, 2, 3)[int(6 * draw())] if near else 0):
+            i = near[int(len(near) * draw())]
+            eng[i] = "a" if eng[i] == "v" else "v"
+        amp = SHAKE[int(len(SHAKE) * draw())]
+        new = solve(eng, [s + amp * (draw() - 0.5) if abs(s - mid) < SPAN else s for s in cur[1]], 2)
+        if new[0] <= cur[0] + KEEP * (1 - it / TRIES):
+            cur = new
+        if new[0] < top[0]:
+            top = new
+    return {on_v[i]["key"]: top[3][i] for i in free}, top[2], top[4]
+
+
+def v(name, a=0, b=None, s=1):
+    return (name, a, INFO[name][1] if b is None else b, s)
+
+
+def ix(win, off):
+    return ("ix", win, off)
+
+
+def width(x):
+    return 16 * width(x[2]) if x[0] == "ix" else len(range(x[1], x[2], x[3]))
+
+
+def meet(x, y):
+    return x[1] < y[2] and y[1] < x[2] and not (x[3] == y[3] and x[3] > 1 and (x[1] - y[1]) % x[3])
+
+
+def steps(g, T, topo, rank, engine_of):
+    n = len(T.cores)
+    S = T.sem
+    q = {"a": g.scalar, "g": g, "s": g.sync, "x": g.sync}
+    nodes, seen, bank, pending = [], {}, {}, [None]
+
+    def E(*key):
+        pending[0] = key
+        return engine_of(key)
+
+    def ap(x, p=slice(0, 128)):
+        if not isinstance(x, tuple):
+            return x
+        if x[0] == "ix":
+            return ap(x[1]).indirect(ap(x[2]))
+        pool, at = PLACE[x[0]]
+        return T[pool][p, at + x[1]:at + x[2]:x[3]]
+
+    def op(e, fns, dur, r=(), w=(), tok=None, lat=HOP, after=()):
+        i, dep, key = len(nodes), set(), pending[0]
+        pending[0] = None
+        acc = []
+        for x, wr in [(x, False) for x in r] + [(x, True) for x in w]:
+            if isinstance(x, tuple):
+                acc += [(x[1], wr), (x[2], False)] if x[0] == "ix" else [(x, wr)]
+        for k in {x[0] for x, wr in acc if INFO[x[0]][0] == "psum"}:
+            cur, prev = bank.get(k, ([], []))
+            same = e != "p" and cur and nodes[cur[0]]["e"] == e and not key and not nodes[cur[0]]["key"]
+            dep |= set(prev if same else cur)
+            bank[k] = (cur + [i], prev) if same else ([i], cur)
+        acc = [(x, wr) for x, wr in acc if INFO[x[0]][0] != "psum"]
+        for x, wr in acc:
+            dep |= {j for y, yw, j in seen.get(x[0], []) if (wr or yw) and meet(x, y)}
+        for x, wr in acc:
+            old = seen.get(x[0], [])
+            if wr and x[3] == 1:
+                old = [t for t in old if not (x[1] <= t[0][1] and t[0][2] <= x[2])]
+            seen[x[0]] = old + [(x, wr, i)]
+        nodes.append(dict(e=e, fns=fns, dur=dur, lat=lat, dep=dep | set(after), wait=dep, tok=tok, key=key, w=w))
+        return i
+
+    vec, act, pe = g.vector, g.scalar, g.tensor
+
+    def two(x):
+        return INFO[(x[1] if x[0] == "ix" else x)[0]][2] in (bf, u16)
+
+    def el(e, call, out, ins, cols=(), k=1.0, also=(), r=None, w=None):
+        if out[0] == "ix":
+            c = SC * width(out)
+        elif ins and ins[0][0] == "ix":
+            c = GA * width(out)
+        else:
+            c = width(out) * k * (0.5 if e == "v" and all(two(x) for x in [out] + ins) else 1.0)
+        return op(e, [lambda: call(*[ap(x) for x in [out] + ins])], FIX[e] + CY * np.maximum(64, c), r or ins + list(cols), w or [out] + list(also))
+
+    def ts(out, in0, s1, s2, o0, o1=None):
+        el("v", lambda o, i: vec.tensor_scalar(o, i, ap(s1), None, o0) if o1 is None else vec.tensor_scalar(o, i, ap(s1), ap(s2), o0, o1), out, [in0], [s1, s2])
+
+    def tt(out, in0, in1, o):
+        psum = any(x[0].startswith("ps") for x in (in0, in1))
+        el("v", lambda x, y, z: vec.tensor_tensor(x, y, z, o), out, [in0, in1], (), 1.0 if psum else 2.0)
+
+    def cp(out, in_):
+        return el("v", vec.tensor_copy, out, [in_])
+
+    def ms(out, c):
+        el("v", lambda o: vec.memset(o, c), out, [])
+
+    def scan(out, a, b, o):
+        el("v", lambda x, y, z: vec.tensor_tensor_scan(x, y, z, 0.0, o, Op.add), out, [a, b])
+
+    def ac(out, in_, func=AF.Copy, **kw):
+        el("a", lambda o, i: act.activation(o, i, func, **{k: ap(x) for k, x in kw.items()}), out, [in_], kw.values(), also=[kw.get("accum_out")])
+
+    def lin(out, in_, sc, bi, e="a"):
+        if e == "a":
+            ac(out, in_, AF.Identity, scale=sc, bias=bi)
+        else:
+            ts(out, in_, sc, bi, Op.mult, Op.add)
+
+    def move(e, out, in_):
+        (cp if e == "v" else ac)(out, in_)
+
+    def flag(e, out, in_, thr, sc=512.0):
+        if e == "v":
+            ts(out, in_, thr, None, Op.is_gt if sc > 0 else Op.is_lt)
+        else:
+            ac(out, in_, AF.Sigmoid, scale=sc, bias=-sc * thr)
+
+    def step(e, out, in_):
+        if e == "v":
+            ts(out, in_, 1.0, -1.0, Op.min, Op.max)
+        else:
+            ac(out, in_, AF.Sign)
+
+    def mm(out, terms, start=True, stop=True):
+        def one(j, l, x):
+            return lambda: pe.matmul(ap(out), ap(l), ap(x), start and j == 0, stop and j == len(terms) - 1)
+        op("p", [one(j, l, x) for j, (l, x) in enumerate(terms)],
+           sum(PY * max(64, width(x)) * (1 if two(x) else 4) for l, x in terms), [y for t in terms for y in t], [out])
+
+    def conv(B, name, a, b):
+        return [(v(B, 15 - k, 143 - k), v(name, a + k, b, 16)) for k in range(16)]
+
+    def iota(out, pat, base, after=()):
+        op("g", [lambda: g.iota(ap(out), pat, base, 0, allow_small_or_imprecise_dtypes=True)], 0.13 + 2 * CY * width(out), (), [out], after=after)
+
+    def dma(e, name, out, in_, r, w, lat, **kw):
+        op(e, [lambda: q[e].dma_start(out, in_, **kw).then_inc(S[name], 16)], {"g": 1.0, "x": 0.0}.get(e, 0.1), r, w, tok=(name, 16), lat=LAT[lat])
+
+    def ps(k, a=0, b=512, s=1):
+        return v("ps%d" % k, a, b, s)
+
+    def mk(a):
+        return v("MK", a, a + 1)
+
+    def third(name, base, k):
+        return v(name, base + 512 * k, base + 512 * (k + 1))
+
+    K3 = range(3)
+    Le, Fe, REM, Lo, Fo = (v("FL", a, a + 96) for a in (0, 128, 240, 336, 448))
+    IDb, IDn, IDf, I8p, I8n = (v(s) for s in ("IDb", "IDn", "IDf", "I8p", "I8n"))
+
+    for name, out, in_, lat in (("ldh", v("HD"), T.head[:], "h"), ("ldn", v("NX"), T.nxt[:], "n"), ("ldx", v("XR", 0, V), T.x[:], "x")):
+        dma("x", name, ap(out), in_, (), [out], lat)
+    mine = engines_for(T, topo, rank)
+    sent = sum(len(m) for m in mine)
+    inc = sum(len(engines_for(T, topo, (rank + s) % n)[b]) for b, s in enumerate(SHIFTS))
+
+    def send(r):
+        trs = []
+        for b, s in enumerate(SHIFTS):
+            rid, pid, _se = topo.addr(T.cores[(rank - s) % n])
+            trs.append(RemoteDMATransfer(dst_ids=[DstId(rid=rid, pnc=pid)], dma_engine_mask=sum(1 << e for e in mine[b]), remote_sem=S["arr%d" % r],
+                                         src=ap(v("HG%d" % r, 64 * b, 64 * b + 64)), dst=ap(v("XW%d" % r, GB + 64 * b, GB + 64 * b + 64))))
+        i = op("g", [lambda: g.remote_dma_fused(trs, local_sem=S["snt%d" % r])], 1.0 if r else 3.0, [v("HG%d" % r)], (), tok=("snt%d" % r, sent), lat=0.0)
+        op("x", [], 0.0, (), [v("XW%d" % r, GB, W)], tok=("arr%d" % r, inc), lat=LAT["arr" if r else "arr0"], after=[i])
+        return i
+
+    op("g", [lambda: g.iota(ap(v("PI", 0, 1)), [[0, 1]], 0, 1)], 0.13, (), [v("PI", 0, 1)])
+    iota(v("I16"), [[1, 16]], 0)
+    iota(v("GQ"), [[1, 8], [0, 16]], 0)
+    iota(v("AQ"), [[0, 8], [1, 16]], 0)
+    iota(v("JJ"), [[1, 144]], 0)
+    iota(v("SE2"), [[16, 96]], 0)
+    iota(v("LO"), [[0, 32], [1, 16]], 0)
+    iota(v("HI"), [[1, 32], [0, 16]], 0)
+    iota(v("CD"), [[0, 2], [16, 8]], W - 128)
+    ts(v("PI", 1, 2), v("PI", 0, 1), 15, None, Op.bitwise_and)
+    ts(v("PI", 2, 3), v("PI", 0, 1), 4, None, Op.arith_shift_right)
+    cp(v("COL", 0, 3), v("PI", 0, 3))
+    pa, pg = v("COL", 1, 2), v("COL", 2, 3)
+    ms(v("FL"), 0.0)
+    ms(v("FL", 96, 108), 1.0)
+    ms(v("XR", V), 0.0)
+    used = [3]
+
+    def col(src, m, a):
+        used[0] += 1
+        c = v("COL", used[0] - 1, used[0])
+        lin(c, src, m, a, E("col", used[0]))
+        return c
+
+    ts(v("MK"), v("I16"), pa, None, Op.is_equal)
+    cg = col(pg, 16.0, 15.0)
+    ts(v("AQm"), v("GQ"), pg, 1000.0, Op.not_equal, Op.mult)
+    ts(v("BM"), v("JJ"), cg, None, Op.is_equal)
+    tt(v("AQm"), v("AQm"), v("AQ"), Op.add)
+    cp(v("HU"), v("HD"))
+    cp(v("NXF"), v("NX"))
+    lin(v("GQ"), v("AQm"), 2.0, 0.0, E("GQ"))
+    for M, c in (("PE0", 0.0), ("PE1", -16.0), ("PO0", 1.0), ("PO1", -15.0)):
+        ts(v(M), v("GQ"), c, pa, Op.add, Op.is_equal)
+    ts(IDb, v("AQm"), pa, None, Op.is_equal)
+    move(E("HG"), v("HG0"), ix(v("XR", 0, V), v("HU")))
+    first = [send(0)]
+
+    def late(out, c):
+        iota(out, [[0, width(out)]], c, first)
+
+    ac(v("T4"), v("NXF"), AF.Relu, bias=1.0 - V)
+    mm(ps(7, 0, 96), [(v(M), v(N, h, 192, 2)) for N in ("NXF", "T4") for h, M in enumerate(("PE0", "PE1"))])
+    mm(ps(7, 96, 192), [(v(M), v(N, h, 192, 2)) for N in ("NXF", "T4") for h, M in enumerate(("PO0", "PO1"))])
+    nx = ps(7, 0, 192)
+    lin(v("SE2"), v("SE2"), 1.0, pa, E("SE2"))
+    ts(v("TI"), nx, 0.5, -0.25, Op.mult, Op.add)
+    ts(Fe, ps(7, 0, 96), 0.0, None, Op.is_lt)
+    flag("a", Fo, ps(7, 96, 192), -0.5, -512.0)
+    nodes[-1]["dur"] = nodes[-1]["dur"] + 1.3
+    lin(v("T1"), nx, float(HS), 0.0, E("T1"))
+    ts(v("T2"), v("TI"), 0.0, 1.0 - 2 * HS, Op.max, Op.mult)
+    tt(v("QF"), v("SE2"), Fe, Op.mult)
+    tt(v("IDX"), v("T1"), v("T2"), Op.add)
+    cp(v("LS0", 96), v("IDX", 96))
+    IX = v("IDX", 0, 96)
+    tt(IX, IX, v("QF"), Op.max)
+    cp(v("LS0", 0, 96), IX)
+    for M, c in (("IDf", 1.0), ("IDn", -1.0), ("I8p", 8192.0), ("I8n", -8192.0), ("IHn", -0.5)):
+        lin(v(M), IDb, c, 0.0, E("I", M))
+
+    def keep(out, in_, pat, how, base, cm):
+        op("g", [lambda: g.affine_select(ap(out), ap(in_), pat, how, 0.0, base, cm)], 0.17 + 2 * CY * width(out), [in_], [out], after=first)
+
+    lin(v("SEN"), v("SE2"), 2.0, 0.0, E("SEN"))
+    mm(ps(5, 0, 96), [(IDf, v("SEN")), (I8p, Fe)])
+    ts(v("LZ"), ps(5, 0, 96), float(V), None, Op.min)
+    lin(v("LO"), v("LO"), mk(5), mk(2), E("AS", -1))
+    lin(v("HI"), v("HI"), mk(13), 0.0, E("AS", 0))
+    ts(v("CK"), v("I16"), mk(13), 32.0, Op.mult, Op.mult)
+    tt(v("A", 0, 512), v("LO"), v("HI"), Op.add)
+    for j in range(1, 7):
+        wd = min(512, W - 512 * j)
+        lin(v("A", 512 * j, 512 * j + wd), v("A", 0, wd), 1.0, v("CK", j, j + 1), E("AS", j))
+    t5 = col(mk(13), 16.0, mk(5))
+    wZ = col(mk(0), 12288.0, col(mk(2), -12288.0, col(t5, -1.0, col(mk(11), 16.0, mk(3)))))
+    if any(FV):
+        w01 = col(mk(0), 0.0625, 0.0)
+        lin(v("B01"), v("BM"), w01, 0.0, E("B", "B01"))
+    for k in K3:
+        move(E("XE", k), third("XW0", 0, k), ix(v("XR"), v("LZ", 32 * k, 32 * k + 32)))
+        move(E("XD", k), third("XW0", HS, k), v("XR", 1024 * k + 1, 1024 * (k + 1), 2))
+        move(E("UO", k), third("U", HS, k), ix(v("A"), v("LS0", 96 + 32 * k, 128 + 32 * k)))
+    ms(v("XW0", H, HS), 0.0)
+    ts(v("HU2"), v("HD"), 0.5, None, Op.mult)
+    ts(v("SG"), v("AQm"), 100.0, None, Op.is_lt)
+    keep(v("TST"), v("SG"), [[1, 128]], Op.is_gt, 0, -1)
+    keep(v("TGE"), v("SG"), [[-1, 128]], Op.is_ge, 0, 1)
+    ts(v("M1"), v("AQm"), 100.0, 2.0, Op.is_lt, Op.mult)
+    tt(v("M1"), v("M1"), IDb, Op.subtract)
+    keep(v("M2"), v("M1"), [[-1, 128]], Op.is_ge, 0, 1)
+    keep(v("M1"), v("M1"), [[1, 128]], Op.is_ge, 0, -1)
+    lin(v("CD"), v("CD"), 1.0, pa, E("CD"))
+    for M, wv in (("BKn", -8192.0), ("BKp", 8192.0), ("BP0", mk(0)), ("BZ", wZ), ("BU", t5), ("BHS", float(HS))):
+        lin(v(M), v("BM"), wv, 0.0, E("B", M))
+    tt(v("BK2", 0, 143), v("BKp", 0, 143), v("BKn", 1, 144), Op.add)
+    move(E("SGf"), v("SGf"), v("SG"))
+    lin(v("SEO"), v("SE2"), 1.0, float(HS - H), E("SEO"))
+    lin(v("SG5"), v("SG"), t5, 0.0, E("SG5"))
+    move(E("HA"), v("HA"), ix(v("A"), v("HU2")))
+    mm(ps(6, 128, 320), [(v("SG5"), v("HA"))])
+    move(E("HCOL"), v("HCOL"), ps(6, 128, 320))
+    iota(v("BV"), [[1, 112]], 0)
+    iota(v("N2"), [[2, 192]], 2)
+    for out in (v("DX", H, HS), v("R"), v("ZR"), v("U", H, HS)):
+        late(out, 0)
+    for r in K3:
+        late(v("LA%d" % r, 0, 192), 0)
+        late(v("LB%d" % r, 0, 192), 0)
+        late(v("XW%d" % (r + 1), H, HS), 0)
+        late(v("SA", 16 * FC * r, 16 * FC * (r + 1)), FSRC[r])
+        if FV[r]:
+            late(v("SV", 16 * FC * r, 16 * FC * (r + 1)), 4 ** r)
+    for k in K3 if any(FV) else ():
+        late(third("FV", HS, k), 0)
+    dma("g", "zfa", ap(v("FA", HS, GB), slice(0, 128, 16)), ap(v("ZR", 0, 96)), [v("ZR")], [v("FA", HS, GB)], "cast")
+    for M, c in (("QE0", 0), ("QE1", -16), ("QO0", 1), ("QO1", -15)):
+        keep(v(M), v("SGf"), [[-32, 8], [-1, 16]], Op.is_equal, c, 2)
+
+    def freed(r):
+        Fa = v("FA", HS, GB)
+        Fb = v("XR", 0, H)
+        dma("g", "fcd%d" % r, ap(Fb, slice(0, 128, 16)), ap(Fa, slice(0, 128, 16)), [Fa], [Fb], "cast")
+        mm(ps(5, 192, 288), (conv("B01", "FV", HS, GB) if FV[r] else []) + [(I8n, Lo), (I8p, REM)] + conv("BP0", "XR", 0, H))
+        flag(E("Fo", r), Fo, ps(5, 192, 288), FTHR[r], 16384.0)
+
+    def level1(r, hs, k1, k2):
+        a, b, c, d = 128 * hs[0], 128 * hs[-1] + 128, 8 * hs[0], 8 * hs[-1] + 8
+        mm(ps(k1, 16 + c, 16 + d), [(v("BKp", 15, 143), v("R", a, b, 16)), (v("BKn", 0, 128), v("R", a + 16, b + 16, 16))] + conv("BK2", "R", a, b)[1:] + [(IDf, v("CD", c, d))])
+        move(E("CE16", r, hs), v("CE16", c, d), ps(k1, 16 + c, 16 + d))
+        mm(ps(k2, 480 + c, 480 + d), conv("BM", "R", a, b))
+        tt(v("OF16", c, d), ps(k2, 480 + c, 480 + d), v("CE16", c, d), Op.max)
+        cp(v("OU", c, d), v("OF16", c, d))
+        b -= 16
+        mm(ps(k2, a, b), [(v("M1"), v("R", a + 1, b + 1)), (v("M2"), v("R", a, b)), (IDb, v("FL", a, b))])
+        move(E("SW", r, hs), v("SW", a, b), ps(k2, a, b))
+
+    def level2(r, hs, k):
+        a, b, c, d = 192 * hs[0], 192 * hs[-1] + 192, 12 * hs[0], 12 * hs[-1] + 12
+        for h in hs:
+            L = "L%s%d" % ("AB"[h], r)
+            cp(ix(v(L), v("OU", 8 * h, 8 * h + 7)), v("BV"))
+            scan(v("BS", 192 * h, 192 * h + 192), v(L, 0, 192), v("ZR"), Op.max)
+        mm(ps(k, 40 + c, 40 + d), conv("BP0", "BS", a, b))
+        cp(v("BL", c, d), ps(k, 40 + c, 40 + d))
+        lin(v("BLb", c, d), ps(k, 40 + c, 40 + d), 16.0, 0.0, E("BLb", r, hs))
+        for h in hs:
+            tt(v("U2", 192 * h, 192 * h + 192), ix(v("SW", 128 * h, 128 * h + 112), v("BL", 12 * h, 12 * h + 12)), v("N2"), Op.subtract)
+        flag(E("PP", r, hs), v("PP", a, b), v("U2", a, b), -1.5, -512.0)
+        ts(v("QQ", a, b), v("U2", a, b), -1.0, None, Op.is_equal)
+        mm(ps(k, 64 + c, 64 + d), conv("BM", "PP", a, b) + [(IDb, v("BLb", c, d))] + conv("BHS", "QQ", a, b))
+        cp(v("SL", c, d), ps(k, 64 + c, 64 + d))
+
+    for r in range(RO):
+        last = r == RO - 1
+        X, Xn, LS = "XW%d" % r, "XW%d" % (r + 1), "LS%d" % r
+        Ao = v("A", HS, GB)
+        An, Ak = v("A", HS, GB, 2), v("A", HS + 1, GB, 2)
+        dma("s", "nxd%d" % r, ap(Ao, slice(3, 128, 8)), ap(v("U", HS, GB), slice(5, 128, 8)), [v("U", HS, GB)], [An], "row")
+        if r > 0:
+            freed(r - 1)
+        scan(v("R", 129, 241), v("FL", 128, 240), v("FL", 448, 560), Op.add)
+        if APART[r]:
+            level1(r, (1,), 5, 5)
+            level2(r, (1,), 5)
+        for k in K3:
+            move(E("G1o", r, k), third("DX", HS, k), ix(v(X), v(LS, 96 + 32 * k, 128 + 32 * k)))
+            mm(ps(k), [(IDb, third("DX", HS, k)), (IDn, third(X, HS, k))])
+            ac(third("ABo", 0, k), ps(k), AF.Abs)
+            step(E("CO", r, k), third(Xn, HS, k), ps(k))
+        kb = 3 if APART[r] else 5
+        mm(ps(kb, 384, 480), [(v("BM", 15 - k, 143 - k), v("ABo", 96 * k, 96 * (k + 1))) for k in range(16)])
+        flag(E("OK", r), v("OK"), ps(kb, 384, 480), 400.5, -512.0)
+        dma("s", "okd%d" % r, ap(Ao, slice(0, 128, 16)), ap(v("OK")), [v("OK")], [Ak], "row")
+        for k, b in zip(K3, BE):
+            move(E("G1e", r, k), third("DX", 0, k), ix(v(X), v(LS, 32 * k, 32 * k + 32)))
+            mm(ps(b), [(IDb, third("DX", 0, k)), (IDn, third(X, 0, k))])
+            ac(third("ABe", 0, k), ps(b), AF.Abs)
+        dma("g", "acc%d" % r, ap(v(Xn, HS, GB)), ap(v(X, HS, GB)), [v(X, HS, GB), Ak], [v(Xn, HS, GB)], "acc", accum_op=Op.add, max_dma_last_dim=4096)
+        mm(ps(3, 0, 96), conv("BM", "ABo", 0, H) + [(I8n, Fo)])
+        mm(ps(4, 0, 96), conv("BM", "ABe", 0, H))
+        for k in K3:
+            move(E("G2", r, k), third("U", 0, k), ix(v("A"), v(LS, 32 * k, 32 * k + 32)))
+        flag(E("Lo", r), Lo, ps(3, 0, 96), 400.5)
+        flag(E("Le", r), Le, ps(4, 0, 96), 400.5)
+        flag(E("NS", r), v("NS"), ps(4, 0, 96), 159.5)
+        scan(v("R", 1, 113), v("FL", 0, 112), v("FL", 336, 448), Op.add)
+        mm(ps(4, 96, 192), [(IDf, IX), (I8p, v("NS"))])
+        cp(v("LF"), ps(4, 96, 192))
+        for j in range(96 // FC):
+            lst, sv, sa = v("LF", FC * j, FC * (j + 1)), v("SV", 16 * FC * r, 16 * FC * (r + 1)), v("SA", 16 * FC * r, 16 * FC * (r + 1))
+            if j < FV[r]:
+                cp(ix(v("FV"), lst), sv)
+            else:
+                ac(ix(v("FA"), lst), sa, AF.Sigmoid)
+        level1(r, (0,) if APART[r] else (0, 1), 6, 7)
+        mm(ps(7, 496, 497), [(v("SG"), v("R", 96, 97))])
+        ts(v("THR", 0, 1), ps(7, 496, 497), 192.0, 8192.0, Op.min, Op.add)
+        if not last:
+            mm(ps(5, 0, 96), [(v("TST"), v("R", 1, 97)), (v("TGE"), v("R", 0, 96))])
+            ac(v("RK"), ps(5, 0, 96), AF.Sigmoid, scale=-512.0, bias=512.0 * 191.5, accum_out=v("THR", 1, 2))
+            mm(ps(3, 96, 97), [(v("SGf"), v("THR", 1, 2))])
+            ts(v("HA"), v("HCOL"), ps(3, 96, 97), None, Op.is_ge)
+            move(E("ABh", r), v("ABh"), ix(v("ABe"), v("HU2")))
+            mm(ps(3, 288, 480), [(v("SG"), v("ABh")), (I8n, v("HA"))])
+            flag(E("KH", r), v("KH"), ps(3, 288, 480), 400.5)
+        level2(r, (0,) if APART[r] else (0, 1), 6)
+        SI, SF = v("SL", 0, 12), v("SL", 12, 24)
+        mm(ps(7, 240, 352), [(v("TST"), v("R", 129, 241)), (v("TGE"), v("R", 128, 240)), (I8p, v("FL", 128, 240))])
+        mm(ps(7, 352, 448), [(v("TST"), v("R", 129, 225)), (v("TGE"), v("R", 128, 224)), (IDb, Fe), (I8p, Fo)])
+        ts(v("FL", 128, 336), ps(7, 240, 448), v("THR", 0, 1), None, Op.is_ge)
+        mm(ps(5, 96, 192), conv("BZ", "U", 0, H) + [(I8n, v("NS"))])
+        flag(E("MM", r), v("MM"), ps(5, 96, 192), -4096.5)
+        tt(v("MD"), ps(5, 96, 192), v("MM"), Op.mult)
+        if L3V:
+            tt(v("TT"), IX, v("MD"), Op.add)
+            cp(v("L3"), v("TT"))
+        else:
+            mm(ps(5, 384, 480), [(IDf, IX), (IDf, v("MD"))])
+            cp(v("L3"), ps(5, 384, 480))
+        for k in K3:
+            move(E("G3", r, k), third("D3", 0, k), ix(v(X), v("L3", 32 * k, 32 * k + 32)))
+        if not last:
+            move(E("DH", r), v("DH"), ix(v("D3"), v("HU2")))
+            mm(ps(3, 288, 480), [(v("IHn"), v("KH")), (IDn, v("HG%d" % r)), (IDb, v("DH"))])
+            ts(v("HC"), ps(3, 288, 480), 1.0, -1.0, Op.min, Op.max)
+            tt(v("HG%d" % (r + 1)), v("HC"), v("HG%d" % r), Op.add)
+            send(r + 1)
+        for k in K3:
+            mm(ps(k), [(IDb, third("D3", 0, k)), (IDn, third(X, 0, k))])
+            if k < EVV[r]:
+                step(E("CE", r, k), ps(k), ps(k))
+                tt(third(Xn, 0, k), ps(k), third(X, 0, k), Op.add)
+                continue
+            step(E("CE", r, k), third("CE", 0, k), ps(k))
+            mm(ps(k), [(IDb, third(X, 0, k)), (IDb, third("CE", 0, k))])
+            move(E("EV", r, k), third(Xn, 0, k), ps(k))
+        move(E("S1", r), v("SRC", 0, 192), ix(v("A"), SF))
+        move(E("S2", r), v("SRC", 192, 384), ix(v("U"), SI))
+        cp(ix(v("U"), v("SL")), v("SRC"))
+        evens = conv("BU", "U", 0, H) + [(IDf, v("MD")), (I8n, Fe)]
+        odds = conv("BU", "U", HS, GB)
+        if not last:
+            mm(ps(3, 192, 288), odds)
+            mm(ps(4, 192, 288), evens)
+            cp(v("LS%d" % (r + 1), 96), ps(3, 192, 288))
+            tt(v("QF"), v("SE2"), Fe, Op.mult)
+            tt(IX, ps(4, 192, 288), v("QF"), Op.max)
+            cp(v("LS%d" % (r + 1), 0, 96), IX)
+        B1, B2 = v("BB", 0, 192), v("BB", 192, 384)
+        move(E("B1", r), B1, ix(v(X, 0, GB), SI))
+        move(E("NI", r), v("DD"), ix(v("DX"), SI))
+        mm(ps(7, 0, 192), [(IDb, B1), (IDb, v("DD"))])
+        ts(v("HH"), ps(7, 0, 192), 0.5, -0.25, Op.mult, Op.add)
+        cp(B2, v("HH"))
+        mm(ps(6, 128, 320), [(IDb, B2), (IDn, B1)])
+        mm(ps(6, 320, 512), [(IDb, v("DD")), (IDn, B2)])
+        step(E("CB", r), v("CB"), ps(6, 128, 512))
+        tt(ix(v(Xn, 0, GB), v("SL")), v("CB"), v("BB"), Op.add)
+
+    freed(RO - 1)
+    mm(ps(3, 0, 96), [(IDf, v("SEO")), (I8n, Fo)])
+    cp(v("LZ"), ps(3, 0, 96))
+    for k in K3:
+        move(E("Y", k), v("XO", 1024 * k + 1, 1024 * (k + 1), 2), ix(v(Xn, H, GB), v("LZ", 32 * k, 32 * k + 32)))
+        move(E("YE", k), v("XO", 1024 * k, 1024 * (k + 1), 2), third(Xn, 0, k))
+        out = v("XO", 1024 * k, 1024 * (k + 1))
+        dma("s", "stx%d" % k, T.yx[:, 1024 * k:1024 * (k + 1)], ap(out), [out], (), "stx")
+    mm(ps(5, 0, 96), [(IDf, v("MD")), (I8n, Fe)])
+    mm(ps(5, 96, 192), [(I8n, Fo)])
+    move(E("T4"), v("T4"), ps(5, 0, 192))
+    c = ps(4, 192, 384)
+    mm(c, [(IDb, v("ZR"))], stop=False)
+    for h, (Qe, Qo) in enumerate((("QE0", "QO0"), ("QE1", "QO1"))):
+        mm(ps(4, 192 + h, 384, 2), [(v(Qe), v("T4", 0, 96)), (v(Qo), v("T4", 96, 192))], start=False, stop=False)
+    mm(c, [(v("BU", 15 - k, 143 - k), v("U", HS * (k % 2) + k // 2, HS * (k % 2) + H, 8)) for k in range(16)], start=False)
+    ts(v("T1"), c, -0.5, 2.0, Op.max, Op.mult)
+    ts(v("T2"), c, float(HS), 1.0 - 2 * HS, Op.is_ge, Op.mult)
+    ac(v("T3"), c, AF.Abs, bias=float(GB - 1))
+    tt(v("T1"), v("T1"), v("T3"), Op.min)
+    tt(v("YN"), v("T1"), v("T2"), Op.add)
+    dma("s", "stn", T.yn[:], ap(v("YN")), [v("YN")], (), "stn")
+    return nodes, sent
 
 
 def rank_program(g, core, T, topo):
     rank = T.rank_of(core)
     if rank is None:
         return
-    n = len(T.cores)
+    if not PLAN:
+        PLAN.extend(plan(steps(g, T, topo, rank, lambda key: "v")[0], steps(g, T, topo, rank, lambda key: "a")[0]))
+    nodes, sent = steps(g, T, topo, rank, PLAN[0].get)
     S = T.sem
     q = {"v": g.vector, "a": g.scalar, "p": g.tensor, "g": g, "s": g.sync}
     sem = {"v": S.sv, "a": S.sa, "p": S.sp, "g": S.sg}
-    nodes, lastw, readers, bank = [], {}, {}, {}
-
-    def op(e, fns, dur, r=(), w=(), b=(), tok=None, lat=HOP):
-        i = len(nodes)
-        dep = {lastw[x] for x in list(r) + list(w) if x in lastw}
-        for x in w:
-            dep |= set(readers.get(x, []))
-        for k in b:
-            cur, prev = bank.get(k, ([], []))
-            same = e != "p" and cur and nodes[cur[0]]["e"] == e
-            dep |= set(prev if same else cur)
-            bank[k] = (cur + [i], prev) if same else ([i], cur)
-        nodes.append(dict(e=e, fns=fns, dur=dur, lat=lat, dep=dep, tok=tok))
-        for x in r:
-            readers.setdefault(x, []).append(i)
-        for x in w:
-            lastw[x], readers[x] = i, []
-
-    def dma(e, name, out, in_, r, w, lat, **kw):
-        op(e, [lambda: q[e].dma_start(out, in_, **kw).then_inc(S[name], 16)], 1.0 if e == "g" else 0.1, r, w, tok=(name, 16), lat=lat)
-
-    vec, act, pe = g.vector, g.scalar, g.tensor
-    ps = [T["ps%d" % k] for k in range(8)]
-    two = (T.XO.dtype, T.HU.dtype)
-
-    def ix(win, off):
-        return (win.indirect(off), 16 * off.shape[1])
-
-    def el(e, call, out, ins, r, w, b, k=1.0):
-        if isinstance(out, tuple):
-            c = SC * out[1]
-        elif ins and isinstance(ins[0], tuple):
-            c = GA * ins[0][1]
-        else:
-            c = out.shape[1] * k * (0.5 if e == "v" and all(x.dtype in two for x in [out] + ins) else 1.0)
-        a = [x[0] if isinstance(x, tuple) else x for x in [out] + ins]
-        op(e, [lambda: call(*a)], FIX + CY * max(64, c), r, w, b)
-
-    def ts(out, in0, s1, s2, o0, o1=None, r=(), w=(), b=()):
-        el("v", lambda o, i: vec.tensor_scalar(o, i, s1, None, o0) if o1 is None else vec.tensor_scalar(o, i, s1, s2, o0, o1), out, [in0], r, w, b)
-
-    def tt(out, in0, in1, o, r=(), w=(), b=()):
-        el("v", lambda x, y, z: vec.tensor_tensor(x, y, z, o), out, [in0, in1], r, w, b, 1.0 if b else 2.0)
-
-    def cp(out, in_, r=(), w=(), b=()):
-        el("v", vec.tensor_copy, out, [in_], r, w, b)
-
-    def ms(ap, c, w):
-        el("v", lambda o: vec.memset(o, c), ap, [], (), w, ())
-
-    def scan(out, a, b, o, r, w):
-        el("v", lambda x, y, z: vec.tensor_tensor_scan(x, y, z, 0.0, o, Op.add), out, [a, b], r, w, ())
-
-    def ac(out, in_, func=AF.Copy, r=(), w=(), b=(), **kw):
-        el("a", lambda o, i: act.activation(o, i, func, **kw), out, [in_], r, w, b)
-
-    def lin(out, in_, sc, bi, r, w):
-        ac(out, in_, AF.Identity, r, w, scale=sc, bias=bi)
-
-    def mm(k, out, terms, r=(), start=True, stop=True):
-        def one(j, l, x):
-            return lambda: pe.matmul(out, l, x, start and j == 0, stop and j == len(terms) - 1)
-        op("p", [one(j, l, x) for j, (l, x) in enumerate(terms)],
-           sum(PY * max(64, x.shape[1]) * (1 if x.dtype in two else 4) for l, x in terms), r, (), (k,))
-
-    def sel(B, a):
-        return B[:, 15 - a:143 - a]
-
-    def conv(B, view):
-        return [(sel(B, a), view(a)) for a in range(16)]
-
-    def iota(out, pat, base, w, r=()):
-        op("g", [lambda: g.iota(out, pat, base, 0, allow_small_or_imprecise_dtypes=True)], 0.13 + 2 * CY * out.shape[1], r, w)
-
-    def late(out, c, w):
-        iota(out, [[0, out.shape[1]]], c, w, ["HG0"])
-
-    def nm(s, r=None):
-        return [s + str(k) + ("" if r is None else "r%d" % r) for k in range(3)]
-
-    def ev(buf, k):
-        return buf[:, 1024 * k:1024 * (k + 1):2]
-
-    def od(buf, k):
-        return buf[:, 1024 * k + 1:1024 * (k + 1):2]
-
-    def ch(buf, k):
-        return buf[:, 512 * k:512 * (k + 1)]
-
-    def mk(a):
-        return T.MK[:, a:a + 1]
-
-    XW = [T["XW%d" % r] for r in range(4)]
-    FW, LA, LB, LS, HG, AB = ([T[s + str(r)] for r in range(3)] for s in ("F", "LA", "LB", "LS", "HG", "AB"))
-    A, U, DX, FL, R, COL = T.A, T.U, T.DX, T.FL, T.R, T.COL
-    K3 = range(3)
-    Xs = [nm("Xe", r) + nm("Xo", r) for r in range(4)]
-
-    for name, out, in_, w, lat in (("ldh", T.HD[:], T.head[:], ["HD"], 2.0), ("ldn", T.NX[:], T.nxt[:], ["NX"], 2.5), ("ldx", T.XW0[:, 0:V], T.x[:], Xs[0], 6.5)):
-        g.sync.dma_start(out, in_).then_inc(S[name], 16)
-        op("x", [], 0.0, (), w, tok=(name, 16), lat=lat)
-    mine = engines_for(T, topo, rank)
-    sent = sum(len(m) for m in mine)
-    inc = sum(len(engines_for(T, topo, (rank + s) % n)[b]) for b, s in enumerate(SHIFTS))
-
-    def heads(r):
-        (cp if r == 0 else ac)(HG[r][:], ix(XW[r][:, 0:V], T.HU[:]), r=Xs[r] + ["HU"], w=["HG%d" % r])
-        trs = []
-        for b, s in enumerate(SHIFTS):
-            rid, pid, _se = topo.addr(T.cores[(rank - s) % n])
-            trs.append(RemoteDMATransfer(dst_ids=[DstId(rid=rid, pnc=pid)], dma_engine_mask=sum(1 << e for e in mine[b]), remote_sem=S["arr%d" % r],
-                                         src=HG[r][:, 64 * b:64 * b + 64], dst=XW[r][:, SP + 64 * b:SP + 64 * b + 64]))
-        op("g", [lambda: g.remote_dma_fused(trs, local_sem=S["snt%d" % r])], 1.0, ["HG%d" % r], ["snt%d" % r], tok=("snt%d" % r, sent), lat=1.3 if r else 4.3)
-        op("x", [], 0.0, ["snt%d" % r], ["gh%d" % r], tok=("arr%d" % r, inc), lat=0.7)
-        dma("s", "cp%d" % r, XW[r + 1][:, 0:V], XW[r][:, 0:V], Xs[r] + ["snt%d" % r], Xs[r + 1], 6.0)
-
-    op("g", [lambda: g.iota(T.PI[:, 0:1], [[0, 1]], 0, 1)], 0.13, (), ["PI"])
-    iota(T.I16[:], [[1, 16]], 0, ["I16"])
-    iota(T.GQ[:], [[1, 8], [0, 16]], 0, ["GQ"])
-    iota(T.AQ[:], [[0, 8], [1, 16]], 0, ["AQ"])
-    iota(T.JJ[:], [[1, 144]], 0, ["JJ"])
-    iota(T.SELF[:], [[1, 2], [32, 96]], 0, ["SELF"])
-    iota(T.LO256[:], [[0, 8], [1, 32]], 0, ["LO256"])
-    iota(T.HI256[:], [[1, 8], [0, 32]], 0, ["HI256"])
-    iota(T.CD[:], [[0, 2], [16, 8]], 3328, ["CD"])
-    ms(FL[:], 0.0, ["Le", "Lo", "Fe", "Fo", "FLp", "FLq"])
-    ts(T.PI[:, 1:2], T.PI[:, 0:1], 15, None, Op.bitwise_and, r=["PI"], w=["PI1"])
-    ts(T.PI[:, 2:3], T.PI[:, 0:1], 4, None, Op.arith_shift_right, r=["PI"], w=["PI2"])
-    ms(XW[0][:, V:SP], 0.0, ["Xd0"])
-    cp(COL[:, 0:3], T.PI[:, 0:3], r=["PI", "PI1", "PI2"], w=["c0"])
-    pa, pg = COL[:, 1:2], COL[:, 2:3]
-    ms(FL[:, 96:102], 1.0, ["FLp"])
-    ms(FL[:, 352:358], 1.0, ["FLq"])
-
-    def col(j, src, m, a, r):
-        lin(COL[:, j:j + 1], src, m, a, r, ["c%d" % j])
-        return COL[:, j:j + 1]
-
-    ts(T.MK[:], T.I16[:], pa, None, Op.is_equal, r=["I16", "c0"], w=["MK"])
-    cg = COL[:, 7:8]
-    ts(cg, pg, 16.0, 15.0, Op.mult, Op.add, r=["c0"], w=["c7"])
-    ts(T.AQm[:], T.GQ[:], pg, 1000.0, Op.not_equal, Op.mult, r=["GQ", "c0"], w=["AQm"])
-    c2a = col(6, pa, 2.0, 0.0, ["c0"])
-    ts(T.BM[:], T.JJ[:], cg, None, Op.is_equal, r=["JJ", "c7"], w=["BM"])
-    tt(T.AQm[:], T.AQm[:], T.AQ[:], Op.add, r=["AQ"], w=["AQm"])
-    cp(T.HU[:], T.HD[:], r=["HD"], w=["HU"])
-    cp(T.NXF[:], T.NX[:], r=["NX"], w=["NXF"])
-    lin(T.GQ[:], T.AQm[:], 2.0, 0.0, ["AQm"], ["AQ2", "GQ"])
-    ts(T.SG[:], T.AQm[:], 100.0, None, Op.is_lt, r=["AQm"], w=["SG"])
-    for M, c in ((T.PE0, 0.0), (T.PE1, -16.0), (T.PO0, 1.0), (T.PO1, -15.0)):
-        ts(M[:], T.GQ[:], c, pa, Op.add, Op.is_equal, r=["AQ2", "c0"], w=["PE%d" % c])
-    mm(6, ps[6][:, 0:96], [(T.PE0[:], T.NXF[:, 0:192:2]), (T.PE1[:], T.NXF[:, 1:192:2])], r=["NXF", "PE0", "PE-16"])
-    mm(6, ps[6][:, 96:192], [(T.PO0[:], T.NXF[:, 0:192:2]), (T.PO1[:], T.NXF[:, 1:192:2])], r=["NXF", "PE1", "PE-15"])
-    lin(T.SELF[:], T.SELF[:], 1.0, c2a, ["c6"], ["SELF"])
-    for a in range(16):
-        lin(T.UMA[:, 144 * a:144 * a + 129], T.BM[:, 11:140], mk(a), 0.0, ["BM", "MK"], ["UMA%d" % a])
-    ts(T.IDb[:], T.AQm[:], pa, None, Op.is_equal, r=["AQm", "c0"], w=["IDb"])
-    Le, Lo, Fe, Fo = FL[:, 0:96], FL[:, 256:352], FL[:, 128:224], FL[:, 384:480]
-    ts(T.T1[:], ps[6][:, 0:192], 3072.0, 192.0, Op.is_ge, Op.mult, w=["T1"], b=[6])
-    ts(Fe, ps[6][:, 0:96], 0.0, None, Op.is_lt, w=["Fe"], b=[6])
-    ts(Fo, ps[6][:, 96:192], 0.0, None, Op.is_lt, w=["Fo"], b=[6])
-    tt(T.T1[:], ps[6][:, 0:192], T.T1[:], Op.add, w=["T1"], b=[6])
-    tt(T.T2[:, 96:192], T.SELF[:, 96:192], Fo, Op.mult, r=["SELF", "Fo"], w=["T2b"])
-    tt(T.T2[:, 0:96], T.SELF[:, 0:96], Fe, Op.mult, r=["SELF", "Fe"], w=["T2"])
-    ts(T.QF[:], Fe, 3072.0, None, Op.mult, r=["Fe"], w=["QF"])
-    tt(T.IDX[:], T.T1[:], T.T2[:], Op.max, r=["T1", "T2", "T2b"], w=["IDX"])
-    heads(0)
-    cp(T.TI[:, 0:96], T.IDX[:, 96:192], r=["IDX"], w=["TI"])
-    tt(T.QF[:], T.QF[:], T.SELF[:, 0:96], Op.max, r=["SELF"], w=["QF"])
-    ts(T.HI[:, 0:96], T.TI[:, 0:96], 31, None, Op.bitwise_and, r=["TI"], w=["HIa"])
-    ts(T.HI[:, 96:192], T.TI[:, 0:96], 5, None, Op.arith_shift_right, r=["TI"], w=["HIb"])
-    cp(T.LZ[:], T.QF[:], r=["QF"], w=["LZ"])
-    cp(T.LOHI[:], T.HI[:], r=["HIa", "HIb"], w=["LOHI"])
-    cp(LS[0][:], T.IDX[:], r=["IDX"], w=["LE0", "LO0"])
-    for k in K3:
-        op("p", [lambda k=k, a=a, h=h: pe.matmul(ps[k][:, a:512:16], T.UMA[:, 144 * a + 1 - h:144 * a + 129 - h],
-                                                 T.LOHI[:, 96 * h + 32 * k:96 * h + 32 * k + 32], h == 0, h == 1)
-                 for a in range(16) for h in range(2)], 32 * 64 * PY, ["LOHI"] + ["UMA%d" % a for a in range(16)], (), (k,))
-    ts(T.LO256[:], T.LO256[:], mk(3), None, Op.mult, r=["MK"], w=["LO256"])
-    ts(T.HI256[:], T.HI256[:], mk(4), None, Op.mult, r=["MK"], w=["HI256"])
-    ts(T.CK[:], T.I16[:], mk(4), 8.0, Op.mult, Op.mult, r=["MK", "I16"], w=["CK"])
-    tt(A[:, 0:256], T.LO256[:], T.HI256[:], Op.add, r=["LO256", "HI256"], w=["A00"])
-    lin(T.IDn[:], T.IDb[:], -1.0, 0.0, ["IDb"], ["IDn"])
-    c34 = col(8, mk(3), 1.0, mk(4), ["MK"])
-    wU = col(9, mk(4), 32.0, mk(3), ["MK"])
-    w12 = col(10, mk(2), 32.0, mk(1), ["MK"])
-    wD = col(15, wU, -1.0, w12, ["c9", "c10"])
-    scA, biA = col(11, mk(0), -2.0, 1.0, ["MK"]), col(12, mk(0), 401.0, 0.0, ["MK"])
-    cT = col(13, mk(0), 0.0, -159.5 * 2048.0, ["MK"])
-    for j in range(1, 14):
-        wd = min(256, W - 256 * j)
-        if j > AV:
-            lin(A[:, 256 * j:256 * j + wd], A[:, 0:wd], 1.0, T.CK[:, j:j + 1], ["A00", "CK"], ["As%d" % j])
-        else:
-            ts(A[:, 256 * j:256 * j + wd], A[:, 0:wd], T.CK[:, j:j + 1], None, Op.add, r=["A00", "CK"], w=["As%d" % j])
-    Ainit = ["A00"] + ["As%d" % j for j in range(1, 14)]
-    for k in K3:
-        ac(od(U, k), ps[k][:], w=["Uo%d" % k], b=[k])
-    ts(T.SELA[:], T.AQm[:], 2.0, pa, Op.add, Op.is_equal, r=["AQm", "c0"], w=["SELA"])
-    ts(T.DG34[:], T.IDb[:], c34, None, Op.mult, r=["IDb", "c8"], w=["DG34"])
-    ts(T.SELA[:], T.SELA[:], c34, None, Op.mult, r=["c8"], w=["SELA"])
-    ts(T.TST[:], T.AQ[:], pa, None, Op.is_gt, r=["AQ", "c0"], w=["TST"])
-    ts(T.CD[:], T.CD[:], pa, None, Op.add, r=["c0"], w=["CD"])
-    for M, wv, nme in ((T.IDf, 1.0, "IDf"), (T.I8192p, 8192.0, "Ip"), (T.I8192n, -8192.0, "In")):
-        ts(M[:], T.IDb[:], wv, None, Op.mult, r=["IDb"], w=[nme])
-    tt(T.TST[:], T.TST[:], T.SG[:], Op.mult, r=["SG"], w=["TST"])
-    for M, wv, rn, nme in ((T.BKn, -8192.0, [], "BKn"), (T.BKp, 8192.0, [], "BKp"), (T.BN, -1.0, [], "BN"), (T.BP0, mk(0), ["MK"], "BP0"),
-                           (T.BD, wD, ["c15"], "BD"), (T.BU, wU, ["c9"], "BU")):
-        ts(M[:], T.BM[:], wv, None, Op.mult, r=["BM"] + rn, w=[nme])
-    tt(T.TGE[:], T.SG[:], T.TST[:], Op.subtract, r=["SG", "TST"], w=["TGE"])
-    tt(T.M1[:], T.TST[:], T.IDb[:], Op.add, r=["TST", "IDb"], w=["M1"])
-    tt(T.BK2[:, 0:143], T.BKp[:, 0:143], T.BKn[:, 1:144], Op.add, r=["BKn", "BKp"], w=["BK2"])
-    tt(T.M2[:], T.TGE[:], T.IDn[:], Op.add, r=["TGE", "IDn"], w=["M2"])
-    tt(T.M1[:], T.M1[:], T.TST[:], Op.add, r=["TST"], w=["M1"])
-    tt(T.M2[:], T.M2[:], T.TGE[:], Op.add, r=["TGE"], w=["M2"])
-    lin(T.SGf[:], T.SG[:], 1.0, 0.0, ["SG"], ["SGf"])
-    for k in K3:
-        ac(ch(T.X0E, k), ix(XW[0][:, 0:SP], T.LZ[:, 32 * k:32 * k + 32]), r=Xs[0] + ["Xd0", "LZ"], w=["X0E%d" % k])
-    late(R[:], 0, ["Rl", "Rf"])
-    for k in K3:
-        late(ev(T.CO, k), 0, ["COz%d" % k])
-    iota(T.BV[:], [[1, 112]], 0, ["BV"])
-    iota(T.N2[:], [[2, 192]], 2, ["N2"])
-    for ap, nme in [(T.ZR[:], "ZR"), (U[:, V:SP], "Ud"), (DX[:, V:SP], "DXd")] + [(XW[r][:, V:SP], "Xd%d" % r) for r in (1, 2, 3)]:
-        late(ap, 0, [nme])
-    for r in K3:
-        late(LA[r][:, 0:192], 0, ["LA%d" % r])
-        late(LB[r][:, 0:192], 0, ["LB%d" % r])
-        for k in K3:
-            late(od(FW[r], k), 255, ["F%d" % r])
-    for M, c in ((T.QE0, 0), (T.QE1, -16), (T.QO0, 1), (T.QO1, -15)):
-        op("g", [lambda M=M, c=c: g.affine_select(M[:], T.SGf[:], [[-32, 8], [-1, 16]], Op.is_equal, 0.0, c, 2)], 0.45, ["SGf", "HG0"], ["Q%d" % c])
-    IDb, IDn, IDf = T.IDb[:], T.IDn[:], T.IDf[:]
-    cI = ["IDb", "IDn"]
-
-    def freed(r):
-        for j in range(0, 96, FC):
-            cp(ix(FW[r][:], LS[r][:, j:j + FC]), AB[r][:, 16 * j:16 * (j + FC)], r=[nm("ABe", r)[j // 32], "LE%d" % r], w=["F%d" % r])
-        mm(0, ps[0][:, 192:288], conv(T.BM, lambda a: FW[r][:, 2 * a + 1:V:32]) + [(T.I8192p[:], Lo), (T.I8192n[:], T.REM[:])],
-           r=["F%d" % r, "Lo", "REM", "Ip", "In"])
-        ts(Fo, ps[0][:, 192:288], 160.0, None, Op.is_lt, w=["Fo"], b=[0])
-
-    for r in range(RO):
-        last = r == RO - 1
-        X, Xn = XW[r], XW[r + 1]
-        Y, Yn = (T.XO, nm("Ye") + nm("Yo")) if last else (Xn, Xs[r + 1])
-        Xall = Xs[r] + ["Xd%d" % r]
-        Xwin = Xall + ["gh%d" % r]
-        Aall = nm("Ao") + Ainit
-        Uall = nm("Uo") + ["Ue0", "Ue1", "Ud"]
-        BE, BO = (1, 6, 1), (2, 7, 0)
-        for k in K3:
-            mm(3 + k, ps[3 + k][:], [(T.SELA[:], od(U, k)), (T.DG34[:], od(A, k))], r=["SELA", "DG34", "Uo%d" % k, "Ao%d" % k] + Ainit, stop=False)
-        if r > 0:
-            freed(r - 1)
-        for k in K3:
-            cp(od(DX, k), ix(X[:], LS[r][:, 96 + 32 * k:128 + 32 * k]), r=Xwin + ["LO%d" % r], w=["DXo%d" % k])
-            mm(BO[k], ps[BO[k]][:], [(IDb, od(DX, k)), (IDn, od(X, k))], r=["DXo%d" % k, Xs[r][3 + k]] + cI)
-            ac(ch(T.ABo, k), ps[BO[k]][:], AF.Abs, w=["ABo%d" % k], b=[BO[k]])
-            ts(od(T.CO, k), ps[BO[k]][:], 1.0, -1.0, Op.min, Op.max, w=["CO%d" % k], b=[BO[k]])
-            mm(3 + k, ps[3 + k][:], [(sel(T.BM, 0), ch(T.ABo, k))], r=["ABo%d" % k, "BM"], start=False)
-            ac(od(A, k), ps[3 + k][:], AF.Relu, scale=scA, bias=biA, r=["c11", "c12"] + Ainit, w=["Ao%d" % k], b=[3 + k])
-            (ac if k in G1A[r] else cp)(ev(DX, k), ix(X[:], LS[r][:, 32 * k:32 * k + 32]), r=Xwin + ["LE%d" % r], w=["DXe%d" % k])
-            mm(BE[k], ps[BE[k]][:], [(IDb, ev(DX, k)), (IDn, ev(X, k))], r=["DXe%d" % k, Xs[r][k]] + cI)
-            ac(ch(AB[r], k), ps[BE[k]][:], AF.Abs, w=[nm("ABe", r)[k]], b=[BE[k]])
-        dma("g", "acc%d" % r, Xn[:, 0:V], T.CO[:], nm("CO") + nm("COz"), Xs[r + 1], 9.0, accum_op=Op.add, max_dma_last_dim=4096)
-        mm(6, ps[6][:, 96:192], conv(T.BM, lambda a: T.ABo[:, a:H:16]), r=nm("ABo") + ["BM"], stop=False)
-        mm(6, ps[6][:, 96:192], [(T.I8192n[:], Fo)], r=["Fo", "In"], start=False)
-        mm(1, ps[1][:, 256:352], conv(T.BM, lambda a: AB[r][:, a:H:16]), r=nm("ABe", r) + ["BM"])
-        for h in range(2):
-            ac(U[:, H * h:H * (h + 1):2], ix(A[:], LS[r][:, 48 * h:48 * h + 48]), r=Aall + ["LE%d" % r], w=["Ue%d" % h])
-        scan(R[:, 129:241], FL[:, 128:240], FL[:, 384:496], Op.add, ["Fe", "Fo", "FLp", "FLq"], ["Rf"])
-        ts(Le, ps[1][:, 256:352], 400.0, None, Op.is_gt, w=["Le"], b=[1])
-        ts(Lo, ps[6][:, 96:192], 400.0, None, Op.is_gt, w=["Lo"], b=[6])
-        scan(R[:, 1:113], FL[:, 0:112], FL[:, 256:368], Op.add, ["Le", "Lo", "FLp", "FLq"], ["Rl"])
-        ac(T.THE[:], ps[1][:, 256:352], AF.Relu, scale=2048.0, bias=cT, r=["c13"], w=["THE"], b=[1])
-        RR = ["Rl", "Rf"]
-        mm(7, ps[7][:, 240:256], conv(T.BM, lambda a: R[:, a:256:16]), r=RR)
-        mm(7, ps[7][:, 256:272], [(sel(T.BKp, 0), R[:, 0:256:16]), (sel(T.BKn, 15), R[:, 16:272:16])]
-           + conv(T.BK2, lambda a: R[:, a:256:16])[1:] + [(IDf, T.CD[:])], r=RR + ["BKp", "BKn", "BK2", "IDf", "CD"])
-        mm(7, ps[7][:, 272:273], [(T.SG[:], R[:, 96:97])], r=RR + ["SG"])
-        mm(2, ps[2][:, 0:240], [(T.M1[:], R[:, 1:241]), (T.M2[:], R[:, 0:240]), (IDb, FL[:, 0:240])], r=RR + ["M1", "M2", "Le", "Fe", "FLp"])
-        ex = [(T.TST[:], R[:, 129:225]), (T.TGE[:], R[:, 128:224])]
-        mm(0, ps[0][:, 0:96], ex + [(T.I8192p[:], Fe)], r=["Rf", "TST", "TGE", "Fe", "Ip"])
-        mm(0, ps[0][:, 96:192], ex + [(IDb, Fe), (T.I8192p[:], Fo)], r=["Rf", "TST", "TGE", "Fe", "Fo", "Ip"])
-        ac(T.CE16[:], ps[7][:, 240:256], w=["CE16"], b=[7])
-        tt(T.OF16[:], ps[7][:, 256:272], T.CE16[:], Op.max, r=["CE16"], w=["OF16"], b=[7])
-        ts(T.THR[:, 0:1], ps[7][:, 272:273], 192.0, 8192.0, Op.min, Op.add, w=["THR"], b=[7])
-        cp(T.OU[:], T.OF16[:], r=["OF16"], w=["OU"])
-        ac(T.SW[:, 0:240], ps[2][:, 0:240], w=["SW"], b=[2])
-        cp(ix(LA[r][:], T.OU[:, 0:7]), T.BV[:], r=["OU", "BV"], w=["LA%d" % r])
-        cp(ix(LB[r][:], T.OU[:, 8:15]), T.BV[:], r=["OU", "BV"], w=["LB%d" % r])
-        scan(T.BS[:, 0:192], LA[r][:, 0:192], T.ZR[:], Op.max, ["LA%d" % r, "ZR"], ["BSa"])
-        scan(T.BS[:, 192:384], LB[r][:, 0:192], T.ZR[:], Op.max, ["LB%d" % r, "ZR"], ["BSb"])
-        mm(7, ps[7][:, 280:304], conv(T.BP0, lambda a: T.BS[:, a:384:16]), r=["BSa", "BSb", "BP0"])
-        cp(T.BL[:], ps[7][:, 280:304], w=["BL"], b=[7])
-        ac(T.BLb[:], ps[7][:, 280:304], AF.Identity, scale=32.0, w=["BLb"], b=[7])
-        tt(T.U2[:, 0:192], ix(T.SW[:, 0:112], T.BL[:, 0:12]), T.N2[:], Op.subtract, r=["SW", "BL", "N2"], w=["U2a"])
-        tt(T.U2[:, 192:384], ix(T.SW[:, 128:240], T.BL[:, 12:24]), T.N2[:], Op.subtract, r=["SW", "BL", "N2"], w=["U2b"])
-        ts(T.CN[:], T.U2[:], -2.0, 0.0, Op.max, Op.min, r=["U2a", "U2b"], w=["CN"])
-        mm(7, ps[7][:, 304:328], conv(T.BN, lambda a: T.CN[:, a:384:16]) + [(IDb, T.BLb[:])], r=["CN", "BLb", "BN"])
-        cp(T.SL[:], ps[7][:, 304:328], w=["SL"], b=[7])
-        ts(T.REM[:], ps[0][:, 96:192], T.THR[:, 0:1], None, Op.is_ge, r=["THR"], w=["REM"], b=[0])
-        ts(Fe, ps[0][:, 0:96], T.THR[:, 0:1], None, Op.is_ge, r=["THR"], w=["Fe"], b=[0])
-        mm(3, ps[3][:, 0:96], conv(T.BP0, lambda a: U[:, 2 * a:V:32]), r=["Ue0", "Ue1", "BP0"])
-        mm(4, ps[4][:, 0:96], conv(T.BD, lambda a: U[:, 2 * a:V:32]), r=["Ue0", "Ue1", "BD"])
-        tt(T.MM[:], ps[3][:, 0:96], T.THE[:], Op.is_gt, r=["THE"], w=["MM"], b=[3])
-        tt(T.MD[:], ps[4][:, 0:96], T.MM[:], Op.mult, r=["MM"], w=["MD"], b=[4])
-        tt(T.I3[:], T.IDX[:, 0:96], T.MD[:], Op.add, r=["IDX", "MD"], w=["I3"])
-        cp(T.L3[:], T.I3[:], r=["I3"], w=["L3"])
-        ac(T.UI[:], ix(U[:], T.SL[:, 0:12]), r=Uall + ["SL"], w=["UI"])
-        mm(7, ps[7][:, 0:192], [(sel(T.BN, 3), T.CN[:, 192:384]), (sel(T.BP0, 4), T.BS[:, 192:384])], r=["CN", "BSb"])
-        mm(7, ps[7][:, 192:384], [(T.DG34[:], T.UI[:])], r=["UI", "DG34"])
-        ac(T.SRC[:], ps[7][:, 0:384], w=["SRC"], b=[7])
-        if last:
-            freed(r)
-        bo = 6 if last else 0
-        cp(ix(U[:], T.SL[:]), T.SRC[:], r=["SL", "SRC"], w=Uall)
-        mm(6, ps[6][:, 288:384], conv(T.BU, lambda a: U[:, 2 * a:V:32]) + [(IDf, T.MD[:]), (T.I8192n[:], Fe)], r=Uall + ["MD", "Fe", "BU"])
-        mm(bo, ps[bo][:, 384:480], conv(T.BU, lambda a: U[:, 2 * a + 1:V:32]) + ([(T.I8192n[:], Fo)] if last else []), r=Uall + ["BU"] + (["Fo"] if last else []))
-        if not last:
-            tt(T.QF[:], T.SELF[:, 0:96], Fe, Op.mult, r=["SELF", "Fe"], w=["QF"])
-            tt(T.IDX[:, 0:96], ps[6][:, 288:384], T.QF[:], Op.max, r=["QF"], w=["IDX"], b=[6])
-            cp(LS[r + 1][:, 0:96], T.IDX[:, 0:96], r=["IDX"], w=["LE%d" % (r + 1)])
-            cp(LS[r + 1][:, 96:192], ps[bo][:, 384:480], w=["LO%d" % (r + 1)], b=[bo])
-        else:
-            ts(T.T1[:], ps[6][:, 288:480], 3072.0, 192.0, Op.is_ge, Op.mult, w=["T1"], b=[6])
-            ts(T.T2[:], ps[6][:, 288:480], -1.0, None, Op.max, w=["T2", "T2b"], b=[6])
-            tt(T.T3[:], T.T2[:], T.T1[:], Op.subtract, r=["T1", "T2"], w=["T3"])
-            mm(6, ps[6][:, 0:192:2], [(T.QE0[:], T.T3[:, 0:96]), (T.QO0[:], T.T3[:, 96:192])], r=["T3", "Q0", "Q1"])
-            mm(6, ps[6][:, 1:192:2], [(T.QE1[:], T.T3[:, 0:96]), (T.QO1[:], T.T3[:, 96:192])], r=["T3", "Q-16", "Q-15"])
-            ac(T.YN[:], ps[6][:, 0:192], w=["YN"], b=[6])
-            dma("a", "stn", T.yn[:], T.YN[:], ["YN"], ["yn"], 4.0)
-        for k in K3:
-            bd, bk = (1, 2, 1)[k], (5, 3, 4)[k]
-            (ac if k in G3A else cp)(ch(T.D3, k), ix(X[:], T.L3[:, 32 * k:32 * k + 32]), r=Xwin + ["L3"], w=["D3%d" % k])
-            mm(bd, ps[bd][:], [(IDb, ch(T.D3, k)), (IDn, ev(X, k))], r=["D3%d" % k, Xs[r][k]])
-            ac(ch(T.CE, k), ps[bd][:], AF.Sign, w=["CE%d" % k], b=[bd])
-            mm(bk, ps[bk][:], [(IDb, ev(X, k) if r > 0 else ch(T.X0E, k)), (IDb, ch(T.CE, k))], r=[Xs[r][k], "X0E%d" % k, "CE%d" % k])
-            ac(ev(Y, k), ps[bk][:], w=[Yn[k]], b=[bk])
-        DXall = nm("DXe") + nm("DXo") + ["DXd", "SL"]
-        ac(T.BB[:, 0:192], ix(X[:, 0:SP], T.SL[:, 0:12]), r=Xall + ["SL"], w=["BBa"])
-        tt(T.DI[:], ix(DX[:], T.SL[:, 0:12]), T.BB[:, 0:192], Op.add, r=DXall + ["BBa"], w=["DI"])
-        ac(T.NI[:], ix(DX[:], T.SL[:, 0:12]), r=DXall, w=["NI"])
-        ts(T.HH[:], T.DI[:], 1, None, Op.arith_shift_right, r=["DI"], w=["HH"])
-        cp(T.BB[:, 192:384], T.HH[:], r=["HH"], w=["BBb"])
-        mm(7, ps[7][:, 0:192], [(IDb, T.BB[:, 192:384]), (IDn, T.BB[:, 0:192])], r=["BBa", "BBb"])
-        mm(7, ps[7][:, 192:384], [(IDb, T.NI[:]), (IDn, T.BB[:, 192:384])], r=["NI", "BBb"])
-        ac(T.CB[:], ps[7][:, 0:384], AF.Sign, w=["CB"], b=[7])
-        if last:
-            ts(T.QF[:], ps[0][:, 192:288], 160.0, 3072.0, Op.is_lt, Op.mult, w=["QF"], b=[0])
-            tt(T.QF[:], T.QF[:], T.SELF[:, 96:192], Op.max, r=["SELF"], w=["QF"])
-            cp(T.LZ[:], T.QF[:], r=["QF"], w=["LZ"])
-            ac(Y[:, 1:H:2], ix(Xn[:, 0:SP], T.LZ[:, 0:48]), r=Xs[3] + ["Xd3", "LZ"], w=["Yo0"])
-            cp(Y[:, H + 1:V:2], ix(Xn[:, 0:SP], T.LZ[:, 48:96]), r=Xs[3] + ["Xd3", "LZ"], w=["Yo1"])
-        tt(ix(Y[:, 0:SP], T.SL[:]), T.CB[:], T.BB[:], Op.add, r=["SL", "CB", "BBa", "BBb"], w=Yn + ([] if last else ["Xd%d" % (r + 1)]))
-        if not last:
-            heads(r + 1)
-        else:
-            dma("s", "stx", T.yx[:], Y[:, 0:V], Yn, ["yx"], 6.0)
-
-    cnt, waited, toks = {e: 0 for e in sem}, {}, {}
-    for i in schedule(nodes):
+    cnt, waited, toks, mark = {e: 0 for e in sem}, {}, {}, {}
+    for i in PLAN[1]:
         x = nodes[i]
         e = x["e"]
         if e != "x":
-            need = {}
-            for d in x["dep"]:
+            need, wait = {}, set(x["wait"])
+            if x["key"] and x["key"][0] == "F":
+                wait |= set(mark.get(e, ()))
+                mark[e] = [i]
+            for d in wait:
                 name, val = toks[d]
                 if not (name == "p" and e == "p"):
                     need[name] = max(need.get(name, 0), val)
@@ -515,7 +655,7 @@ def rank_program(g, core, T, topo):
                 cnt[e] += 1
                 ins.then_inc(sem[e], 1)
         toks[i] = x["tok"] or (e, cnt[e])
-    g.sync.wait_ge(S.stx, 16)
-    g.sync.wait_ge(S.stn, 16)
+    for name, val in [("stx%d" % k, 16) for k in range(3)] + [("stn", 16)] + [("snt%d" % r, sent) for r in range(RO)]:
+        g.sync.wait_ge(S[name], val)
     for e in sem:
         g.sync.wait_ge(sem[e], cnt[e])

@@ -7,17 +7,24 @@ SHIFTS = (1, 2, 4)
 FC = 16
 FW = 8192 + W
 FSRC, FTHR = (-3, -1, 9), (0.03, 0.17, 0.65)
-FV = (0, 0, 0)
+NS_ = 3
+FLEX = (False, False, False)
 EVV = (3, 3, 3)
+EVD = (1, 1, 0)
+CUTS = (0, 16, 40, 68, 96)
+FLATE, FGATE = (3, 3, 0), 0
+EARLY = True
+KB, SPL = 3, 0
 L3V = False
 APART = (False, False, False)
 BE = (6, 7, 4)
 CY, GA, SC = np.array([0.83e-3, 1.15e-3, 1.1e-3, 1.0e-3]), np.array([1.56, 1.1, 1.9, 1.3]), np.array([3.8, 1.8, 3.0, 5.3])
 SLOW = (1.0, 1.3, 1.0, 1.2)
 PY, FIX, HOP = CY * np.array([0.55, 0.58, 0.5, 0.55]), dict(v=0.05, a=np.array([0.065, 0.1, 0.065, 0.1])), 0.07
-LAT = dict(h=1.5, n=1.8, x=4.0, acc=4.5, arr0=2.6, arr=2.8, row=1.8, cast=1.8, zero=4.5, stx=2.6, stn=2.2)
+LAT = dict(h=1.5, n=1.8, x=4.0, acc=4.5, arr0=2.6, arr=2.8, row=1.8, cast=1.8, ac3=2.6, zero=4.5, stx=1.7, stn=2.2)
 ON_VECTOR = ("G1e", "CO", "Lo", "Le", "Fo", "MM", "PP", "KH", "XD", "YE", "AS", "B")
-TRIES, SEED, SPAN, SHAKE, KEEP = 9000, 1, 5.0, (0.0, 0.5, 1.5, 3.0), 0.1
+TRIES, SEED, SPAN, SHAKE, KEEP = 6500, 1, 5.0, (0.0, 0.5, 1.5, 3.0), 0.1
+MOVES, COOL, SHARE = 80000, 0.02, (1.0, 1.6, 1.2, 0.7)
 PLAN = []
 bf, f32, i32, u16 = "bfloat16", "float32", "int32", "uint16"
 SCRATCH, INFO, PLACE = {}, {}, {}
@@ -64,12 +71,13 @@ _sb("SW", 256, f32)
 _sb("FL", 560, bf)
 _sb("R", 272, bf)
 _sb("BV", 112, bf)
+_sb("BLK", 224, bf)
 _sb("THR", 8, f32)
 _sb("BS U2 PP QQ BB CB SRC", 384, bf)
 for _k in range(8):
     SCRATCH["ps%d" % _k] = ("psum", [128, 512], f32)
     INFO["ps%d" % _k], PLACE["ps%d" % _k] = ("psum", 512, f32), ("ps%d" % _k, 0)
-SEMAPHORES = ["sv", "sa", "sp", "sg", "ldx", "ldn", "ldh", "stn", "zfa"] + [s + str(r) for s in ("stx", "arr", "snt", "acc", "okd", "nxd", "fcd") for r in range(RO)]
+SEMAPHORES = ["sv", "sa", "sp", "sg", "ldx", "ldn", "ldh", "stn", "zfa"] + ["stx%d" % k for k in range(6)] + [s + str(r) for s in ("arr", "snt", "acc", "ac0", "ac1", "ac2", "okd", "nxd", "fcd") for r in range(RO)]
 
 
 def engines_for(T, topo, q):
@@ -98,7 +106,7 @@ def plan(on_v, on_a):
             users[d].append(i)
     lat = [x["lat"] for x in on_v]
     cost = {e: [[float((x["dur"] + 0 * CY)[m]) for x in nodes] for m in range(len(CY))] for e, nodes in (("v", on_v), ("a", on_a))}
-    weight = [1.0 / sum(c) for c in cost["v"]]
+    weight = [k / sum(c) for c, k in zip(cost["v"], SHARE)]
     weight = [k / sum(weight) for k in weight]
     free = [i for i in range(n) if on_v[i]["key"]]
 
@@ -179,7 +187,62 @@ def plan(on_v, on_a):
             cur = new
         if new[0] < top[0]:
             top = new
-    return {on_v[i]["key"]: top[3][i] for i in free}, top[2], top[4]
+
+    order, eng = list(top[2]), list(top[3])
+    other = {"v": "a", "a": "v"}
+
+    def ends(order, eng, m, p, old):
+        end, at, lm, cv, ca = list(old), {}, lats[m], cost["v"][m], cost["a"][m]
+        for i in reversed(order[:p]):
+            if eng[i] not in at:
+                at[eng[i]] = end[i] - lm[i]
+                if len(at) == 6:
+                    break
+        for i in order[p:]:
+            e = eng[i]
+            t = at.get(e, 0.0)
+            for j in before[i]:
+                if end[j] > t:
+                    t = end[j]
+            t += ca[i] if e == "a" else cv[i]
+            at[e] = t
+            end[i] = t + lm[i]
+        return end
+
+    now = [ends(order, eng, m, 0, [0.0] * n) for m in range(len(CY))]
+    span = sum(max(x) * k for x, k in zip(now, weight))
+    top = (span, list(order), list(eng), [max(x) for x in now])
+    for it in range(MOVES):
+        p = int(n * draw())
+        i = order[p]
+        flip = on_v[i]["key"] and draw() < 0.3
+        new, first = order, p
+        if not flip or draw() < 0.5:
+            d, k, s, ties = (1 if draw() < 0.5 else -1), 1 + int(4 * draw() ** 2), p, set(before[i]) | set(users[i])
+            e = other[eng[i]] if flip else eng[i]
+            while k > 0 and 0 <= s + d < n and order[s + d] not in ties:
+                s += d
+                k -= eng[order[s]] == e
+            if k > 0 and not flip:
+                continue
+            new, first = order[:p] + order[p + 1:], min(p, s)
+            new.insert(s, i)
+        if flip:
+            eng[i] = other[eng[i]]
+        room, trial = COOL * (1 - it / MOVES) * draw(), []
+        for m in range(len(CY)):
+            trial.append(ends(new, eng, m, first, now[m]))
+            room -= (max(trial[m]) - max(now[m])) * weight[m]
+            if room < -0.3:
+                break
+        if room >= 0 and len(trial) == len(CY):
+            order, now = new, trial
+            span = sum(max(x) * k for x, k in zip(now, weight))
+            if span < top[0]:
+                top = (span, list(order), list(eng), [max(x) for x in now])
+        elif flip:
+            eng[i] = other[eng[i]]
+    return {on_v[i]["key"]: top[2][i] for i in free}, top[1], top[3]
 
 
 def v(name, a=0, b=None, s=1):
@@ -299,6 +362,10 @@ def steps(g, T, topo, rank, engine_of):
         op("p", [one(j, l, x) for j, (l, x) in enumerate(terms)],
            sum(PY * max(64, width(x)) * (1 if two(x) else 4) for l, x in terms), [y for t in terms for y in t], [out])
 
+    def mms(out, *parts):
+        for j, terms in enumerate(parts):
+            mm(out, terms, j == 0, j == len(parts) - 1)
+
     def conv(B, name, a, b):
         return [(v(B, 15 - k, 143 - k), v(name, a + k, b, 16)) for k in range(16)]
 
@@ -395,7 +462,7 @@ def steps(g, T, topo, rank, engine_of):
     IX = v("IDX", 0, 96)
     tt(IX, IX, v("QF"), Op.max)
     cp(v("LS0", 0, 96), IX)
-    for M, c in (("IDf", 1.0), ("IDn", -1.0), ("I8p", 8192.0), ("I8n", -8192.0), ("IHn", -0.5)):
+    for M, c in (("IDf", 1.0), ("IDn", -1.0), ("I8p", 8192.0), ("I8n", -8192.0)):
         lin(v(M), IDb, c, 0.0, E("I", M))
 
     def keep(out, in_, pat, how, base, cm):
@@ -413,8 +480,8 @@ def steps(g, T, topo, rank, engine_of):
         lin(v("A", 512 * j, 512 * j + wd), v("A", 0, wd), 1.0, v("CK", j, j + 1), E("AS", j))
     t5 = col(mk(13), 16.0, mk(5))
     wZ = col(mk(0), 12288.0, col(mk(2), -12288.0, col(t5, -1.0, col(mk(11), 16.0, mk(3)))))
-    if any(FV):
-        w01 = col(mk(0), 0.0625, 0.0)
+    if any(FLEX):
+        w01 = col(mk(0), 0.0625, mk(1))
         lin(v("B01"), v("BM"), w01, 0.0, E("B", "B01"))
     for k in K3:
         move(E("XE", k), third("XW0", 0, k), ix(v("XR"), v("LZ", 32 * k, 32 * k + 32)))
@@ -435,10 +502,11 @@ def steps(g, T, topo, rank, engine_of):
     tt(v("BK2", 0, 143), v("BKp", 0, 143), v("BKn", 1, 144), Op.add)
     move(E("SGf"), v("SGf"), v("SG"))
     lin(v("SEO"), v("SE2"), 1.0, float(HS - H), E("SEO"))
-    lin(v("SG5"), v("SG"), t5, 0.0, E("SG5"))
-    move(E("HA"), v("HA"), ix(v("A"), v("HU2")))
-    mm(ps(6, 128, 320), [(v("SG5"), v("HA"))])
-    move(E("HCOL"), v("HCOL"), ps(6, 128, 320))
+    if EARLY:
+        lin(v("SG5"), v("SG"), t5, 0.0, E("SG5"))
+        move(E("HA"), v("HA"), ix(v("A"), v("HU2")))
+        mm(ps(6, 128, 320), [(v("SG5"), v("HA"))])
+        move(E("HCOL"), v("HCOL"), ps(6, 128, 320))
     iota(v("BV"), [[1, 112]], 0)
     iota(v("N2"), [[2, 192]], 2)
     for out in (v("DX", H, HS), v("R"), v("ZR"), v("U", H, HS)):
@@ -448,9 +516,9 @@ def steps(g, T, topo, rank, engine_of):
         late(v("LB%d" % r, 0, 192), 0)
         late(v("XW%d" % (r + 1), H, HS), 0)
         late(v("SA", 16 * FC * r, 16 * FC * (r + 1)), FSRC[r])
-        if FV[r]:
+        if FLEX[r]:
             late(v("SV", 16 * FC * r, 16 * FC * (r + 1)), 4 ** r)
-    for k in K3 if any(FV) else ():
+    for k in K3 if any(FLEX) else ():
         late(third("FV", HS, k), 0)
     dma("g", "zfa", ap(v("FA", HS, GB), slice(0, 128, 16)), ap(v("ZR", 0, 96)), [v("ZR")], [v("FA", HS, GB)], "cast")
     for M, c in (("QE0", 0), ("QE1", -16), ("QO0", 1), ("QO1", -15)):
@@ -458,9 +526,14 @@ def steps(g, T, topo, rank, engine_of):
 
     def freed(r):
         Fa = v("FA", HS, GB)
-        Fb = v("XR", 0, H)
-        dma("g", "fcd%d" % r, ap(Fb, slice(0, 128, 16)), ap(Fa, slice(0, 128, 16)), [Fa], [Fb], "cast")
-        mm(ps(5, 192, 288), (conv("B01", "FV", HS, GB) if FV[r] else []) + [(I8n, Lo), (I8p, REM)] + conv("BP0", "XR", 0, H))
+        if FLEX[r]:
+            Fb = v("FV", HS, GB)
+            dma("g", "fcd%d" % r, ap(Fb, slice(1, 128, 16)), ap(Fa, slice(0, 128, 16)), [Fa], [Fb], "cast")
+            mm(ps(5, 192, 288), [(I8n, Lo), (I8p, REM)] + conv("B01", "FV", HS, GB))
+        else:
+            Fb = v("XR", 0, H)
+            dma("g", "fcd%d" % r, ap(Fb, slice(0, 128, 16)), ap(Fa, slice(0, 128, 16)), [Fa], [Fb], "cast")
+            mm(ps(5, 192, 288), [(I8n, Lo), (I8p, REM)] + conv("BP0", "XR", 0, H))
         flag(E("Fo", r), Fo, ps(5, 192, 288), FTHR[r], 16384.0)
 
     def level1(r, hs, k1, k2):
@@ -487,7 +560,7 @@ def steps(g, T, topo, rank, engine_of):
             tt(v("U2", 192 * h, 192 * h + 192), ix(v("SW", 128 * h, 128 * h + 112), v("BL", 12 * h, 12 * h + 12)), v("N2"), Op.subtract)
         flag(E("PP", r, hs), v("PP", a, b), v("U2", a, b), -1.5, -512.0)
         ts(v("QQ", a, b), v("U2", a, b), -1.0, None, Op.is_equal)
-        mm(ps(k, 64 + c, 64 + d), conv("BM", "PP", a, b) + [(IDb, v("BLb", c, d))] + conv("BHS", "QQ", a, b))
+        mms(ps(k, 64 + c, 64 + d), conv("BHS", "QQ", a, b) + [(IDb, v("BLb", c, d))], conv("BM", "PP", a, b))
         cp(v("SL", c, d), ps(k, 64 + c, 64 + d))
 
     for r in range(RO):
@@ -504,69 +577,92 @@ def steps(g, T, topo, rank, engine_of):
             level2(r, (1,), 5)
         for k in K3:
             move(E("G1o", r, k), third("DX", HS, k), ix(v(X), v(LS, 96 + 32 * k, 128 + 32 * k)))
-            mm(ps(k), [(IDb, third("DX", HS, k)), (IDn, third(X, HS, k))])
+            mm(ps(k), [(IDn, third(X, HS, k))], stop=False)
+            mm(ps(k), [(IDb, third("DX", HS, k))], start=False)
             ac(third("ABo", 0, k), ps(k), AF.Abs)
             step(E("CO", r, k), third(Xn, HS, k), ps(k))
-        kb = 3 if APART[r] else 5
-        mm(ps(kb, 384, 480), [(v("BM", 15 - k, 143 - k), v("ABo", 96 * k, 96 * (k + 1))) for k in range(16)])
+        kb = KB
+        rows = [(v("BM", 15 - k, 143 - k), v("ABo", 96 * k, 96 * (k + 1))) for k in range(16)]
+        mms(ps(kb, 384, 480), rows[:5], rows[5:10], rows[10:])
         flag(E("OK", r), v("OK"), ps(kb, 384, 480), 400.5, -512.0)
         dma("s", "okd%d" % r, ap(Ao, slice(0, 128, 16)), ap(v("OK")), [v("OK")], [Ak], "row")
         for k, b in zip(K3, BE):
             move(E("G1e", r, k), third("DX", 0, k), ix(v(X), v(LS, 32 * k, 32 * k + 32)))
-            mm(ps(b), [(IDb, third("DX", 0, k)), (IDn, third(X, 0, k))])
+            mm(ps(b), [(IDn, third(X, 0, k))], stop=False)
+            mm(ps(b), [(IDb, third("DX", 0, k))], start=False)
             ac(third("ABe", 0, k), ps(b), AF.Abs)
         dma("g", "acc%d" % r, ap(v(Xn, HS, GB)), ap(v(X, HS, GB)), [v(X, HS, GB), Ak], [v(Xn, HS, GB)], "acc", accum_op=Op.add, max_dma_last_dim=4096)
-        mm(ps(3, 0, 96), conv("BM", "ABo", 0, H) + [(I8n, Fo)])
-        mm(ps(4, 0, 96), conv("BM", "ABe", 0, H))
+        mm(ps(3, 0, 96), conv("BM", "ABo", 0, H), stop=False)
+        mm(ps(3, 0, 96), [(I8n, Fo)], start=False)
+        if SPL & 1:
+            mm(ps(4, 0, 64), conv("BM", "ABe", 0, 1024))
+            mm(ps(4, 64, 96), conv("BM", "ABe", 1024, H))
+        else:
+            mm(ps(4, 0, 96), conv("BM", "ABe", 0, H))
         for k in K3:
             move(E("G2", r, k), third("U", 0, k), ix(v("A"), v(LS, 32 * k, 32 * k + 32)))
         flag(E("Lo", r), Lo, ps(3, 0, 96), 400.5)
         flag(E("Le", r), Le, ps(4, 0, 96), 400.5)
         flag(E("NS", r), v("NS"), ps(4, 0, 96), 159.5)
         scan(v("R", 1, 113), v("FL", 0, 112), v("FL", 336, 448), Op.add)
-        mm(ps(4, 96, 192), [(IDf, IX), (I8p, v("NS"))])
+        mms(ps(4, 96, 192), [(IDf, IX)], [(I8p, v("NS"))])
         cp(v("LF"), ps(4, 96, 192))
-        for j in range(96 // FC):
+        def marks_(j):
             lst, sv, sa = v("LF", FC * j, FC * (j + 1)), v("SV", 16 * FC * r, 16 * FC * (r + 1)), v("SA", 16 * FC * r, 16 * FC * (r + 1))
-            if j < FV[r]:
-                cp(ix(v("FV"), lst), sv)
-            else:
+            marks = dict(r=[lst, sv, sa], w=[v("FV", HS + j, GB, 96 // FC), v("FA", HS + j, GB, 96 // FC)])
+            if not FLEX[r]:
                 ac(ix(v("FA"), lst), sa, AF.Sigmoid)
+            elif E("F", r, j) == "v":
+                el("v", vec.tensor_copy, ix(v("FV"), lst), [sv], **marks)
+            else:
+                el("a", lambda o, i: act.activation(o, i, AF.Sigmoid), ix(v("FA"), lst), [sa], **marks)
+
+        for j in range(96 // FC - FLATE[r]):
+            marks_(j)
         level1(r, (0,) if APART[r] else (0, 1), 6, 7)
         mm(ps(7, 496, 497), [(v("SG"), v("R", 96, 97))])
         ts(v("THR", 0, 1), ps(7, 496, 497), 192.0, 8192.0, Op.min, Op.add)
-        if not last:
+        if not last and EARLY:
             mm(ps(5, 0, 96), [(v("TST"), v("R", 1, 97)), (v("TGE"), v("R", 0, 96))])
             ac(v("RK"), ps(5, 0, 96), AF.Sigmoid, scale=-512.0, bias=512.0 * 191.5, accum_out=v("THR", 1, 2))
             mm(ps(3, 96, 97), [(v("SGf"), v("THR", 1, 2))])
             ts(v("HA"), v("HCOL"), ps(3, 96, 97), None, Op.is_ge)
             move(E("ABh", r), v("ABh"), ix(v("ABe"), v("HU2")))
             mm(ps(3, 288, 480), [(v("SG"), v("ABh")), (I8n, v("HA"))])
-            flag(E("KH", r), v("KH"), ps(3, 288, 480), 400.5)
+            ts(v("KH"), ps(3, 288, 480), 400.5, 0.5, Op.is_gt, Op.mult)
         level2(r, (0,) if APART[r] else (0, 1), 6)
         SI, SF = v("SL", 0, 12), v("SL", 12, 24)
         mm(ps(7, 240, 352), [(v("TST"), v("R", 129, 241)), (v("TGE"), v("R", 128, 240)), (I8p, v("FL", 128, 240))])
         mm(ps(7, 352, 448), [(v("TST"), v("R", 129, 225)), (v("TGE"), v("R", 128, 224)), (IDb, Fe), (I8p, Fo)])
         ts(v("FL", 128, 336), ps(7, 240, 448), v("THR", 0, 1), None, Op.is_ge)
-        mm(ps(5, 96, 192), conv("BZ", "U", 0, H) + [(I8n, v("NS"))])
+        if SPL & 2:
+            mm(ps(5, 96, 160), conv("BZ", "U", 0, 1024) + [(I8n, v("NS", 0, 64))])
+            mm(ps(5, 160, 192), conv("BZ", "U", 1024, H) + [(I8n, v("NS", 64, 96))])
+        else:
+            mm(ps(5, 96, 192), conv("BZ", "U", 0, H) + [(I8n, v("NS"))])
         flag(E("MM", r), v("MM"), ps(5, 96, 192), -4096.5)
         tt(v("MD"), ps(5, 96, 192), v("MM"), Op.mult)
         if L3V:
             tt(v("TT"), IX, v("MD"), Op.add)
             cp(v("L3"), v("TT"))
         else:
-            mm(ps(5, 384, 480), [(IDf, IX), (IDf, v("MD"))])
-            cp(v("L3"), ps(5, 384, 480))
+            mms(ps(4, 384, 480), [(IDf, IX)], [(IDf, v("MD"))])
+            cp(v("L3"), ps(4, 384, 480))
         for k in K3:
             move(E("G3", r, k), third("D3", 0, k), ix(v(X), v("L3", 32 * k, 32 * k + 32)))
-        if not last:
+        if not last and EARLY:
             move(E("DH", r), v("DH"), ix(v("D3"), v("HU2")))
-            mm(ps(3, 288, 480), [(v("IHn"), v("KH")), (IDn, v("HG%d" % r)), (IDb, v("DH"))])
+            mms(ps(3, 288, 480), [(IDn, v("KH")), (IDn, v("HG%d" % r))], [(IDb, v("DH"))])
             ts(v("HC"), ps(3, 288, 480), 1.0, -1.0, Op.min, Op.max)
             tt(v("HG%d" % (r + 1)), v("HC"), v("HG%d" % r), Op.add)
             send(r + 1)
         for k in K3:
-            mm(ps(k), [(IDb, third("D3", 0, k)), (IDn, third(X, 0, k))])
+            mm(ps(k), [(IDn, third(X, 0, k))], stop=False)
+            mm(ps(k), [(IDb, third("D3", 0, k))], start=False)
+            if k < EVD[r]:
+                step(E("CE", r, k), third(Xn, 0, k), ps(k))
+                dma("g", "ac%d%d" % (k, r), ap(third(Xn, 0, k)), ap(third(X, 0, k)), [third(X, 0, k)], [third(Xn, 0, k)], "ac3", accum_op=Op.add)
+                continue
             if k < EVV[r]:
                 step(E("CE", r, k), ps(k), ps(k))
                 tt(third(Xn, 0, k), ps(k), third(X, 0, k), Op.add)
@@ -581,7 +677,7 @@ def steps(g, T, topo, rank, engine_of):
         odds = conv("BU", "U", HS, GB)
         if not last:
             mm(ps(3, 192, 288), odds)
-            mm(ps(4, 192, 288), evens)
+            mms(ps(4, 192, 288), evens[16:], evens[:16])
             cp(v("LS%d" % (r + 1), 96), ps(3, 192, 288))
             tt(v("QF"), v("SE2"), Fe, Op.mult)
             tt(IX, ps(4, 192, 288), v("QF"), Op.max)
@@ -595,16 +691,24 @@ def steps(g, T, topo, rank, engine_of):
         mm(ps(6, 128, 320), [(IDb, B2), (IDn, B1)])
         mm(ps(6, 320, 512), [(IDb, v("DD")), (IDn, B2)])
         step(E("CB", r), v("CB"), ps(6, 128, 512))
+        gate = len(nodes) - 1 - FGATE
+        for j in range(96 // FC - FLATE[r], 96 // FC):
+            marks_(j)
+            nodes[-1]["dep"] = nodes[-1]["dep"] | {gate}
         tt(ix(v(Xn, 0, GB), v("SL")), v("CB"), v("BB"), Op.add)
+        if not last and not EARLY:
+            move(E("HG", r), v("HG%d" % (r + 1)), ix(v(Xn, 0, H), v("HU2")))
+            send(r + 1)
 
     freed(RO - 1)
     mm(ps(3, 0, 96), [(IDf, v("SEO")), (I8n, Fo)])
     cp(v("LZ"), ps(3, 0, 96))
-    for k in K3:
-        move(E("Y", k), v("XO", 1024 * k + 1, 1024 * (k + 1), 2), ix(v(Xn, H, GB), v("LZ", 32 * k, 32 * k + 32)))
-        move(E("YE", k), v("XO", 1024 * k, 1024 * (k + 1), 2), third(Xn, 0, k))
-        out = v("XO", 1024 * k, 1024 * (k + 1))
-        dma("s", "stx%d" % k, T.yx[:, 1024 * k:1024 * (k + 1)], ap(out), [out], (), "stx")
+    for k, (a, b) in enumerate(zip(CUTS, CUTS[1:])):
+        move(E("Y", k), v("XO", 32 * a + 1, 32 * b, 2), ix(v(Xn, H, GB), v("LZ", a, b)))
+        move(E("YE", k), v("XO", 32 * a, 32 * b, 2), v(Xn, 16 * a, 16 * b))
+        out = v("XO", 32 * a, 32 * b)
+        dma("s", "stx%d" % k, T.yx[:, 32 * a:32 * b], ap(out), [out], (), "stx")
+        nodes[-1]["dur"] = 0.03 * (b - a)
     mm(ps(5, 0, 96), [(IDf, v("MD")), (I8n, Fe)])
     mm(ps(5, 96, 192), [(I8n, Fo)])
     move(E("T4"), v("T4"), ps(5, 0, 192))
@@ -632,7 +736,7 @@ def rank_program(g, core, T, topo):
     S = T.sem
     q = {"v": g.vector, "a": g.scalar, "p": g.tensor, "g": g, "s": g.sync}
     sem = {"v": S.sv, "a": S.sa, "p": S.sp, "g": S.sg}
-    cnt, waited, toks, mark = {e: 0 for e in sem}, {}, {}, {}
+    cnt, waited, toks, mark, past = {e: 0 for e in sem}, {}, {}, {}, {}
     for i in PLAN[1]:
         x = nodes[i]
         e = x["e"]
@@ -645,17 +749,22 @@ def rank_program(g, core, T, topo):
                 name, val = toks[d]
                 if not (name == "p" and e == "p"):
                     need[name] = max(need.get(name, 0), val)
+            seen = waited.setdefault(e, {})
+            need = {k: val for k, val in need.items() if seen.get(k, 0) < val}
             for name in sorted(need):
-                if waited.get((e, name), 0) < need[name]:
+                if not any(past[k, val].get(name, 0) >= need[name] for k, val in need.items() if k != name):
                     q[e].wait_ge(sem[name] if name in sem else S[name], need[name])
-                    waited[(e, name)] = need[name]
+            for name in need:
+                for k, val in list(past[name, need[name]].items()) + [(name, need[name])]:
+                    seen[k] = max(seen.get(k, 0), val)
         for fn in x["fns"]:
             ins = fn()
             if x["tok"] is None:
                 cnt[e] += 1
                 ins.then_inc(sem[e], 1)
         toks[i] = x["tok"] or (e, cnt[e])
-    for name, val in [("stx%d" % k, 16) for k in range(3)] + [("stn", 16)] + [("snt%d" % r, sent) for r in range(RO)]:
+        past[toks[i]] = dict(waited.get(e, {}))
+    for name, val in [("stx%d" % k, 16) for k in range(len(CUTS) - 1)] + [("stn", 16)] + [("snt%d" % r, sent) for r in range(RO)]:
         g.sync.wait_ge(S[name], val)
     for e in sem:
         g.sync.wait_ge(sem[e], cnt[e])

import numpy as np
from concourse.bass import DstId, RemoteDMATransfer
from concourse.mybir import AluOpType as Op, ActivationFunctionType as AF

V, H, HS, GB, W, RO = 3072, 1536, 1728, 3264, 3456, 3
SHIFTS = (1, 2, 4)
FC = 16
FW = 8192 + W
FSRC, FTHR = (-3, -1, 9), (0.03, 0.17, 0.65)
NS_ = 3
FLEX = (False, False, False)
EVV = (3, 3, 3)
EVD = (1, 1, 0)
CUTS = (0, 16, 40, 68, 96)
FLATE, FGATE = (3, 3, 0), 0
EARLY = True
KB, SPL = 3, 0
L3V = False
APART = (False, False, False)
BE = (6, 7, 4)
CY, GA, SC = np.array([0.83e-3, 1.15e-3, 1.1e-3, 1.0e-3]), np.array([1.56, 1.1, 1.9, 1.3]), np.array([3.8, 1.8, 3.0, 5.3])
SLOW = (1.0, 1.3, 1.0, 1.2)
PY, FIX, HOP = CY * np.array([0.55, 0.58, 0.5, 0.55]), dict(v=0.05, a=np.array([0.065, 0.1, 0.065, 0.1])), 0.07
LAT = dict(h=1.5, n=1.8, x=4.0, acc=4.5, arr0=2.6, arr=2.8, row=1.8, cast=1.8, ac3=2.6, zero=4.5, stx=1.7, stn=2.2)
ON_VECTOR = ("G1e", "CO", "Lo", "Le", "Fo", "MM", "PP", "KH", "XD", "YE", "AS", "B")
TRIES, SEED, SPAN, SHAKE, KEEP = 6500, 1, 5.0, (0.0, 0.5, 1.5, 3.0), 0.1
MOVES, COOL, SHARE = 80000, 0.02, (1.0, 1.6, 1.2, 0.7)
PLAN = []
bf, f32, i32, u16 = "bfloat16", "float32", "int32", "uint16"
SCRATCH, INFO, PLACE = {}, {}, {}


def _sb(names, cols, dt):
    for n in names.split():
        pool = n if cols > 600 else "pool_" + dt
        at = SCRATCH[pool][1][1] if pool in SCRATCH else 0
        SCRATCH[pool] = ("sbuf", [128, at + (cols + 15) // 16 * 16], dt)
        INFO[n], PLACE[n] = ("sbuf", cols, dt), (pool, at)


_sb("XW0 XW1 XW2 XW3 A LA0 LA1 LA2 LB0 LB1 LB2", W, bf)
_sb("XR", V + 16, bf)
_sb("XO", V, bf)
_sb("U DX", GB, bf)
_sb("FV", FW, bf)
_sb("FA", FW, f32)
_sb("SV", RO * 16 * FC, bf)
_sb("SA", RO * 16 * FC, f32)
_sb("ABe ABo CE D3", H, bf)
_sb("LO HI", 512, bf)
_sb("HG0 HG1 HG2 ZR DD ABh HA KH DH", 192, bf)
_sb("BM BP0 B01 BZ BU BKn BKp BK2 BHS", 144, bf)
_sb("JJ", 144, f32)
_sb("IDb I8p I8n IDn IHn M1 M2 TST TGE SG SG5", 128, bf)
_sb("IDf SGf AQ GQ AQm PE0 PE1 PO0 PO1 QE0 QE1 QO0 QO1", 128, f32)
_sb("COL", 32, f32)
_sb("MK CD CK CE16 OF16 I16", 16, f32)
_sb("PI", 8, i32)
_sb("NX TI HH HC", 192, i32)
_sb("HD", 12, i32)
_sb("HU HU2", 12, u16)
_sb("OU", 16, u16)
_sb("BL SL", 24, u16)
_sb("BLb", 24, bf)
_sb("LS0 LS1 LS2", 192, u16)
_sb("L3 LZ LF", 96, u16)
_sb("NXF N2 IDX T1 T2 T3 T4 YN HCOL", 192, f32)
_sb("MD TT QF SE2 SEN SEO", 96, f32)
_sb("MM NS OK RK", 96, bf)
_sb("SW", 256, f32)
_sb("FL", 560, bf)
_sb("R", 272, bf)
_sb("BV", 112, bf)
_sb("BLK", 224, bf)
_sb("THR", 8, f32)
_sb("BS U2 PP QQ BB CB SRC", 384, bf)
for _k in range(8):
    SCRATCH["ps%d" % _k] = ("psum", [128, 512], f32)
    INFO["ps%d" % _k], PLACE["ps%d" % _k] = ("psum", 512, f32), ("ps%d" % _k, 0)
SEMAPHORES = ["sv", "sa", "sp", "sg", "ldx", "ldn", "ldh", "stn", "zfa"] + ["stx%d" % k for k in range(6)] + [s + str(r) for s in ("arr", "snt", "acc", "ac0", "ac1", "ac2", "okd", "nxd", "fcd") for r in range(RO)]


def engines_for(T, topo, q):
    n = len(T.cores)
    allowed = [topo.engines(T.cores[q], T.cores[(q - s) % n]) for s in SHIFTS]
    narrow = min(len(a) for a in allowed)
    tight = [b for b in range(3) if len(allowed[b]) == narrow]
    share = {1: [4], 2: [4, 4], 3: [4, 2, 2]}[len(tight)] if narrow < 12 else [4, 4, 4]
    out, used = {}, set()
    for b, k in zip(reversed(tight), share):
        out[b] = [e for e in allowed[b] if e not in used][:k]
        used |= set(out[b])
    for b in range(3):
        if b not in out:
            out[b] = [e for e in reversed(allowed[b]) if e not in used][:4]
            used |= set(out[b])
    return [out[b] for b in range(3)]


def plan(on_v, on_a):
    n = len(on_v)
    before = [sorted(x["dep"]) for x in on_v]
    users = [[] for _ in on_v]
    for i in range(n):
        for d in before[i]:
            users[d].append(i)
    lat = [x["lat"] for x in on_v]
    cost = {e: [[float((x["dur"] + 0 * CY)[m]) for x in nodes] for m in range(len(CY))] for e, nodes in (("v", on_v), ("a", on_a))}
    weight = [k / sum(c) for c, k in zip(cost["v"], SHARE)]
    weight = [k / sum(weight) for k in weight]
    free = [i for i in range(n) if on_v[i]["key"]]

    def place(rank, pred, succ, back, eng, dur):
        left, start, est = [len(p) for p in pred], [0.0] * n, [lat[i] if back else 0.0 for i in range(n)]
        busy = {e: [] for e in "vapgsx"}
        ready = [(rank[i], i) for i in range(n) if left[i] == 0]
        while ready:
            m = min(ready)
            ready.remove(m)
            i = m[1]
            t, d, row = est[i], dur[i], busy[eng[i]]
            k = len(row)
            while k > 0 and row[k - 1][1] > t:
                k -= 1
            while k < len(row) and row[k][0] < t + d - 1e-9:
                t = row[k][1]
                k += 1
            row.insert(k, (t, t + d))
            start[i] = t
            for u in succ[i]:
                e = t + d + (lat[u] if back else lat[i])
                if e > est[u]:
                    est[u] = e
                left[u] -= 1
                if left[u] == 0:
                    ready.append((rank[u], u))
        return start

    lats = [[x * k for x in lat] for k in SLOW]
    lat = [x * sum(SLOW) / len(SLOW) for x in lat]

    def replay(order, eng, d, lat):
        end, at = [0.0] * n, {e: 0.0 for e in "vapgsx"}
        for i in order:
            t = at[eng[i]]
            for j in before[i]:
                if end[j] > t:
                    t = end[j]
            at[eng[i]] = t + d[i]
            end[i] = t + d[i] + lat[i]
        return max(end)

    def solve(eng, rank, passes):
        cases = [[cost["a" if eng[i] == "a" else "v"][m][i] for i in range(n)] for m in range(len(CY))]
        dur = [sum(c[i] * k for c, k in zip(cases, weight)) for i in range(n)]
        best = None
        for it in range(passes):
            start = place(rank, before, users, False, eng, dur)
            if passes > 2 or it == 1:
                order = sorted(range(n), key=lambda i: (start[i], i))
                spans = [replay(order, eng, c, x) for c, x in zip(cases, lats)]
                span = sum(s * k for s, k in zip(spans, weight))
                if best is None or span < best[0]:
                    best = (span, start, order, eng, spans)
            if it + 1 < passes:
                back = place([-(start[i] + dur[i]) for i in range(n)], users, before, True, eng, dur)
                rank = [-(back[i] + dur[i]) for i in range(n)]
        return best

    seed = [SEED]

    def draw():
        seed[0] = (seed[0] * 1103515245 + 12345) % 2147483648
        return seed[0] / 2147483648

    eng = [("v" if x["key"][0] in ON_VECTOR else "a") if x["key"] else x["e"] for x in on_v]
    cur = top = solve(eng, list(range(n)), 12)
    for it in range(TRIES):
        eng, mid = list(cur[3]), cur[0] * draw()
        near = [i for i in free if abs(cur[1][i] - mid) < SPAN]
        for _ in range((0, 1, 1, 2, 2, 3)[int(6 * draw())] if near else 0):
            i = near[int(len(near) * draw())]
            eng[i] = "a" if eng[i] == "v" else "v"
        amp = SHAKE[int(len(SHAKE) * draw())]
        new = solve(eng, [s + amp * (draw() - 0.5) if abs(s - mid) < SPAN else s for s in cur[1]], 2)
        if new[0] <= cur[0] + KEEP * (1 - it / TRIES):
            cur = new
        if new[0] < top[0]:
            top = new

    order, eng = list(top[2]), list(top[3])
    other = {"v": "a", "a": "v"}

    def ends(order, eng, m, p, old):
        end, at, lm, cv, ca = list(old), {}, lats[m], cost["v"][m], cost["a"][m]
        for i in reversed(order[:p]):
            if eng[i] not in at:
                at[eng[i]] = end[i] - lm[i]
                if len(at) == 6:
                    break
        for i in order[p:]:
            e = eng[i]
            t = at.get(e, 0.0)
            for j in before[i]:
                if end[j] > t:
                    t = end[j]
            t += ca[i] if e == "a" else cv[i]
            at[e] = t
            end[i] = t + lm[i]
        return end

    now = [ends(order, eng, m, 0, [0.0] * n) for m in range(len(CY))]
    span = sum(max(x) * k for x, k in zip(now, weight))
    top = (span, list(order), list(eng), [max(x) for x in now])
    for it in range(MOVES):
        p = int(n * draw())
        i = order[p]
        flip = on_v[i]["key"] and draw() < 0.3
        new, first = order, p
        if not flip or draw() < 0.5:
            d, k, s, ties = (1 if draw() < 0.5 else -1), 1 + int(4 * draw() ** 2), p, set(before[i]) | set(users[i])
            e = other[eng[i]] if flip else eng[i]
            while k > 0 and 0 <= s + d < n and order[s + d] not in ties:
                s += d
                k -= eng[order[s]] == e
            if k > 0 and not flip:
                continue
            new, first = order[:p] + order[p + 1:], min(p, s)
            new.insert(s, i)
        if flip:
            eng[i] = other[eng[i]]
        room, trial = COOL * (1 - it / MOVES) * draw(), []
        for m in range(len(CY)):
            trial.append(ends(new, eng, m, first, now[m]))
            room -= (max(trial[m]) - max(now[m])) * weight[m]
            if room < -0.3:
                break
        if room >= 0 and len(trial) == len(CY):
            order, now = new, trial
            span = sum(max(x) * k for x, k in zip(now, weight))
            if span < top[0]:
                top = (span, list(order), list(eng), [max(x) for x in now])
        elif flip:
            eng[i] = other[eng[i]]
    return {on_v[i]["key"]: top[2][i] for i in free}, top[1], top[3]


def v(name, a=0, b=None, s=1):
    return (name, a, INFO[name][1] if b is None else b, s)


def ix(win, off):
    return ("ix", win, off)


def width(x):
    return 16 * width(x[2]) if x[0] == "ix" else len(range(x[1], x[2], x[3]))


def meet(x, y):
    return x[1] < y[2] and y[1] < x[2] and not (x[3] == y[3] and x[3] > 1 and (x[1] - y[1]) % x[3])


def steps(g, T, topo, rank, engine_of):
    n = len(T.cores)
    S = T.sem
    q = {"a": g.scalar, "g": g, "s": g.sync, "x": g.sync}
    nodes, seen, bank, pending = [], {}, {}, [None]

    def E(*key):
        pending[0] = key
        return engine_of(key)

    def ap(x, p=slice(0, 128)):
        if not isinstance(x, tuple):
            return x
        if x[0] == "ix":
            return ap(x[1]).indirect(ap(x[2]))
        pool, at = PLACE[x[0]]
        return T[pool][p, at + x[1]:at + x[2]:x[3]]

    def op(e, fns, dur, r=(), w=(), tok=None, lat=HOP, after=()):
        i, dep, key = len(nodes), set(), pending[0]
        pending[0] = None
        acc = []
        for x, wr in [(x, False) for x in r] + [(x, True) for x in w]:
            if isinstance(x, tuple):
                acc += [(x[1], wr), (x[2], False)] if x[0] == "ix" else [(x, wr)]
        for k in {x[0] for x, wr in acc if INFO[x[0]][0] == "psum"}:
            cur, prev = bank.get(k, ([], []))
            same = e != "p" and cur and nodes[cur[0]]["e"] == e and not key and not nodes[cur[0]]["key"]
            dep |= set(prev if same else cur)
            bank[k] = (cur + [i], prev) if same else ([i], cur)
        acc = [(x, wr) for x, wr in acc if INFO[x[0]][0] != "psum"]
        for x, wr in acc:
            dep |= {j for y, yw, j in seen.get(x[0], []) if (wr or yw) and meet(x, y)}
        for x, wr in acc:
            old = seen.get(x[0], [])
            if wr and x[3] == 1:
                old = [t for t in old if not (x[1] <= t[0][1] and t[0][2] <= x[2])]
            seen[x[0]] = old + [(x, wr, i)]
        nodes.append(dict(e=e, fns=fns, dur=dur, lat=lat, dep=dep | set(after), wait=dep, tok=tok, key=key, w=w))
        return i

    vec, act, pe = g.vector, g.scalar, g.tensor

    def two(x):
        return INFO[(x[1] if x[0] == "ix" else x)[0]][2] in (bf, u16)

    def el(e, call, out, ins, cols=(), k=1.0, also=(), r=None, w=None):
        if out[0] == "ix":
            c = SC * width(out)
        elif ins and ins[0][0] == "ix":
            c = GA * width(out)
        else:
            c = width(out) * k * (0.5 if e == "v" and all(two(x) for x in [out] + ins) else 1.0)
        return op(e, [lambda: call(*[ap(x) for x in [out] + ins])], FIX[e] + CY * np.maximum(64, c), r or ins + list(cols), w or [out] + list(also))

    def ts(out, in0, s1, s2, o0, o1=None):
        el("v", lambda o, i: vec.tensor_scalar(o, i, ap(s1), None, o0) if o1 is None else vec.tensor_scalar(o, i, ap(s1), ap(s2), o0, o1), out, [in0], [s1, s2])

    def tt(out, in0, in1, o):
        psum = any(x[0].startswith("ps") for x in (in0, in1))
        el("v", lambda x, y, z: vec.tensor_tensor(x, y, z, o), out, [in0, in1], (), 1.0 if psum else 2.0)

    def cp(out, in_):
        return el("v", vec.tensor_copy, out, [in_])

    def ms(out, c):
        el("v", lambda o: vec.memset(o, c), out, [])

    def scan(out, a, b, o):
        el("v", lambda x, y, z: vec.tensor_tensor_scan(x, y, z, 0.0, o, Op.add), out, [a, b])

    def ac(out, in_, func=AF.Copy, **kw):
        el("a", lambda o, i: act.activation(o, i, func, **{k: ap(x) for k, x in kw.items()}), out, [in_], kw.values(), also=[kw.get("accum_out")])

    def lin(out, in_, sc, bi, e="a"):
        if e == "a":
            ac(out, in_, AF.Identity, scale=sc, bias=bi)
        else:
            ts(out, in_, sc, bi, Op.mult, Op.add)

    def move(e, out, in_):
        (cp if e == "v" else ac)(out, in_)

    def flag(e, out, in_, thr, sc=512.0):
        if e == "v":
            ts(out, in_, thr, None, Op.is_gt if sc > 0 else Op.is_lt)
        else:
            ac(out, in_, AF.Sigmoid, scale=sc, bias=-sc * thr)

    def step(e, out, in_):
        if e == "v":
            ts(out, in_, 1.0, -1.0, Op.min, Op.max)
        else:
            ac(out, in_, AF.Sign)

    def mm(out, terms, start=True, stop=True):
        def one(j, l, x):
            return lambda: pe.matmul(ap(out), ap(l), ap(x), start and j == 0, stop and j == len(terms) - 1)
        op("p", [one(j, l, x) for j, (l, x) in enumerate(terms)],
           sum(PY * max(64, width(x)) * (1 if two(x) else 4) for l, x in terms), [y for t in terms for y in t], [out])

    def mms(out, *parts):
        for j, terms in enumerate(parts):
            mm(out, terms, j == 0, j == len(parts) - 1)

    def conv(B, name, a, b):
        return [(v(B, 15 - k, 143 - k), v(name, a + k, b, 16)) for k in range(16)]

    def iota(out, pat, base, after=()):
        op("g", [lambda: g.iota(ap(out), pat, base, 0, allow_small_or_imprecise_dtypes=True)], 0.13 + 2 * CY * width(out), (), [out], after=after)

    def dma(e, name, out, in_, r, w, lat, **kw):
        op(e, [lambda: q[e].dma_start(out, in_, **kw).then_inc(S[name], 16)], {"g": 1.0, "x": 0.0}.get(e, 0.1), r, w, tok=(name, 16), lat=LAT[lat])

    def ps(k, a=0, b=512, s=1):
        return v("ps%d" % k, a, b, s)

    def mk(a):
        return v("MK", a, a + 1)

    def third(name, base, k):
        return v(name, base + 512 * k, base + 512 * (k + 1))

    K3 = range(3)
    Le, Fe, REM, Lo, Fo = (v("FL", a, a + 96) for a in (0, 128, 240, 336, 448))
    IDb, IDn, IDf, I8p, I8n = (v(s) for s in ("IDb", "IDn", "IDf", "I8p", "I8n"))

    for name, out, in_, lat in (("ldh", v("HD"), T.head[:], "h"), ("ldn", v("NX"), T.nxt[:], "n"), ("ldx", v("XR", 0, V), T.x[:], "x")):
        dma("x", name, ap(out), in_, (), [out], lat)
    mine = engines_for(T, topo, rank)
    sent = sum(len(m) for m in mine)
    inc = sum(len(engines_for(T, topo, (rank + s) % n)[b]) for b, s in enumerate(SHIFTS))

    def send(r):
        trs = []
        for b, s in enumerate(SHIFTS):
            rid, pid, _se = topo.addr(T.cores[(rank - s) % n])
            trs.append(RemoteDMATransfer(dst_ids=[DstId(rid=rid, pnc=pid)], dma_engine_mask=sum(1 << e for e in mine[b]), remote_sem=S["arr%d" % r],
                                         src=ap(v("HG%d" % r, 64 * b, 64 * b + 64)), dst=ap(v("XW%d" % r, GB + 64 * b, GB + 64 * b + 64))))
        i = op("g", [lambda: g.remote_dma_fused(trs, local_sem=S["snt%d" % r])], 1.0 if r else 3.0, [v("HG%d" % r)], (), tok=("snt%d" % r, sent), lat=0.0)
        op("x", [], 0.0, (), [v("XW%d" % r, GB, W)], tok=("arr%d" % r, inc), lat=LAT["arr" if r else "arr0"], after=[i])
        return i

    op("g", [lambda: g.iota(ap(v("PI", 0, 1)), [[0, 1]], 0, 1)], 0.13, (), [v("PI", 0, 1)])
    iota(v("I16"), [[1, 16]], 0)
    iota(v("GQ"), [[1, 8], [0, 16]], 0)
    iota(v("AQ"), [[0, 8], [1, 16]], 0)
    iota(v("JJ"), [[1, 144]], 0)
    iota(v("SE2"), [[16, 96]], 0)
    iota(v("LO"), [[0, 32], [1, 16]], 0)
    iota(v("HI"), [[1, 32], [0, 16]], 0)
    iota(v("CD"), [[0, 2], [16, 8]], W - 128)
    ts(v("PI", 1, 2), v("PI", 0, 1), 15, None, Op.bitwise_and)
    ts(v("PI", 2, 3), v("PI", 0, 1), 4, None, Op.arith_shift_right)
    cp(v("COL", 0, 3), v("PI", 0, 3))
    pa, pg = v("COL", 1, 2), v("COL", 2, 3)
    ms(v("FL"), 0.0)
    ms(v("FL", 96, 108), 1.0)
    ms(v("XR", V), 0.0)
    used = [3]

    def col(src, m, a):
        used[0] += 1
        c = v("COL", used[0] - 1, used[0])
        lin(c, src, m, a, E("col", used[0]))
        return c

    ts(v("MK"), v("I16"), pa, None, Op.is_equal)
    cg = col(pg, 16.0, 15.0)
    ts(v("AQm"), v("GQ"), pg, 1000.0, Op.not_equal, Op.mult)
    ts(v("BM"), v("JJ"), cg, None, Op.is_equal)
    tt(v("AQm"), v("AQm"), v("AQ"), Op.add)
    cp(v("HU"), v("HD"))
    cp(v("NXF"), v("NX"))
    lin(v("GQ"), v("AQm"), 2.0, 0.0, E("GQ"))
    for M, c in (("PE0", 0.0), ("PE1", -16.0), ("PO0", 1.0), ("PO1", -15.0)):
        ts(v(M), v("GQ"), c, pa, Op.add, Op.is_equal)
    ts(IDb, v("AQm"), pa, None, Op.is_equal)
    move(E("HG"), v("HG0"), ix(v("XR", 0, V), v("HU")))
    first = [send(0)]

    def late(out, c):
        iota(out, [[0, width(out)]], c, first)

    ac(v("T4"), v("NXF"), AF.Relu, bias=1.0 - V)
    mm(ps(7, 0, 96), [(v(M), v(N, h, 192, 2)) for N in ("NXF", "T4") for h, M in enumerate(("PE0", "PE1"))])
    mm(ps(7, 96, 192), [(v(M), v(N, h, 192, 2)) for N in ("NXF", "T4") for h, M in enumerate(("PO0", "PO1"))])
    nx = ps(7, 0, 192)
    lin(v("SE2"), v("SE2"), 1.0, pa, E("SE2"))
    ts(v("TI"), nx, 0.5, -0.25, Op.mult, Op.add)
    ts(Fe, ps(7, 0, 96), 0.0, None, Op.is_lt)
    flag("a", Fo, ps(7, 96, 192), -0.5, -512.0)
    nodes[-1]["dur"] = nodes[-1]["dur"] + 1.3
    lin(v("T1"), nx, float(HS), 0.0, E("T1"))
    ts(v("T2"), v("TI"), 0.0, 1.0 - 2 * HS, Op.max, Op.mult)
    tt(v("QF"), v("SE2"), Fe, Op.mult)
    tt(v("IDX"), v("T1"), v("T2"), Op.add)
    cp(v("LS0", 96), v("IDX", 96))
    IX = v("IDX", 0, 96)
    tt(IX, IX, v("QF"), Op.max)
    cp(v("LS0", 0, 96), IX)
    for M, c in (("IDf", 1.0), ("IDn", -1.0), ("I8p", 8192.0), ("I8n", -8192.0)):
        lin(v(M), IDb, c, 0.0, E("I", M))

    def keep(out, in_, pat, how, base, cm):
        op("g", [lambda: g.affine_select(ap(out), ap(in_), pat, how, 0.0, base, cm)], 0.17 + 2 * CY * width(out), [in_], [out], after=first)

    lin(v("SEN"), v("SE2"), 2.0, 0.0, E("SEN"))
    mm(ps(5, 0, 96), [(IDf, v("SEN")), (I8p, Fe)])
    ts(v("LZ"), ps(5, 0, 96), float(V), None, Op.min)
    lin(v("LO"), v("LO"), mk(5), mk(2), E("AS", -1))
    lin(v("HI"), v("HI"), mk(13), 0.0, E("AS", 0))
    ts(v("CK"), v("I16"), mk(13), 32.0, Op.mult, Op.mult)
    tt(v("A", 0, 512), v("LO"), v("HI"), Op.add)
    for j in range(1, 7):
        wd = min(512, W - 512 * j)
        lin(v("A", 512 * j, 512 * j + wd), v("A", 0, wd), 1.0, v("CK", j, j + 1), E("AS", j))
    t5 = col(mk(13), 16.0, mk(5))
    wZ = col(mk(0), 12288.0, col(mk(2), -12288.0, col(t5, -1.0, col(mk(11), 16.0, mk(3)))))
    if any(FLEX):
        w01 = col(mk(0), 0.0625, mk(1))
        lin(v("B01"), v("BM"), w01, 0.0, E("B", "B01"))
    for k in K3:
        move(E("XE", k), third("XW0", 0, k), ix(v("XR"), v("LZ", 32 * k, 32 * k + 32)))
        move(E("XD", k), third("XW0", HS, k), v("XR", 1024 * k + 1, 1024 * (k + 1), 2))
        move(E("UO", k), third("U", HS, k), ix(v("A"), v("LS0", 96 + 32 * k, 128 + 32 * k)))
    ms(v("XW0", H, HS), 0.0)
    ts(v("HU2"), v("HD"), 0.5, None, Op.mult)
    ts(v("SG"), v("AQm"), 100.0, None, Op.is_lt)
    keep(v("TST"), v("SG"), [[1, 128]], Op.is_gt, 0, -1)
    keep(v("TGE"), v("SG"), [[-1, 128]], Op.is_ge, 0, 1)
    ts(v("M1"), v("AQm"), 100.0, 2.0, Op.is_lt, Op.mult)
    tt(v("M1"), v("M1"), IDb, Op.subtract)
    keep(v("M2"), v("M1"), [[-1, 128]], Op.is_ge, 0, 1)
    keep(v("M1"), v("M1"), [[1, 128]], Op.is_ge, 0, -1)
    lin(v("CD"), v("CD"), 1.0, pa, E("CD"))
    for M, wv in (("BKn", -8192.0), ("BKp", 8192.0), ("BP0", mk(0)), ("BZ", wZ), ("BU", t5), ("BHS", float(HS))):
        lin(v(M), v("BM"), wv, 0.0, E("B", M))
    tt(v("BK2", 0, 143), v("BKp", 0, 143), v("BKn", 1, 144), Op.add)
    move(E("SGf"), v("SGf"), v("SG"))
    lin(v("SEO"), v("SE2"), 1.0, float(HS - H), E("SEO"))
    if EARLY:
        lin(v("SG5"), v("SG"), t5, 0.0, E("SG5"))
        move(E("HA"), v("HA"), ix(v("A"), v("HU2")))
        mm(ps(6, 128, 320), [(v("SG5"), v("HA"))])
        move(E("HCOL"), v("HCOL"), ps(6, 128, 320))
    iota(v("BV"), [[1, 112]], 0)
    iota(v("N2"), [[2, 192]], 2)
    for out in (v("DX", H, HS), v("R"), v("ZR"), v("U", H, HS)):
        late(out, 0)
    for r in K3:
        late(v("LA%d" % r, 0, 192), 0)
        late(v("LB%d" % r, 0, 192), 0)
        late(v("XW%d" % (r + 1), H, HS), 0)
        late(v("SA", 16 * FC * r, 16 * FC * (r + 1)), FSRC[r])
        if FLEX[r]:
            late(v("SV", 16 * FC * r, 16 * FC * (r + 1)), 4 ** r)
    for k in K3 if any(FLEX) else ():
        late(third("FV", HS, k), 0)
    dma("g", "zfa", ap(v("FA", HS, GB), slice(0, 128, 16)), ap(v("ZR", 0, 96)), [v("ZR")], [v("FA", HS, GB)], "cast")
    for M, c in (("QE0", 0), ("QE1", -16), ("QO0", 1), ("QO1", -15)):
        keep(v(M), v("SGf"), [[-32, 8], [-1, 16]], Op.is_equal, c, 2)

    def freed(r):
        Fa = v("FA", HS, GB)
        if FLEX[r]:
            Fb = v("FV", HS, GB)
            dma("g", "fcd%d" % r, ap(Fb, slice(1, 128, 16)), ap(Fa, slice(0, 128, 16)), [Fa], [Fb], "cast")
            mm(ps(5, 192, 288), [(I8n, Lo), (I8p, REM)] + conv("B01", "FV", HS, GB))
        else:
            Fb = v("XR", 0, H)
            dma("g", "fcd%d" % r, ap(Fb, slice(0, 128, 16)), ap(Fa, slice(0, 128, 16)), [Fa], [Fb], "cast")
            mm(ps(5, 192, 288), [(I8n, Lo), (I8p, REM)] + conv("BP0", "XR", 0, H))
        flag(E("Fo", r), Fo, ps(5, 192, 288), FTHR[r], 16384.0)

    def level1(r, hs, k1, k2):
        a, b, c, d = 128 * hs[0], 128 * hs[-1] + 128, 8 * hs[0], 8 * hs[-1] + 8
        mm(ps(k1, 16 + c, 16 + d), [(v("BKp", 15, 143), v("R", a, b, 16)), (v("BKn", 0, 128), v("R", a + 16, b + 16, 16))] + conv("BK2", "R", a, b)[1:] + [(IDf, v("CD", c, d))])
        move(E("CE16", r, hs), v("CE16", c, d), ps(k1, 16 + c, 16 + d))
        mm(ps(k2, 480 + c, 480 + d), conv("BM", "R", a, b))
        tt(v("OF16", c, d), ps(k2, 480 + c, 480 + d), v("CE16", c, d), Op.max)
        cp(v("OU", c, d), v("OF16", c, d))
        b -= 16
        mm(ps(k2, a, b), [(v("M1"), v("R", a + 1, b + 1)), (v("M2"), v("R", a, b)), (IDb, v("FL", a, b))])
        move(E("SW", r, hs), v("SW", a, b), ps(k2, a, b))

    def level2(r, hs, k):
        a, b, c, d = 192 * hs[0], 192 * hs[-1] + 192, 12 * hs[0], 12 * hs[-1] + 12
        for h in hs:
            L = "L%s%d" % ("AB"[h], r)
            cp(ix(v(L), v("OU", 8 * h, 8 * h + 7)), v("BV"))
            scan(v("BS", 192 * h, 192 * h + 192), v(L, 0, 192), v("ZR"), Op.max)
        mm(ps(k, 40 + c, 40 + d), conv("BP0", "BS", a, b))
        cp(v("BL", c, d), ps(k, 40 + c, 40 + d))
        lin(v("BLb", c, d), ps(k, 40 + c, 40 + d), 16.0, 0.0, E("BLb", r, hs))
        for h in hs:
            tt(v("U2", 192 * h, 192 * h + 192), ix(v("SW", 128 * h, 128 * h + 112), v("BL", 12 * h, 12 * h + 12)), v("N2"), Op.subtract)
        flag(E("PP", r, hs), v("PP", a, b), v("U2", a, b), -1.5, -512.0)
        ts(v("QQ", a, b), v("U2", a, b), -1.0, None, Op.is_equal)
        mms(ps(k, 64 + c, 64 + d), conv("BHS", "QQ", a, b) + [(IDb, v("BLb", c, d))], conv("BM", "PP", a, b))
        cp(v("SL", c, d), ps(k, 64 + c, 64 + d))

    for r in range(RO):
        last = r == RO - 1
        X, Xn, LS = "XW%d" % r, "XW%d" % (r + 1), "LS%d" % r
        Ao = v("A", HS, GB)
        An, Ak = v("A", HS, GB, 2), v("A", HS + 1, GB, 2)
        dma("s", "nxd%d" % r, ap(Ao, slice(3, 128, 8)), ap(v("U", HS, GB), slice(5, 128, 8)), [v("U", HS, GB)], [An], "row")
        if r > 0:
            freed(r - 1)
        scan(v("R", 129, 241), v("FL", 128, 240), v("FL", 448, 560), Op.add)
        if APART[r]:
            level1(r, (1,), 5, 5)
            level2(r, (1,), 5)
        for k in K3:
            move(E("G1o", r, k), third("DX", HS, k), ix(v(X), v(LS, 96 + 32 * k, 128 + 32 * k)))
            mm(ps(k), [(IDn, third(X, HS, k))], stop=False)
            mm(ps(k), [(IDb, third("DX", HS, k))], start=False)
            ac(third("ABo", 0, k), ps(k), AF.Abs)
            step(E("CO", r, k), third(Xn, HS, k), ps(k))
        kb = KB
        rows = [(v("BM", 15 - k, 143 - k), v("ABo", 96 * k, 96 * (k + 1))) for k in range(16)]
        mms(ps(kb, 384, 480), rows[:5], rows[5:10], rows[10:])
        flag(E("OK", r), v("OK"), ps(kb, 384, 480), 400.5, -512.0)
        dma("s", "okd%d" % r, ap(Ao, slice(0, 128, 16)), ap(v("OK")), [v("OK")], [Ak], "row")
        for k, b in zip(K3, BE):
            move(E("G1e", r, k), third("DX", 0, k), ix(v(X), v(LS, 32 * k, 32 * k + 32)))
            mm(ps(b), [(IDn, third(X, 0, k))], stop=False)
            mm(ps(b), [(IDb, third("DX", 0, k))], start=False)
            ac(third("ABe", 0, k), ps(b), AF.Abs)
        dma("g", "acc%d" % r, ap(v(Xn, HS, GB)), ap(v(X, HS, GB)), [v(X, HS, GB), Ak], [v(Xn, HS, GB)], "acc", accum_op=Op.add, max_dma_last_dim=4096)
        mm(ps(3, 0, 96), conv("BM", "ABo", 0, H), stop=False)
        mm(ps(3, 0, 96), [(I8n, Fo)], start=False)
        if SPL & 1:
            mm(ps(4, 0, 64), conv("BM", "ABe", 0, 1024))
            mm(ps(4, 64, 96), conv("BM", "ABe", 1024, H))
        else:
            mm(ps(4, 0, 96), conv("BM", "ABe", 0, H))
        for k in K3:
            move(E("G2", r, k), third("U", 0, k), ix(v("A"), v(LS, 32 * k, 32 * k + 32)))
        flag(E("Lo", r), Lo, ps(3, 0, 96), 400.5)
        flag(E("Le", r), Le, ps(4, 0, 96), 400.5)
        flag(E("NS", r), v("NS"), ps(4, 0, 96), 159.5)
        scan(v("R", 1, 113), v("FL", 0, 112), v("FL", 336, 448), Op.add)
        mms(ps(4, 96, 192), [(IDf, IX)], [(I8p, v("NS"))])
        cp(v("LF"), ps(4, 96, 192))
        def marks_(j):
            lst, sv, sa = v("LF", FC * j, FC * (j + 1)), v("SV", 16 * FC * r, 16 * FC * (r + 1)), v("SA", 16 * FC * r, 16 * FC * (r + 1))
            marks = dict(r=[lst, sv, sa], w=[v("FV", HS + j, GB, 96 // FC), v("FA", HS + j, GB, 96 // FC)])
            if not FLEX[r]:
                ac(ix(v("FA"), lst), sa, AF.Sigmoid)
            elif E("F", r, j) == "v":
                el("v", vec.tensor_copy, ix(v("FV"), lst), [sv], **marks)
            else:
                el("a", lambda o, i: act.activation(o, i, AF.Sigmoid), ix(v("FA"), lst), [sa], **marks)

        for j in range(96 // FC - FLATE[r]):
            marks_(j)
        level1(r, (0,) if APART[r] else (0, 1), 6, 7)
        mm(ps(7, 496, 497), [(v("SG"), v("R", 96, 97))])
        ts(v("THR", 0, 1), ps(7, 496, 497), 192.0, 8192.0, Op.min, Op.add)
        if not last and EARLY:
            mm(ps(5, 0, 96), [(v("TST"), v("R", 1, 97)), (v("TGE"), v("R", 0, 96))])
            ac(v("RK"), ps(5, 0, 96), AF.Sigmoid, scale=-512.0, bias=512.0 * 191.5, accum_out=v("THR", 1, 2))
            mm(ps(3, 96, 97), [(v("SGf"), v("THR", 1, 2))])
            ts(v("HA"), v("HCOL"), ps(3, 96, 97), None, Op.is_ge)
            move(E("ABh", r), v("ABh"), ix(v("ABe"), v("HU2")))
            mm(ps(3, 288, 480), [(v("SG"), v("ABh")), (I8n, v("HA"))])
            ts(v("KH"), ps(3, 288, 480), 400.5, 0.5, Op.is_gt, Op.mult)
        level2(r, (0,) if APART[r] else (0, 1), 6)
        SI, SF = v("SL", 0, 12), v("SL", 12, 24)
        mm(ps(7, 240, 352), [(v("TST"), v("R", 129, 241)), (v("TGE"), v("R", 128, 240)), (I8p, v("FL", 128, 240))])
        mm(ps(7, 352, 448), [(v("TST"), v("R", 129, 225)), (v("TGE"), v("R", 128, 224)), (IDb, Fe), (I8p, Fo)])
        ts(v("FL", 128, 336), ps(7, 240, 448), v("THR", 0, 1), None, Op.is_ge)
        if SPL & 2:
            mm(ps(5, 96, 160), conv("BZ", "U", 0, 1024) + [(I8n, v("NS", 0, 64))])
            mm(ps(5, 160, 192), conv("BZ", "U", 1024, H) + [(I8n, v("NS", 64, 96))])
        else:
            mm(ps(5, 96, 192), conv("BZ", "U", 0, H) + [(I8n, v("NS"))])
        flag(E("MM", r), v("MM"), ps(5, 96, 192), -4096.5)
        tt(v("MD"), ps(5, 96, 192), v("MM"), Op.mult)
        if L3V:
            tt(v("TT"), IX, v("MD"), Op.add)
            cp(v("L3"), v("TT"))
        else:
            mms(ps(4, 384, 480), [(IDf, IX)], [(IDf, v("MD"))])
            cp(v("L3"), ps(4, 384, 480))
        for k in K3:
            move(E("G3", r, k), third("D3", 0, k), ix(v(X), v("L3", 32 * k, 32 * k + 32)))
        if not last and EARLY:
            move(E("DH", r), v("DH"), ix(v("D3"), v("HU2")))
            mms(ps(3, 288, 480), [(IDn, v("KH")), (IDn, v("HG%d" % r))], [(IDb, v("DH"))])
            ts(v("HC"), ps(3, 288, 480), 1.0, -1.0, Op.min, Op.max)
            tt(v("HG%d" % (r + 1)), v("HC"), v("HG%d" % r), Op.add)
            send(r + 1)
        for k in K3:
            mm(ps(k), [(IDn, third(X, 0, k))], stop=False)
            mm(ps(k), [(IDb, third("D3", 0, k))], start=False)
            if k < EVD[r]:
                step(E("CE", r, k), third(Xn, 0, k), ps(k))
                dma("g", "ac%d%d" % (k, r), ap(third(Xn, 0, k)), ap(third(X, 0, k)), [third(X, 0, k)], [third(Xn, 0, k)], "ac3", accum_op=Op.add)
                continue
            if k < EVV[r]:
                step(E("CE", r, k), ps(k), ps(k))
                tt(third(Xn, 0, k), ps(k), third(X, 0, k), Op.add)
                continue
            step(E("CE", r, k), third("CE", 0, k), ps(k))
            mm(ps(k), [(IDb, third(X, 0, k)), (IDb, third("CE", 0, k))])
            move(E("EV", r, k), third(Xn, 0, k), ps(k))
        move(E("S1", r), v("SRC", 0, 192), ix(v("A"), SF))
        move(E("S2", r), v("SRC", 192, 384), ix(v("U"), SI))
        cp(ix(v("U"), v("SL")), v("SRC"))
        evens = conv("BU", "U", 0, H) + [(IDf, v("MD")), (I8n, Fe)]
        odds = conv("BU", "U", HS, GB)
        if not last:
            mm(ps(3, 192, 288), odds)
            mms(ps(4, 192, 288), evens[16:], evens[:16])
            cp(v("LS%d" % (r + 1), 96), ps(3, 192, 288))
            tt(v("QF"), v("SE2"), Fe, Op.mult)
            tt(IX, ps(4, 192, 288), v("QF"), Op.max)
            cp(v("LS%d" % (r + 1), 0, 96), IX)
        B1, B2 = v("BB", 0, 192), v("BB", 192, 384)
        move(E("B1", r), B1, ix(v(X, 0, GB), SI))
        move(E("NI", r), v("DD"), ix(v("DX"), SI))
        mm(ps(7, 0, 192), [(IDb, B1), (IDb, v("DD"))])
        ts(v("HH"), ps(7, 0, 192), 0.5, -0.25, Op.mult, Op.add)
        cp(B2, v("HH"))
        mm(ps(6, 128, 320), [(IDb, B2), (IDn, B1)])
        mm(ps(6, 320, 512), [(IDb, v("DD")), (IDn, B2)])
        step(E("CB", r), v("CB"), ps(6, 128, 512))
        gate = len(nodes) - 1 - FGATE
        for j in range(96 // FC - FLATE[r], 96 // FC):
            marks_(j)
            nodes[-1]["dep"] = nodes[-1]["dep"] | {gate}
        tt(ix(v(Xn, 0, GB), v("SL")), v("CB"), v("BB"), Op.add)
        if not last and not EARLY:
            move(E("HG", r), v("HG%d" % (r + 1)), ix(v(Xn, 0, H), v("HU2")))
            send(r + 1)

    freed(RO - 1)
    mm(ps(3, 0, 96), [(IDf, v("SEO")), (I8n, Fo)])
    cp(v("LZ"), ps(3, 0, 96))
    for k, (a, b) in enumerate(zip(CUTS, CUTS[1:])):
        move(E("Y", k), v("XO", 32 * a + 1, 32 * b, 2), ix(v(Xn, H, GB), v("LZ", a, b)))
        move(E("YE", k), v("XO", 32 * a, 32 * b, 2), v(Xn, 16 * a, 16 * b))
        out = v("XO", 32 * a, 32 * b)
        dma("s", "stx%d" % k, T.yx[:, 32 * a:32 * b], ap(out), [out], (), "stx")
        nodes[-1]["dur"] = 0.03 * (b - a)
    mm(ps(5, 0, 96), [(IDf, v("MD")), (I8n, Fe)])
    mm(ps(5, 96, 192), [(I8n, Fo)])
    move(E("T4"), v("T4"), ps(5, 0, 192))
    c = ps(4, 192, 384)
    mm(c, [(IDb, v("ZR"))], stop=False)
    for h, (Qe, Qo) in enumerate((("QE0", "QO0"), ("QE1", "QO1"))):
        mm(ps(4, 192 + h, 384, 2), [(v(Qe), v("T4", 0, 96)), (v(Qo), v("T4", 96, 192))], start=False, stop=False)
    mm(c, [(v("BU", 15 - k, 143 - k), v("U", HS * (k % 2) + k // 2, HS * (k % 2) + H, 8)) for k in range(16)], start=False)
    ts(v("T1"), c, -0.5, 2.0, Op.max, Op.mult)
    ts(v("T2"), c, float(HS), 1.0 - 2 * HS, Op.is_ge, Op.mult)
    ac(v("T3"), c, AF.Abs, bias=float(GB - 1))
    tt(v("T1"), v("T1"), v("T3"), Op.min)
    tt(v("YN"), v("T1"), v("T2"), Op.add)
    dma("s", "stn", T.yn[:], ap(v("YN")), [v("YN")], (), "stn")
    return nodes, sent


def rank_program(g, core, T, topo):
    rank = T.rank_of(core)
    if rank is None:
        return
    if not PLAN:
        PLAN.extend(plan(steps(g, T, topo, rank, lambda key: "v")[0], steps(g, T, topo, rank, lambda key: "a")[0]))
    nodes, sent = steps(g, T, topo, rank, PLAN[0].get)
    S = T.sem
    q = {"v": g.vector, "a": g.scalar, "p": g.tensor, "g": g, "s": g.sync}
    sem = {"v": S.sv, "a": S.sa, "p": S.sp, "g": S.sg}
    cnt, waited, toks, mark, past = {e: 0 for e in sem}, {}, {}, {}, {}
    for i in PLAN[1]:
        x = nodes[i]
        e = x["e"]
        if e != "x":
            need, wait = {}, set(x["wait"])
            if x["key"] and x["key"][0] == "F":
                wait |= set(mark.get(e, ()))
                mark[e] = [i]
            for d in wait:
                name, val = toks[d]
                if not (name == "p" and e == "p"):
                    need[name] = max(need.get(name, 0), val)
            seen = waited.setdefault(e, {})
            need = {k: val for k, val in need.items() if seen.get(k, 0) < val}
            for name in sorted(need):
                if not any(past[k, val].get(name, 0) >= need[name] for k, val in need.items() if k != name):
                    q[e].wait_ge(sem[name] if name in sem else S[name], need[name])
            for name in need:
                for k, val in list(past[name, need[name]].items()) + [(name, need[name])]:
                    seen[k] = max(seen.get(k, 0), val)
        for fn in x["fns"]:
            ins = fn()
            if x["tok"] is None:
                cnt[e] += 1
                ins.then_inc(sem[e], 1)
        toks[i] = x["tok"] or (e, cnt[e])
        past[toks[i]] = dict(waited.get(e, {}))
    for name, val in [("stx%d" % k, 16) for k in range(len(CUTS) - 1)] + [("stn", 16)] + [("snt%d" % r, sent) for r in range(RO)]:
        g.sync.wait_ge(S[name], val)
    for e in sem:
        g.sync.wait_ge(sem[e], cnt[e])
